import numpy as np
import ml_dtypes


def mxq(x, axis, fmt="e4m3"):
    dtype, down = {"e4m3": (ml_dtypes.float8_e4m3fn, 7), "e5m2": (ml_dtypes.float8_e5m2, 14)}[fmt]
    v = np.moveaxis(np.asarray(x, np.float32).astype(ml_dtypes.bfloat16).astype(np.float64), axis, -1)
    blocks = v.reshape(v.shape[:-1] + (-1, 32))
    amax = np.abs(blocks).max(-1, keepdims=True)
    byte = np.maximum(np.where(amax > 0, np.frexp(amax)[1] - 1 + 127, 0) - down, 1)
    scale = np.exp2(byte - 127.0)
    codes = (blocks / scale).astype(np.float32).astype(dtype).astype(np.float64)
    return np.moveaxis((codes * scale).reshape(v.shape), -1, axis)


WIDE = False


def mx_kscale(k):
    if not WIDE:
        return np.ones(k)
    levels = np.array([10, -10, 5, -5, 0])
    if k % 512:
        return np.exp2(np.random.permutation(np.resize(levels, k // 32))).repeat(32)
    a = np.empty((k // 512, 16))
    for p in range(k // 512):
        a[p, :8] = np.random.permutation(np.resize(levels, 8))
        for g in range(8):
            far = levels[np.abs(levels - a[p, g]) >= 10]
            a[p, g + 8] = far[np.random.randint(len(far))]
    return np.exp2(a.ravel()).repeat(32)


def f64(x):
    return np.asarray(x).astype(np.float64)


def striped(idx):
    return np.tile(idx.reshape(-1, 16).T, (8, 1)).astype(np.uint16)


def unstriped(offs):
    return offs[:16].T.reshape(-1).astype(np.int64)


E2M1 = np.array([0.0, 0.5, 1.0, 1.5, 2.0, 3.0, 4.0, 6.0, -0.0, -0.5, -1.0, -1.5, -2.0, -3.0, -4.0, -6.0])


def pack_weight(w, fmt):
    k, n = w.shape
    w = f64(np.asarray(w, np.float32).astype(ml_dtypes.bfloat16)).reshape(k // 32, 32, n)
    amax = np.abs(w).max(1)
    if fmt == "e4m3":
        byte = np.frexp(amax)[1] - 1 + 127 - 7
    else:
        mant, ex = np.frexp(amax / 6.0)
        byte = np.where(mant > 0.5, ex, ex - 1) + 127
    byte = np.clip(np.where(amax > 0, byte, 1), 1, 254)
    scaled = (w * np.exp2(127.0 - byte)[:, None, :]).reshape(k, n).astype(np.float32)
    by_word = np.ascontiguousarray(scaled.reshape(k // 512, 128, 4, n).transpose(0, 1, 3, 2))
    if fmt == "e4m3":
        words = by_word.astype(ml_dtypes.float8_e4m3fn).view(np.uint8)
    else:
        c = by_word.astype(ml_dtypes.float4_e2m1fn).view(np.uint8) & 0xF
        words = (c[..., 0::2] | (c[..., 1::2] << 4)).reshape(k // 512, 128, 2 * n)
    return np.ascontiguousarray(words), np.ascontiguousarray(byte.astype(np.uint8).reshape(k // 512, 16, n))


def unpack_weight(words, scales, fmt):
    g, _, n = scales.shape
    words = np.ascontiguousarray(words).reshape(g, 128, n, -1)
    if fmt == "e4m3":
        vals = words.view(ml_dtypes.float8_e4m3fn).astype(np.float64)
    else:
        nib = np.empty((g, 128, n, 4), np.uint8)
        nib[..., 0::2] = words & 0xF
        nib[..., 1::2] = words >> 4
        vals = E2M1[nib]
    vals = vals * np.repeat(np.exp2(scales.astype(np.float64) - 127.0), 8, axis=1)[..., None]
    return vals.transpose(0, 1, 3, 2).reshape(g * 512, n)


def gelu(v):
    return 0.5 * v * (1.0 + np.tanh(np.sqrt(2.0 / np.pi) * (v + 0.044715 * v**3)))


K, T, S, T2, H, N, P = 1024, 4096, 1024, 2048, 512, 512, 128

def setup_inputs():
    n = np.random.standard_normal
    s = mx_kscale(K)[:, None]
    u = mx_kscale(H)[:, None]
    tab_words, tab_scales = pack_weight(n((K, T)) * s, "e4m3")
    w4_words, w4_scales = pack_weight(n((K, H)) / np.sqrt(K) / s * u.T, "e2m1")
    w8_words, w8_scales = pack_weight(n((H, N)) / np.sqrt(H) / u, "e4m3")
    return {
        "tab_words": tab_words, "tab_scales": tab_scales,
        "offs": striped(np.random.permutation(T)[:S]),
        "w1": (n((K, H)) / np.sqrt(K) / s * u.T).astype(np.float32),
        "w4_words": w4_words, "w4_scales": w4_scales,
        "wgs": np.exp(0.3 * n((P, S))).astype(np.float32),
        "offs2": striped(np.random.permutation(T2)[:S]),
        "state": (n((H, T2)) * u).astype(np.float32),
        "w8_words": w8_words, "w8_scales": w8_scales,
    }

def reference(tab_words, tab_scales, offs, w1, w4_words, w4_scales, wgs, offs2, state, w8_words, w8_scales):
    v = unpack_weight(tab_words, tab_scales, "e4m3")[:, unstriped(offs)]
    w1q = mxq(f64(w1), 0, "e4m3")
    w4 = unpack_weight(w4_words, w4_scales, "e2m1")
    a = np.maximum(w1q.T @ v, 0.0)
    b = w4.T @ v
    h = np.abs(a - b)
    page = np.zeros((H, T2))
    page[:, unstriped(offs2)] = np.tile(f64(wgs), (H // P, 1)) * h
    z = np.maximum(page, f64(state))
    zq = mxq(z, 0, "e4m3")
    w8 = unpack_weight(w8_words, w8_scales, "e4m3")
    return w8.T @ zq

@@ -1,0 +1,270 @@
+from contextlib import ExitStack
+
+import concourse.mybir as mybir
+from concourse.masks import make_identity
+
+K, T, S, T2, H, N = 1024, 4096, 1024, 2048, 512, 512
+FLOPS = 2 * (2 * K * H * S + H * N * T2)
+
+F32 = mybir.dt.float32
+BF16 = mybir.dt.bfloat16
+I32 = mybir.dt.int32
+U32 = mybir.dt.uint32
+U16 = mybir.dt.uint16
+U8 = mybir.dt.uint8
+FP8X4 = mybir.dt.float8_e4m3fn_x4
+FP4X4 = mybir.dt.float4_e2m1fn_x4
+ALU = mybir.AluOpType
+ACT = mybir.ActivationFunctionType
+
+P = 128
+PACK = 4
+PASSES = K // (P * PACK)
+BANK = 512
+QUAD = 32
+ROWS = 16
+W4_AT = S
+W8_AT = S + H
+PLANE = S + H + N
+
+SCATTERS = ((0, 0, 256), (1, 0, 256), (0, 256, 768), (1, 256, 1024), (0, 768, 1024), (2, 0, 1024), (3, 0, 1024))
+NODE_CHUNKS = (512, 512, 512, 256, 256)
+SCALAR_SHARE = 5
+
+
+def tile_list_neighbour_gap_message_kernel(
+    tc, tab_words, tab_scales, offs, w1, w4_words, w4_scales, wgs, offs2, state, w8_words, w8_scales, out
+):
+    nc = tc.nc
+    with ExitStack() as ctx:
+        keep = ctx.enter_context(tc.tile_pool(name="keep", bufs=1))
+        ring = ctx.enter_context(tc.tile_pool(name="ring", bufs=2))
+        outs = ctx.enter_context(tc.tile_pool(name="outs", bufs=6))
+        psum = ctx.enter_context(tc.psum_pool(name="psum", bufs=8))
+
+        idx = keep.tile([P, S // 16], U16, name="idx")
+        idx2 = keep.tile([P, S // 16], U16, name="idx2")
+        tsc = keep.tile([P, T], U8, name="tsc", align_bytes=64)
+        w4s_raw = keep.tile([P, H], U8, name="w4s_raw", align_bytes=64)
+        rows = keep.tile([P, PLANE], U8, name="rows", align_bytes=64)
+        planes = keep.tile([P, PASSES * PLANE], U8, name="planes", align_bytes=64)
+        tab = [keep.tile([P, T], I32, name="tab%d" % a, align_bytes=64) for a in range(PASSES)]
+        w4_raw = keep.tile([P, PASSES, 2 * H], U8, name="w4_raw", align_bytes=64)
+        w1_raw = [keep.tile([P, PACK, H], F32, name="w1_raw%d" % a, align_bytes=64) for a in range(PASSES)]
+        wg_lo = keep.tile([P, 2, S], F32, name="wg_lo", align_bytes=64)
+        wg_hi = keep.tile([P, 2, S], F32, name="wg_hi", tag="late", align_bytes=64)
+        w8 = keep.tile([P, N], I32, name="w8", align_bytes=64)
+        st = [keep.tile([P, PACK, BANK], F32, name="st%d" % c, align_bytes=64) for c in range(T2 // BANK)]
+        pages = [keep.tile([P, T2], F32, name="page%d" % t, align_bytes=64) for t in range(2)]
+        ident = keep.tile([P, P], F32, name="ident", align_bytes=64)
+
+        live = PASSES * ROWS
+        for lo, hi in ((QUAD, 2 * QUAD), (2 * QUAD, P)):
+            nc.vector.memset(tsc[lo:hi, :].bitcast(I32), 0)
+            nc.vector.memset(w4s_raw[lo:hi, :].bitcast(I32), 0)
+        nc.vector.memset(planes[:].bitcast(I32), 0)
+        make_identity(nc, ident[:])
+        for page in pages:
+            nc.gpsimd.memset(page[:], 0.0)
+
+        nc.sync.dma_start(idx[:], offs)
+        nc.sync.dma_start(tsc[0:live, :].bitcast(I32), tab_scales.rearrange("a q t -> (a q) t").bitcast(I32))
+        nc.sync.dma_start(w4s_raw[0:live, :].bitcast(I32), w4_scales.rearrange("a q c -> (a q) c").bitcast(I32))
+        nc.sync.dma_start(tab[0][:], tab_words[0].rearrange("p t i -> p (t i)").bitcast(I32))
+        nc.sync.dma_start(rows[0:ROWS, W8_AT:PLANE].bitcast(I32), w8_scales[0].bitcast(I32))
+        nc.sync.dma_start(w4_raw[:].bitcast(I32), w4_words.rearrange("a p b -> p a b").bitcast(I32))
+        for a in range(PASSES):
+            nc.sync.dma_start(w1_raw[a][:], w1[a * 512 : (a + 1) * 512, :].rearrange("(p j) c -> p j c", j=PACK))
+        nc.sync.dma_start(tab[1][:], tab_words[1].rearrange("p t i -> p (t i)").bitcast(I32))
+        nc.sync.dma_start(idx2[:], offs2)
+        wgs_rows = wgs.rearrange("(q t) j -> q t j", t=PACK)
+        for half, wg in enumerate((wg_lo, wg_hi)):
+            for g in range(P // QUAD):
+                nc.sync.dma_start(wg[g * QUAD : (g + 1) * QUAD, :, :], wgs_rows[:, 2 * half : 2 * half + 2, :])
+        nc.sync.dma_start(w8[:], w8_words[0].rearrange("p c i -> p (c i)").bitcast(I32))
+        state_rows = state.rearrange("(p t) n -> p t n", t=PACK)
+        for c in range(T2 // BANK):
+            nc.sync.dma_start(st[c][:], state_rows[:, :, c * BANK : (c + 1) * BANK])
+
+        gsc = keep.tile([P, S], U8, name="gsc", align_bytes=64)
+        nc.vector.tensor_copy(gsc[:], tsc[:].indirect(idx[:]))
+        nc.vector.tensor_copy(rows[:, 0:S].bitcast(I32), gsc[:].bitcast(I32))
+        nc.vector.tensor_copy(
+            rows[:, W4_AT:W8_AT].rearrange("p (t m) -> p t m", t=PACK),
+            w4s_raw[:].rearrange("p (m t) -> p t m", t=PACK),
+        )
+        for a in range(PASSES):
+            width = PLANE if a == 0 else W8_AT
+            for q in range(P // QUAD):
+                src = ROWS * a + 4 * q
+                nc.gpsimd.dma_start(
+                    planes[QUAD * q : QUAD * q + 4, a * PLANE : a * PLANE + width].bitcast(I32),
+                    rows[src : src + 4, 0:width].bitcast(I32),
+                )
+
+        v = [keep.tile([P, S], U32, name="v%d" % a, align_bytes=64) for a in range(PASSES)]
+        nc.vector.tensor_copy(v[0][:], tab[0][:].bitcast(U32).indirect(idx[:]))
+
+        w4 = keep.tile([P, PASSES, 2 * H], U8, name="w4", align_bytes=64)
+        nc.vector.tensor_copy(
+            w4[:].bitcast(U16).rearrange("p a (t m) -> p a t m", t=PACK),
+            w4_raw[:].bitcast(U16).rearrange("p a (m t) -> p a t m", t=PACK),
+        )
+        w1_codes = keep.tile([P, PASSES, H], U32, name="w1_codes", align_bytes=64)
+        w1_scales = keep.tile([P, PASSES, H], U8, name="w1_scales", align_bytes=64)
+        for a in range(PASSES):
+            grouped = ring.tile([P, H * PACK], BF16, name="grouped", tag="grouped", align_bytes=64)
+            nc.scalar.copy(
+                grouped[:].rearrange("p (t m j) -> p m t j", t=PACK, j=PACK),
+                w1_raw[a][:].rearrange("p j (m t) -> p m t j", t=PACK),
+            )
+            nc.vector.quantize_mx(out=w1_codes[:, a, :].bitcast(FP8X4), scales=w1_scales[:, a, :], in_=grouped[:])
+
+        for t in range(2, PACK):
+            page = ring.tile([P, T2], F32, name="page%d" % t, tag="grouped", align_bytes=64)
+            nc.gpsimd.memset(page[:], 0.0)
+            pages.append(page)
+
+        for lo in (0, S // 2):
+            nc.vector.tensor_copy(
+                v[1][:, lo : lo + S // 2], tab[1][:].bitcast(U32).indirect(idx[:, lo // 16 : (lo + S // 2) // 16])
+            )
+
+        h = [keep.tile([P, S], F32, name="h%d" % t, align_bytes=64) for t in range(PACK)]
+
+        def views(t, e0, e1):
+            blocks = (e1 - e0) // P
+            a_ps = psum.tile([P, BANK], F32, name="a_ps", tag="bank")
+            b_ps = psum.tile([P, BANK], F32, name="b_ps", tag="bank")
+            for a in range(PASSES):
+                for acc, is_w1 in ((a_ps, True), (b_ps, False)):
+                    if is_w1:
+                        rhs = w1_codes[:, a, t * P : (t + 1) * P].bitcast(FP8X4)
+                        rhs_scale = w1_scales[:, a, t * P : (t + 1) * P]
+                    else:
+                        rhs = w4[:, a, 2 * t * P : 2 * (t + 1) * P].bitcast(FP4X4)
+                        at = a * PLANE + W4_AT + t * P
+                        rhs_scale = planes[:, at : at + P]
+                    for b in range(blocks):
+                        e = e0 + b * P
+                        nc.tensor.matmul_mx(
+                            out=acc[:, b * P : (b + 1) * P],
+                            lhsT=v[a][:, e : e + P].bitcast(FP8X4),
+                            lhsT_scale=planes[:, a * PLANE + e : a * PLANE + e + P],
+                            rhs=rhs,
+                            rhs_scale=rhs_scale,
+                            start=(a == 0 and b == 0),
+                            stop=(a == PASSES - 1 and b == blocks - 1),
+                        )
+            width = e1 - e0
+            a_sb = ring.tile([P, BANK], F32, name="a_sb", bufs=3, align_bytes=64)
+            nb_sb = ring.tile([P, BANK], F32, name="nb_sb", bufs=3, align_bytes=64)
+            nc.scalar.activation(a_sb[:, :width], a_ps[:, :width], ACT.Relu)
+            nc.scalar.activation(nb_sb[:, :width], b_ps[:, :width], ACT.Copy, scale=-1.0)
+            return a_sb, nb_sb
+
+        def gaps(t, e0, e1, terms):
+            width = e1 - e0
+            blocks = width // P
+            d_ps = psum.tile([P, BANK], F32, name="d_ps", tag="bank")
+            for k, term in enumerate(terms):
+                for b in range(blocks):
+                    nc.tensor.matmul(
+                        d_ps[:, b * P : (b + 1) * P],
+                        lhsT=term[:, b * P : (b + 1) * P],
+                        rhs=ident[:],
+                        is_transpose=True,
+                        start=(k == 0 and b == 0),
+                        stop=(k == 1 and b == blocks - 1),
+                    )
+            nc.scalar.activation(h[t][:, e0:e1], d_ps[:, :width], ACT.Abs)
+
+        units = [(t, lo, min(lo + BANK, e1)) for t, e0, e1 in SCATTERS for lo in range(e0, e1, BANK)]
+        ahead = views(*units[0])
+        u = 0
+        for t, e0, e1 in SCATTERS:
+            for lo in range(e0, e1, BANK):
+                terms = ahead
+                if u + 1 < len(units):
+                    ahead = views(*units[u + 1])
+                gaps(*units[u], terms)
+                u = u + 1
+            wg = wg_lo if t < 2 else wg_hi
+            nc.vector.tensor_tensor(
+                pages[t][:].indirect(idx2[:, e0 // 16 : e1 // 16]), h[t][:, e0:e1], wg[:, t % 2, e0:e1], ALU.mult
+            )
+
+        first = NODE_CHUNKS[0]
+        z_first = keep.tile([P, PACK * first], BF16, name="z_first", align_bytes=64)
+        z_rest = keep.tile([P, PACK * (T2 - first)], BF16, name="z_rest", tag="late", align_bytes=64)
+        starts = [sum(NODE_CHUNKS[:c]) for c in range(len(NODE_CHUNKS))]
+
+        def z_chunk(c):
+            n0, width = starts[c], NODE_CHUNKS[c]
+            z = z_first[:] if c == 0 else z_rest[:, PACK * (n0 - first) : PACK * (n0 - first + width)]
+            return z.rearrange("p (t n) -> p t n", t=PACK)
+
+        def maximum(c, t):
+            if c < len(NODE_CHUNKS):
+                n0, width = starts[c], NODE_CHUNKS[c]
+                part, at = divmod(n0, BANK)
+                nc.vector.tensor_tensor(
+                    z_chunk(c)[:, t, :], pages[t][:, n0 : n0 + width], st[part][:, t, at : at + width], ALU.max
+                )
+
+        def weave(c):
+            width = NODE_CHUNKS[c]
+            woven = ring.tile([P, PACK * BANK], BF16, name="woven", align_bytes=64)
+            split = width * SCALAR_SHARE // 16
+            for lo, hi, copy in ((0, split, nc.scalar.copy), (split, width, nc.vector.tensor_copy)):
+                copy(
+                    woven[:, PACK * lo : PACK * hi].rearrange("p (c i t) -> p c t i", i=4, t=PACK),
+                    z_chunk(c)[:, :, lo:hi].rearrange("p t (c i) -> p c t i", i=4),
+                )
+            return woven
+
+        def quantise(c, woven):
+            width = NODE_CHUNKS[c]
+            z_codes = ring.tile([P, BANK], U32, name="z_codes", align_bytes=64)
+            z_scales = ring.tile([P, BANK], U8, name="z_scales", align_bytes=64)
+            nc.vector.quantize_mx(
+                out=z_codes[:, :width].bitcast(FP8X4), scales=z_scales[:, :width], in_=woven[:, : PACK * width]
+            )
+            return z_codes, z_scales
+
+        def messages(c, z_codes, z_scales):
+            n0, width = starts[c], NODE_CHUNKS[c]
+            per_bank = BANK // width
+            for b0 in range(0, N // P, per_bank):
+                o_ps = psum.tile([P, BANK], F32, name="o_ps", tag="bank")
+                for k in range(per_bank):
+                    b = b0 + k
+                    nc.tensor.matmul_mx(
+                        out=o_ps[:, k * width : (k + 1) * width],
+                        lhsT=w8[:, b * P : (b + 1) * P].bitcast(FP8X4),
+                        lhsT_scale=planes[:, W8_AT + b * P : W8_AT + (b + 1) * P],
+                        rhs=z_codes[:, :width].bitcast(FP8X4),
+                        rhs_scale=z_scales[:, :width],
+                        start=True,
+                        stop=True,
+                    )
+                o_sb = outs.tile([P, BANK], F32, name="o_sb", align_bytes=64)
+                if c == len(NODE_CHUNKS) - 1 and b0 > 0:
+                    nc.vector.tensor_copy(o_sb[:], o_ps[:])
+                else:
+                    nc.scalar.copy(o_sb[:], o_ps[:])
+                nc.sync.dma_start(
+                    out[b0 * P : (b0 + per_bank) * P, n0 : n0 + width].rearrange("(k p) n -> p k n", p=P),
+                    o_sb[:].rearrange("p (k n) -> p k n", k=per_bank),
+                )
+
+        for t in range(PACK):
+            maximum(0, t)
+        for c in range(len(NODE_CHUNKS)):
+            maximum(c + 1, 0)
+            woven = weave(c)
+            maximum(c + 1, 1)
+            maximum(c + 1, 2)
+            z_codes, z_scales = quantise(c, woven)
+            maximum(c + 1, 3)
+            messages(c, z_codes, z_scales)

@@ -24,8 +24,8 @@ BANK = 512
 QUAD = 32
 ROWS = 16
 W4_AT = S
-W8_AT = S + H
-PLANE = S + H + N
+PLANE = S + H
+FIRST = 256
 
 SCATTERS = ((0, 0, 256), (1, 0, 256), (0, 256, 768), (1, 256, 1024), (0, 768, 1024), (2, 0, 1024), (3, 0, 1024))
 NODE_CHUNKS = (512, 512, 512, 256, 256)
@@ -46,63 +46,52 @@ def tile_list_neighbour_gap_message_kernel(
         idx2 = keep.tile([P, S // 16], U16, name="idx2")
         tsc = keep.tile([P, T], U8, name="tsc", align_bytes=64)
         w4s_raw = keep.tile([P, H], U8, name="w4s_raw", align_bytes=64)
-        rows = keep.tile([P, PLANE], U8, name="rows", align_bytes=64)
         planes = keep.tile([P, PASSES * PLANE], U8, name="planes", align_bytes=64)
-        tab = [keep.tile([P, T], I32, name="tab%d" % a, align_bytes=64) for a in range(PASSES)]
+        tab = [keep.tile([P, T], I32, name="tab%d" % a, tag="big%d" % a, align_bytes=64) for a in range(PASSES)]
         w4_raw = keep.tile([P, PASSES, 2 * H], U8, name="w4_raw", align_bytes=64)
-        w1_raw = [keep.tile([P, PACK, H], F32, name="w1_raw%d" % a, align_bytes=64) for a in range(PASSES)]
-        wg_lo = keep.tile([P, 2, S], F32, name="wg_lo", align_bytes=64)
-        wg_hi = keep.tile([P, 2, S], F32, name="wg_hi", tag="late", align_bytes=64)
-        w8 = keep.tile([P, N], I32, name="w8", align_bytes=64)
-        st = [keep.tile([P, PACK, BANK], F32, name="st%d" % c, align_bytes=64) for c in range(T2 // BANK)]
+        w1_raw = [
+            keep.tile([P, PACK, H], F32, name="w1_raw%d" % a, tag="w1_raw%d" % a, align_bytes=64) for a in range(PASSES)
+        ]
         pages = [keep.tile([P, T2], F32, name="page%d" % t, align_bytes=64) for t in range(2)]
         ident = keep.tile([P, P], F32, name="ident", align_bytes=64)
 
         live = PASSES * ROWS
         for lo, hi in ((QUAD, 2 * QUAD), (2 * QUAD, P)):
-            nc.vector.memset(tsc[lo:hi, :].bitcast(I32), 0)
+            nc.gpsimd.memset(tsc[lo:hi, :].bitcast(I32), 0)
             nc.vector.memset(w4s_raw[lo:hi, :].bitcast(I32), 0)
-        nc.vector.memset(planes[:].bitcast(I32), 0)
+        nc.vector.memset(planes[:, PLANE:].bitcast(I32), 0)
         make_identity(nc, ident[:])
-        for page in pages:
-            nc.gpsimd.memset(page[:], 0.0)
 
         nc.sync.dma_start(idx[:], offs)
         nc.sync.dma_start(tsc[0:live, :].bitcast(I32), tab_scales.rearrange("a q t -> (a q) t").bitcast(I32))
         nc.sync.dma_start(w4s_raw[0:live, :].bitcast(I32), w4_scales.rearrange("a q c -> (a q) c").bitcast(I32))
-        nc.sync.dma_start(tab[0][:], tab_words[0].rearrange("p t i -> p (t i)").bitcast(I32))
-        nc.sync.dma_start(rows[0:ROWS, W8_AT:PLANE].bitcast(I32), w8_scales[0].bitcast(I32))
+        nc.sync.dma_start(idx2[:], offs2)
         nc.sync.dma_start(w4_raw[:].bitcast(I32), w4_words.rearrange("a p b -> p a b").bitcast(I32))
+        nc.sync.dma_start(tab[0][:], tab_words[0].rearrange("p t i -> p (t i)").bitcast(I32))
         for a in range(PASSES):
             nc.sync.dma_start(w1_raw[a][:], w1[a * 512 : (a + 1) * 512, :].rearrange("(p j) c -> p j c", j=PACK))
         nc.sync.dma_start(tab[1][:], tab_words[1].rearrange("p t i -> p (t i)").bitcast(I32))
-        nc.sync.dma_start(idx2[:], offs2)
-        wgs_rows = wgs.rearrange("(q t) j -> q t j", t=PACK)
-        for half, wg in enumerate((wg_lo, wg_hi)):
-            for g in range(P // QUAD):
-                nc.sync.dma_start(wg[g * QUAD : (g + 1) * QUAD, :, :], wgs_rows[:, 2 * half : 2 * half + 2, :])
-        nc.sync.dma_start(w8[:], w8_words[0].rearrange("p c i -> p (c i)").bitcast(I32))
-        state_rows = state.rearrange("(p t) n -> p t n", t=PACK)
-        for c in range(T2 // BANK):
-            nc.sync.dma_start(st[c][:], state_rows[:, :, c * BANK : (c + 1) * BANK])
 
         gsc = keep.tile([P, S], U8, name="gsc", align_bytes=64)
-        nc.vector.tensor_copy(gsc[:], tsc[:].indirect(idx[:]))
-        nc.vector.tensor_copy(rows[:, 0:S].bitcast(I32), gsc[:].bitcast(I32))
         nc.vector.tensor_copy(
-            rows[:, W4_AT:W8_AT].rearrange("p (t m) -> p t m", t=PACK),
+            planes[:, W4_AT:PLANE].rearrange("p (t m) -> p t m", t=PACK),
             w4s_raw[:].rearrange("p (m t) -> p t m", t=PACK),
         )
+        nc.vector.tensor_copy(gsc[:], tsc[:].indirect(idx[:]))
+        nc.vector.tensor_copy(planes[:, 0:S].bitcast(I32), gsc[:].bitcast(I32))
         for a in range(PASSES):
-            width = PLANE if a == 0 else W8_AT
             for q in range(P // QUAD):
                 src = ROWS * a + 4 * q
-                nc.gpsimd.dma_start(
-                    planes[QUAD * q : QUAD * q + 4, a * PLANE : a * PLANE + width].bitcast(I32),
-                    rows[src : src + 4, 0:width].bitcast(I32),
-                )
+                if src > 0:
+                    nc.scalar.dma_start(
+                        planes[QUAD * q : QUAD * q + 4, a * PLANE : (a + 1) * PLANE].bitcast(I32),
+                        planes[src : src + 4, 0:PLANE].bitcast(I32),
+                    )
 
-        v = [keep.tile([P, S], U32, name="v%d" % a, align_bytes=64) for a in range(PASSES)]
+        for page in pages:
+            nc.vector.memset(page[:].bitcast(I32), 0)
+
+        v = [keep.tile([P, S], U32, name="v%d" % a, tag="v%d" % a, align_bytes=64) for a in range(PASSES)]
         nc.vector.tensor_copy(v[0][:], tab[0][:].bitcast(U32).indirect(idx[:]))
 
         w4 = keep.tile([P, PASSES, 2 * H], U8, name="w4", align_bytes=64)
@@ -112,23 +101,32 @@ def tile_list_neighbour_gap_message_kernel(
         )
         w1_codes = keep.tile([P, PASSES, H], U32, name="w1_codes", align_bytes=64)
         w1_scales = keep.tile([P, PASSES, H], U8, name="w1_scales", align_bytes=64)
-        for a in range(PASSES):
-            grouped = ring.tile([P, H * PACK], BF16, name="grouped", tag="grouped", align_bytes=64)
-            nc.scalar.copy(
+        for a, copy in enumerate((nc.scalar.copy, nc.vector.tensor_copy)):
+            grouped = keep.tile([P, H * PACK], BF16, name="grouped%d" % a, tag="grouped%d" % a, align_bytes=64)
+            copy(
                 grouped[:].rearrange("p (t m j) -> p m t j", t=PACK, j=PACK),
                 w1_raw[a][:].rearrange("p j (m t) -> p m t j", t=PACK),
             )
             nc.vector.quantize_mx(out=w1_codes[:, a, :].bitcast(FP8X4), scales=w1_scales[:, a, :], in_=grouped[:])
 
-        for t in range(2, PACK):
-            page = ring.tile([P, T2], F32, name="page%d" % t, tag="grouped", align_bytes=64)
-            nc.gpsimd.memset(page[:], 0.0)
-            pages.append(page)
-
         for lo in (0, S // 2):
             nc.vector.tensor_copy(
                 v[1][:, lo : lo + S // 2], tab[1][:].bitcast(U32).indirect(idx[:, lo // 16 : (lo + S // 2) // 16])
             )
+
+        wgs_rows = wgs.rearrange("(q t) j -> q t j", t=PACK)
+        wg = keep.tile([P, PACK, S], F32, name="wg", tag="w1_raw1", align_bytes=64)
+        for t0, t1, e0, e1 in ((0, 2, 0, FIRST), (0, 2, FIRST, S), (2, PACK, 0, S)):
+            for g in range(P // QUAD):
+                nc.sync.dma_start(wg[g * QUAD : (g + 1) * QUAD, t0:t1, e0:e1], wgs_rows[:, t0:t1, e0:e1])
+        page = keep.tile([P, T2], F32, name="page2", tag="big1", align_bytes=64)
+        nc.gpsimd.memset(page[:].bitcast(I32), 0)
+        pages = pages + [page, pages[0]]
+        saved = keep.tile([P, T2], F32, name="saved", align_bytes=64)
+
+        state_rows = state.rearrange("(p t) n -> p t n", t=PACK)
+        st = [keep.tile([P, PACK, T2 // 2], F32, name="st0", tag="grouped1", align_bytes=64)]
+        nc.sync.dma_start(st[0][:], state_rows[:, :, 0 : T2 // 2])
 
         h = [keep.tile([P, S], F32, name="h%d" % t, align_bytes=64) for t in range(PACK)]
 
@@ -189,14 +187,26 @@ def tile_list_neighbour_gap_message_kernel(
                     ahead = views(*units[u + 1])
                 gaps(*units[u], terms)
                 u = u + 1
-            wg = wg_lo if t < 2 else wg_hi
             nc.vector.tensor_tensor(
-                pages[t][:].indirect(idx2[:, e0 // 16 : e1 // 16]), h[t][:, e0:e1], wg[:, t % 2, e0:e1], ALU.mult
+                pages[t][:].indirect(idx2[:, e0 // 16 : e1 // 16]), h[t][:, e0:e1], wg[:, t, e0:e1], ALU.mult
             )
+            if e1 == S and t == 0:
+                nc.sync.dma_start(saved[:], pages[0][:])
 
+        w8 = keep.tile([P, N], I32, name="w8", tag="v0", align_bytes=64)
+        nc.sync.dma_start(w8[:], w8_words[0].rearrange("p c i -> p (c i)").bitcast(I32))
+        w8_plane = keep.tile([P, N], U8, name="w8_plane", tag="grouped0", align_bytes=64)
+        nc.vector.memset(w8_plane[:].bitcast(I32), 0)
+        for q in range(P // QUAD):
+            nc.sync.dma_start(
+                w8_plane[QUAD * q : QUAD * q + 4, :].bitcast(I32), w8_scales[0, 4 * q : 4 * q + 4, :].bitcast(I32)
+            )
+        st.append(keep.tile([P, PACK, T2 // 2], F32, name="st1", tag="v1", align_bytes=64))
+        nc.sync.dma_start(st[1][:], state_rows[:, :, T2 // 2 : T2])
+        filled = [saved] + pages[1:]
         first = NODE_CHUNKS[0]
         z_first = keep.tile([P, PACK * first], BF16, name="z_first", align_bytes=64)
-        z_rest = keep.tile([P, PACK * (T2 - first)], BF16, name="z_rest", tag="late", align_bytes=64)
+        z_rest = keep.tile([P, PACK * (T2 - first)], BF16, name="z_rest", tag="w1_raw1", align_bytes=64)
         starts = [sum(NODE_CHUNKS[:c]) for c in range(len(NODE_CHUNKS))]
 
         def z_chunk(c):
@@ -207,9 +217,9 @@ def tile_list_neighbour_gap_message_kernel(
         def maximum(c, t):
             if c < len(NODE_CHUNKS):
                 n0, width = starts[c], NODE_CHUNKS[c]
-                part, at = divmod(n0, BANK)
+                part, at = divmod(n0, T2 // 2)
                 nc.vector.tensor_tensor(
-                    z_chunk(c)[:, t, :], pages[t][:, n0 : n0 + width], st[part][:, t, at : at + width], ALU.max
+                    z_chunk(c)[:, t, :], filled[t][:, n0 : n0 + width], st[part][:, t, at : at + width], ALU.max
                 )
 
         def weave(c):
@@ -242,7 +252,7 @@ def tile_list_neighbour_gap_message_kernel(
                     nc.tensor.matmul_mx(
                         out=o_ps[:, k * width : (k + 1) * width],
                         lhsT=w8[:, b * P : (b + 1) * P].bitcast(FP8X4),
-                        lhsT_scale=planes[:, W8_AT + b * P : W8_AT + (b + 1) * P],
+                        lhsT_scale=w8_plane[:, b * P : (b + 1) * P],
                         rhs=z_codes[:, :width].bitcast(FP8X4),
                         rhs_scale=z_scales[:, :width],
                         start=True,

@@ -29,7 +29,7 @@ FIRST = 256
 
 SCATTERS = ((0, 0, 256), (1, 0, 256), (0, 256, 768), (1, 256, 1024), (0, 768, 1024), (2, 0, 1024), (3, 0, 1024))
 NODE_CHUNKS = (512, 512, 512, 256, 256)
-SCALAR_SHARE = 5
+SCALAR_SHARES = (11, 7, 6, 5, 5)
 
 
 def tile_list_neighbour_gap_message_kernel(
@@ -83,7 +83,8 @@ def tile_list_neighbour_gap_message_kernel(
             for q in range(P // QUAD):
                 src = ROWS * a + 4 * q
                 if src > 0:
-                    nc.scalar.dma_start(
+                    queue = nc.gpsimd if src >= ROWS + 8 else nc.scalar
+                    queue.dma_start(
                         planes[QUAD * q : QUAD * q + 4, a * PLANE : (a + 1) * PLANE].bitcast(I32),
                         planes[src : src + 4, 0:PLANE].bitcast(I32),
                     )
@@ -225,7 +226,7 @@ def tile_list_neighbour_gap_message_kernel(
         def weave(c):
             width = NODE_CHUNKS[c]
             woven = ring.tile([P, PACK * BANK], BF16, name="woven", align_bytes=64)
-            split = width * SCALAR_SHARE // 16
+            split = width * SCALAR_SHARES[c] // 16
             for lo, hi, copy in ((0, split, nc.scalar.copy), (split, width, nc.vector.tensor_copy)):
                 copy(
                     woven[:, PACK * lo : PACK * hi].rearrange("p (c i t) -> p c t i", i=4, t=PACK),

@@ -52,12 +52,12 @@ def tile_list_neighbour_gap_message_kernel(
         w1_raw = [
             keep.tile([P, PACK, H], F32, name="w1_raw%d" % a, tag="w1_raw%d" % a, align_bytes=64) for a in range(PASSES)
         ]
-        pages = [keep.tile([P, T2], F32, name="page%d" % t, align_bytes=64) for t in range(2)]
+        pages = [keep.tile([P, T2], F32, name="page%d" % t, align_bytes=64) for t in range(PACK - 1)]
         ident = keep.tile([P, P], F32, name="ident", align_bytes=64)
 
         live = PASSES * ROWS
         for lo, hi in ((QUAD, 2 * QUAD), (2 * QUAD, P)):
-            nc.gpsimd.memset(tsc[lo:hi, :].bitcast(I32), 0)
+            nc.vector.memset(tsc[lo:hi, :].bitcast(I32), 0)
             nc.vector.memset(w4s_raw[lo:hi, :].bitcast(I32), 0)
         nc.vector.memset(planes[:, PLANE:].bitcast(I32), 0)
         make_identity(nc, ident[:])
@@ -83,7 +83,7 @@ def tile_list_neighbour_gap_message_kernel(
             for q in range(P // QUAD):
                 src = ROWS * a + 4 * q
                 if src > 0:
-                    queue = nc.gpsimd if src >= ROWS + 8 else nc.scalar
+                    queue = nc.sync if src >= ROWS + 8 else nc.scalar
                     queue.dma_start(
                         planes[QUAD * q : QUAD * q + 4, a * PLANE : (a + 1) * PLANE].bitcast(I32),
                         planes[src : src + 4, 0:PLANE].bitcast(I32),
@@ -120,9 +120,7 @@ def tile_list_neighbour_gap_message_kernel(
         for t0, t1, e0, e1 in ((0, 2, 0, FIRST), (0, 2, FIRST, S), (2, PACK, 0, S)):
             for g in range(P // QUAD):
                 nc.sync.dma_start(wg[g * QUAD : (g + 1) * QUAD, t0:t1, e0:e1], wgs_rows[:, t0:t1, e0:e1])
-        page = keep.tile([P, T2], F32, name="page2", tag="big1", align_bytes=64)
-        nc.gpsimd.memset(page[:].bitcast(I32), 0)
-        pages = pages + [page, pages[0]]
+        pages = pages + [pages[0]]
         saved = keep.tile([P, T2], F32, name="saved", align_bytes=64)
 
         state_rows = state.rearrange("(p t) n -> p t n", t=PACK)

@@ -28,8 +28,9 @@ PLANE = S + H
 FIRST = 256
 
 SCATTERS = ((0, 0, 256), (1, 0, 256), (0, 256, 768), (1, 256, 1024), (0, 768, 1024), (2, 0, 1024), (3, 0, 1024))
-NODE_CHUNKS = (512, 512, 512, 256, 256)
-SCALAR_SHARES = (11, 7, 6, 5, 5)
+NODE_CHUNKS = (128, 128, 256, 512, 512, 256, 128, 128)
+HALF = T2 // 2
+PAIR = 2
 
 
 def tile_list_neighbour_gap_message_kernel(
@@ -121,7 +122,7 @@ def tile_list_neighbour_gap_message_kernel(
             for g in range(P // QUAD):
                 nc.sync.dma_start(wg[g * QUAD : (g + 1) * QUAD, t0:t1, e0:e1], wgs_rows[:, t0:t1, e0:e1])
         pages = pages + [pages[0]]
-        saved = keep.tile([P, T2], F32, name="saved", align_bytes=64)
+        stack = [keep.tile([P, PACK, HALF], F32, name="stack%d" % a, tag="big%d" % a, align_bytes=64) for a in range(2)]
 
         state_rows = state.rearrange("(p t) n -> p t n", t=PACK)
         st = [keep.tile([P, PACK, T2 // 2], F32, name="st0", tag="grouped1", align_bytes=64)]
@@ -189,8 +190,9 @@ def tile_list_neighbour_gap_message_kernel(
             nc.vector.tensor_tensor(
                 pages[t][:].indirect(idx2[:, e0 // 16 : e1 // 16]), h[t][:, e0:e1], wg[:, t, e0:e1], ALU.mult
             )
-            if e1 == S and t == 0:
-                nc.sync.dma_start(saved[:], pages[0][:])
+            if e1 == S and t < PACK - 1:
+                for part in range(2):
+                    nc.sync.dma_start(stack[part][:, t, :], pages[t][:, part * HALF : (part + 1) * HALF])
 
         w8 = keep.tile([P, N], I32, name="w8", tag="v0", align_bytes=64)
         nc.sync.dma_start(w8[:], w8_words[0].rearrange("p c i -> p (c i)").bitcast(I32))
@@ -202,34 +204,21 @@ def tile_list_neighbour_gap_message_kernel(
             )
         st.append(keep.tile([P, PACK, T2 // 2], F32, name="st1", tag="v1", align_bytes=64))
         nc.sync.dma_start(st[1][:], state_rows[:, :, T2 // 2 : T2])
-        filled = [saved] + pages[1:]
-        first = NODE_CHUNKS[0]
-        z_first = keep.tile([P, PACK * first], BF16, name="z_first", align_bytes=64)
-        z_rest = keep.tile([P, PACK * (T2 - first)], BF16, name="z_rest", tag="w1_raw1", align_bytes=64)
         starts = [sum(NODE_CHUNKS[:c]) for c in range(len(NODE_CHUNKS))]
+        for lo, hi in ((0, 128), (128, 256), (256, 512), (512, 1024), (1024, 2048)):
+            part, at = divmod(lo, HALF)
+            nc.scalar.copy(stack[part][:, PACK - 1, at : at + hi - lo], pages[PACK - 1][:, lo:hi])
 
-        def z_chunk(c):
+        def maximum(c):
             n0, width = starts[c], NODE_CHUNKS[c]
-            z = z_first[:] if c == 0 else z_rest[:, PACK * (n0 - first) : PACK * (n0 - first + width)]
-            return z.rearrange("p (t n) -> p t n", t=PACK)
-
-        def maximum(c, t):
-            if c < len(NODE_CHUNKS):
-                n0, width = starts[c], NODE_CHUNKS[c]
-                part, at = divmod(n0, T2 // 2)
-                nc.vector.tensor_tensor(
-                    z_chunk(c)[:, t, :], filled[t][:, n0 : n0 + width], st[part][:, t, at : at + width], ALU.max
-                )
-
-        def weave(c):
-            width = NODE_CHUNKS[c]
-            woven = ring.tile([P, PACK * BANK], BF16, name="woven", align_bytes=64)
-            split = width * SCALAR_SHARES[c] // 16
-            for lo, hi, copy in ((0, split, nc.scalar.copy), (split, width, nc.vector.tensor_copy)):
-                copy(
-                    woven[:, PACK * lo : PACK * hi].rearrange("p (c i t) -> p c t i", i=4, t=PACK),
-                    z_chunk(c)[:, :, lo:hi].rearrange("p t (c i) -> p c t i", i=4),
-                )
+            part, at = divmod(n0, HALF)
+            woven = ring.tile([P, PACK * BANK], BF16, name="woven", bufs=3, align_bytes=64)
+            nc.vector.tensor_tensor(
+                woven[:, : PACK * width].rearrange("p (c i t) -> p c t i", i=PAIR, t=PACK),
+                stack[part][:, :, at : at + width].rearrange("p t (c i) -> p c t i", i=PAIR),
+                st[part][:, :, at : at + width].rearrange("p t (c i) -> p c t i", i=PAIR),
+                ALU.max,
+            )
             return woven
 
         def quantise(c, woven):
@@ -243,7 +232,7 @@ def tile_list_neighbour_gap_message_kernel(
 
         def messages(c, z_codes, z_scales):
             n0, width = starts[c], NODE_CHUNKS[c]
-            per_bank = BANK // width
+            per_bank = 2 if c == len(NODE_CHUNKS) - 1 else BANK // width
             for b0 in range(0, N // P, per_bank):
                 o_ps = psum.tile([P, BANK], F32, name="o_ps", tag="bank")
                 for k in range(per_bank):
@@ -258,22 +247,20 @@ def tile_list_neighbour_gap_message_kernel(
                         stop=True,
                     )
                 o_sb = outs.tile([P, BANK], F32, name="o_sb", align_bytes=64)
+                used = per_bank * width
                 if c == len(NODE_CHUNKS) - 1 and b0 > 0:
-                    nc.vector.tensor_copy(o_sb[:], o_ps[:])
+                    nc.vector.tensor_copy(o_sb[:, :used], o_ps[:, :used])
                 else:
-                    nc.scalar.copy(o_sb[:], o_ps[:])
+                    nc.scalar.copy(o_sb[:, :used], o_ps[:, :used])
                 nc.sync.dma_start(
                     out[b0 * P : (b0 + per_bank) * P, n0 : n0 + width].rearrange("(k p) n -> p k n", p=P),
-                    o_sb[:].rearrange("p (k n) -> p k n", k=per_bank),
+                    o_sb[:, :used].rearrange("p (k n) -> p k n", k=per_bank),
                 )
 
-        for t in range(PACK):
-            maximum(0, t)
+        ahead = maximum(0)
         for c in range(len(NODE_CHUNKS)):
-            maximum(c + 1, 0)
-            woven = weave(c)
-            maximum(c + 1, 1)
-            maximum(c + 1, 2)
+            woven = ahead
+            if c + 1 < len(NODE_CHUNKS):
+                ahead = maximum(c + 1)
             z_codes, z_scales = quantise(c, woven)
-            maximum(c + 1, 3)
             messages(c, z_codes, z_scales)

@@ -28,9 +28,12 @@ PLANE = S + H
 FIRST = 256
 
 SCATTERS = ((0, 0, 256), (1, 0, 256), (0, 256, 768), (1, 256, 1024), (0, 768, 1024), (2, 0, 1024), (3, 0, 1024))
-NODE_CHUNKS = (128, 128, 256, 512, 512, 256, 128, 128)
+NODE_CHUNKS = (128, 128, 256, 256, 256, 256, 256, 256, 128, 128)
+LAST_COPIES = ((0, 128), (128, 256), (256, 512), (512, 1024), (1024, 2048))
 HALF = T2 // 2
 PAIR = 2
+EARLY_UNITS = (0, 2)
+QUAD_ORDER = (0, 2, 1, 3)
 
 
 def tile_list_neighbour_gap_message_kernel(
@@ -39,8 +42,9 @@ def tile_list_neighbour_gap_message_kernel(
     nc = tc.nc
     with ExitStack() as ctx:
         keep = ctx.enter_context(tc.tile_pool(name="keep", bufs=1))
+        laid = ctx.enter_context(tc.tile_pool(name="laid", bufs=1))
         ring = ctx.enter_context(tc.tile_pool(name="ring", bufs=2))
-        outs = ctx.enter_context(tc.tile_pool(name="outs", bufs=6))
+        outs = ctx.enter_context(tc.tile_pool(name="outs", bufs=12))
         psum = ctx.enter_context(tc.psum_pool(name="psum", bufs=8))
 
         idx = keep.tile([P, S // 16], U16, name="idx")
@@ -48,12 +52,9 @@ def tile_list_neighbour_gap_message_kernel(
         tsc = keep.tile([P, T], U8, name="tsc", align_bytes=64)
         w4s_raw = keep.tile([P, H], U8, name="w4s_raw", align_bytes=64)
         planes = keep.tile([P, PASSES * PLANE], U8, name="planes", align_bytes=64)
-        tab = [keep.tile([P, T], I32, name="tab%d" % a, tag="big%d" % a, align_bytes=64) for a in range(PASSES)]
+        tab = [laid.tile([P, T], I32, name="tab%d" % a, offset=(2 + 4 * a) * 4 * S, align_bytes=64) for a in range(PASSES)]
         w4_raw = keep.tile([P, PASSES, 2 * H], U8, name="w4_raw", align_bytes=64)
-        w1_raw = [
-            keep.tile([P, PACK, H], F32, name="w1_raw%d" % a, tag="w1_raw%d" % a, align_bytes=64) for a in range(PASSES)
-        ]
-        pages = [keep.tile([P, T2], F32, name="page%d" % t, align_bytes=64) for t in range(PACK - 1)]
+        pages = [keep.tile([P, T2], F32, name="page0", align_bytes=64)]
         ident = keep.tile([P, P], F32, name="ident", align_bytes=64)
 
         live = PASSES * ROWS
@@ -62,16 +63,18 @@ def tile_list_neighbour_gap_message_kernel(
             nc.vector.memset(w4s_raw[lo:hi, :].bitcast(I32), 0)
         nc.vector.memset(planes[:, PLANE:].bitcast(I32), 0)
         make_identity(nc, ident[:])
+        nc.gpsimd.memset(pages[0][:].bitcast(I32), 0)
 
+        w1_rows = w1.rearrange("(a p j) c -> a p j c", a=PASSES, j=PACK)
         nc.sync.dma_start(idx[:], offs)
         nc.sync.dma_start(tsc[0:live, :].bitcast(I32), tab_scales.rearrange("a q t -> (a q) t").bitcast(I32))
         nc.sync.dma_start(w4s_raw[0:live, :].bitcast(I32), w4_scales.rearrange("a q c -> (a q) c").bitcast(I32))
         nc.sync.dma_start(idx2[:], offs2)
         nc.sync.dma_start(w4_raw[:].bitcast(I32), w4_words.rearrange("a p b -> p a b").bitcast(I32))
-        nc.sync.dma_start(tab[0][:], tab_words[0].rearrange("p t i -> p (t i)").bitcast(I32))
         for a in range(PASSES):
-            nc.sync.dma_start(w1_raw[a][:], w1[a * 512 : (a + 1) * 512, :].rearrange("(p j) c -> p j c", j=PACK))
-        nc.sync.dma_start(tab[1][:], tab_words[1].rearrange("p t i -> p (t i)").bitcast(I32))
+            nc.sync.dma_start(tab[a][:], tab_words[a].rearrange("p t i -> p (t i)").bitcast(I32))
+        w1_raw = [keep.tile([P, PACK, H], F32, name="w1_raw0", tag="w1_raw0", align_bytes=64)]
+        nc.sync.dma_start(w1_raw[0][:], w1_rows[0])
 
         gsc = keep.tile([P, S], U8, name="gsc", align_bytes=64)
         nc.vector.tensor_copy(
@@ -84,92 +87,129 @@ def tile_list_neighbour_gap_message_kernel(
             for q in range(P // QUAD):
                 src = ROWS * a + 4 * q
                 if src > 0:
-                    queue = nc.sync if src >= ROWS + 8 else nc.scalar
+                    queue = nc.gpsimd if src == live - 4 else nc.scalar
                     queue.dma_start(
                         planes[QUAD * q : QUAD * q + 4, a * PLANE : (a + 1) * PLANE].bitcast(I32),
                         planes[src : src + 4, 0:PLANE].bitcast(I32),
                     )
-
-        for page in pages:
-            nc.vector.memset(page[:].bitcast(I32), 0)
-
-        v = [keep.tile([P, S], U32, name="v%d" % a, tag="v%d" % a, align_bytes=64) for a in range(PASSES)]
-        nc.vector.tensor_copy(v[0][:], tab[0][:].bitcast(U32).indirect(idx[:]))
-
         w4 = keep.tile([P, PASSES, 2 * H], U8, name="w4", align_bytes=64)
         nc.vector.tensor_copy(
             w4[:].bitcast(U16).rearrange("p a (t m) -> p a t m", t=PACK),
             w4_raw[:].bitcast(U16).rearrange("p a (m t) -> p a t m", t=PACK),
         )
-        w1_codes = keep.tile([P, PASSES, H], U32, name="w1_codes", align_bytes=64)
-        w1_scales = keep.tile([P, PASSES, H], U8, name="w1_scales", align_bytes=64)
-        for a, copy in enumerate((nc.scalar.copy, nc.vector.tensor_copy)):
-            grouped = keep.tile([P, H * PACK], BF16, name="grouped%d" % a, tag="grouped%d" % a, align_bytes=64)
-            copy(
-                grouped[:].rearrange("p (t m j) -> p m t j", t=PACK, j=PACK),
-                w1_raw[a][:].rearrange("p j (m t) -> p m t j", t=PACK),
-            )
-            nc.vector.quantize_mx(out=w1_codes[:, a, :].bitcast(FP8X4), scales=w1_scales[:, a, :], in_=grouped[:])
 
-        for lo in (0, S // 2):
-            nc.vector.tensor_copy(
-                v[1][:, lo : lo + S // 2], tab[1][:].bitcast(U32).indirect(idx[:, lo // 16 : (lo + S // 2) // 16])
-            )
+        v = [keep.tile([P, S], U32, name="v%d" % a, tag="v%d" % a, align_bytes=64) for a in range(PASSES)]
+        for a in range(PASSES):
+            nc.vector.tensor_copy(v[a][:], tab[a][:].bitcast(U32).indirect(idx[:]))
 
+        w1_raw.append(laid.tile([P, PACK, H], F32, name="w1_raw1", offset=2 * 4 * S, align_bytes=64))
+        nc.sync.dma_start(w1_raw[1][:], w1_rows[1])
         wgs_rows = wgs.rearrange("(q t) j -> q t j", t=PACK)
-        wg = keep.tile([P, PACK, S], F32, name="wg", tag="w1_raw1", align_bytes=64)
-        for t0, t1, e0, e1 in ((0, 2, 0, FIRST), (0, 2, FIRST, S), (2, PACK, 0, S)):
-            for g in range(P // QUAD):
-                nc.sync.dma_start(wg[g * QUAD : (g + 1) * QUAD, t0:t1, e0:e1], wgs_rows[:, t0:t1, e0:e1])
-        pages = pages + [pages[0]]
-        stack = [keep.tile([P, PACK, HALF], F32, name="stack%d" % a, tag="big%d" % a, align_bytes=64) for a in range(2)]
+        wg = [laid.tile([P, S], F32, name="wg%d" % t, offset=(4 + t) * 4 * S, align_bytes=64) for t in range(PACK)]
+        for t, e0, e1 in ((0, 0, FIRST), (1, 0, FIRST), (0, FIRST, S), (1, FIRST, S), (2, 0, S), (3, 0, S)):
+            for g in QUAD_ORDER:
+                nc.sync.dma_start(wg[t][g * QUAD : (g + 1) * QUAD, e0:e1], wgs_rows[:, t, e0:e1])
+
+        w1_codes = keep.tile([P, PASSES, H], U32, name="w1_codes", tag="w1_codes", align_bytes=64)
+        w1_scales = keep.tile([P, PASSES, H], U8, name="w1_scales", align_bytes=64)
+        grouped = [
+            keep.tile([P, H * PACK], BF16, name="grouped%d" % a, tag="grouped%d" % a, align_bytes=64)
+            for a in range(PASSES)
+        ]
+
+        def cast(a, t0, t1, copy):
+            copy(
+                grouped[a][:, t0 * BANK : t1 * BANK].rearrange("p (t m j) -> p m t j", t=t1 - t0, j=PACK),
+                w1_raw[a][:].rearrange("p j (m t) -> p m t j", t=PACK)[:, :, t0:t1, :],
+            )
+
+        def quantise_w1(a, t0, t1):
+            nc.vector.quantize_mx(
+                out=w1_codes[:, a, t0 * P : t1 * P].bitcast(FP8X4),
+                scales=w1_scales[:, a, t0 * P : t1 * P],
+                in_=grouped[a][:, t0 * BANK : t1 * BANK],
+            )
+
+        cast(0, 0, 1, nc.vector.tensor_copy)
+        cast(0, 1, PACK, nc.scalar.copy)
+        quantise_w1(0, 0, 1)
+        cast(1, 0, 1, nc.vector.tensor_copy)
+        quantise_w1(1, 0, 1)
+        cast(1, 1, PACK, nc.vector.tensor_copy)
+        for a in range(PASSES):
+            quantise_w1(a, 1, 2)
+        for a in range(PASSES):
+            quantise_w1(a, 2, PACK)
 
         state_rows = state.rearrange("(p t) n -> p t n", t=PACK)
-        st = [keep.tile([P, PACK, T2 // 2], F32, name="st0", tag="grouped1", align_bytes=64)]
-        nc.sync.dma_start(st[0][:], state_rows[:, :, 0 : T2 // 2])
+        st = [
+            keep.tile([P, PACK, HALF], F32, name="st0", tag="w1_raw0", align_bytes=64),
+            laid.tile([P, PACK, HALF], F32, name="st1", offset=0, align_bytes=64),
+        ]
+        for a in range(PASSES):
+            pages.append(keep.tile([P, T2], F32, name="page%d" % (a + 1), tag="grouped%d" % a, align_bytes=64))
+            nc.gpsimd.memset(pages[a + 1][:].bitcast(I32), 0)
+        for part in range(2):
+            nc.sync.dma_start(st[part][:], state_rows[:, :, part * HALF : (part + 1) * HALF])
 
         h = [keep.tile([P, S], F32, name="h%d" % t, align_bytes=64) for t in range(PACK)]
+        units = [(t, lo, min(lo + BANK, e1)) for t, e0, e1 in SCATTERS for lo in range(e0, e1, BANK)]
+        sums = {}
+        terms = {}
 
-        def views(t, e0, e1):
+        def products(u, a):
+            t, e0, e1 = units[u]
             blocks = (e1 - e0) // P
-            a_ps = psum.tile([P, BANK], F32, name="a_ps", tag="bank")
-            b_ps = psum.tile([P, BANK], F32, name="b_ps", tag="bank")
-            for a in range(PASSES):
-                for acc, is_w1 in ((a_ps, True), (b_ps, False)):
-                    if is_w1:
-                        rhs = w1_codes[:, a, t * P : (t + 1) * P].bitcast(FP8X4)
-                        rhs_scale = w1_scales[:, a, t * P : (t + 1) * P]
-                    else:
-                        rhs = w4[:, a, 2 * t * P : 2 * (t + 1) * P].bitcast(FP4X4)
-                        at = a * PLANE + W4_AT + t * P
-                        rhs_scale = planes[:, at : at + P]
-                    for b in range(blocks):
-                        e = e0 + b * P
-                        nc.tensor.matmul_mx(
-                            out=acc[:, b * P : (b + 1) * P],
-                            lhsT=v[a][:, e : e + P].bitcast(FP8X4),
-                            lhsT_scale=planes[:, a * PLANE + e : a * PLANE + e + P],
-                            rhs=rhs,
-                            rhs_scale=rhs_scale,
-                            start=(a == 0 and b == 0),
-                            stop=(a == PASSES - 1 and b == blocks - 1),
-                        )
-            width = e1 - e0
-            a_sb = ring.tile([P, BANK], F32, name="a_sb", bufs=3, align_bytes=64)
-            nb_sb = ring.tile([P, BANK], F32, name="nb_sb", bufs=3, align_bytes=64)
-            nc.scalar.activation(a_sb[:, :width], a_ps[:, :width], ACT.Relu)
-            nc.scalar.activation(nb_sb[:, :width], b_ps[:, :width], ACT.Copy, scale=-1.0)
-            return a_sb, nb_sb
+            if a == 0:
+                a_ps = psum.tile([P, BANK], F32, name="a_ps", tag="bank")
+                b_ps = psum.tile([P, BANK], F32, name="b_ps", tag="bank")
+                sums.setdefault(u, (a_ps, b_ps))
+            for k, acc in enumerate(sums[u]):
+                if k == 0:
+                    rhs = w1_codes[:, a, t * P : (t + 1) * P].bitcast(FP8X4)
+                    rhs_scale = w1_scales[:, a, t * P : (t + 1) * P]
+                else:
+                    rhs = w4[:, a, 2 * t * P : 2 * (t + 1) * P].bitcast(FP4X4)
+                    at = a * PLANE + W4_AT + t * P
+                    rhs_scale = planes[:, at : at + P]
+                for b in range(blocks):
+                    e = e0 + b * P
+                    nc.tensor.matmul_mx(
+                        out=acc[:, b * P : (b + 1) * P],
+                        lhsT=v[a][:, e : e + P].bitcast(FP8X4),
+                        lhsT_scale=planes[:, a * PLANE + e : a * PLANE + e + P],
+                        rhs=rhs,
+                        rhs_scale=rhs_scale,
+                        start=(a == 0 and b == 0),
+                        stop=(a == PASSES - 1 and b == blocks - 1),
+                    )
 
-        def gaps(t, e0, e1, terms):
+        def finish_products(u):
+            if u < len(units):
+                if u not in EARLY_UNITS:
+                    products(u, 0)
+                products(u, 1)
+
+        def term(u, k):
+            if u < len(units):
+                width = units[u][2] - units[u][1]
+                sb = ring.tile([P, BANK], F32, name="term%d" % k, tag="term%d" % k, bufs=3, align_bytes=64)
+                if k == 0:
+                    nc.scalar.activation(sb[:, :width], sums[u][0][:, :width], ACT.Relu)
+                else:
+                    nc.scalar.activation(sb[:, :width], sums[u][1][:, :width], ACT.Copy, scale=-1.0)
+                terms.setdefault(u, []).append(sb)
+
+        def gaps(u):
+            t, e0, e1 = units[u]
             width = e1 - e0
             blocks = width // P
             d_ps = psum.tile([P, BANK], F32, name="d_ps", tag="bank")
-            for k, term in enumerate(terms):
+            for k, sb in enumerate(terms[u]):
                 for b in range(blocks):
                     nc.tensor.matmul(
                         d_ps[:, b * P : (b + 1) * P],
-                        lhsT=term[:, b * P : (b + 1) * P],
+                        lhsT=sb[:, b * P : (b + 1) * P],
                         rhs=ident[:],
                         is_transpose=True,
                         start=(k == 0 and b == 0),
@@ -177,37 +217,40 @@ def tile_list_neighbour_gap_message_kernel(
                     )
             nc.scalar.activation(h[t][:, e0:e1], d_ps[:, :width], ACT.Abs)
 
-        units = [(t, lo, min(lo + BANK, e1)) for t, e0, e1 in SCATTERS for lo in range(e0, e1, BANK)]
-        ahead = views(*units[0])
-        u = 0
-        for t, e0, e1 in SCATTERS:
-            for lo in range(e0, e1, BANK):
-                terms = ahead
-                if u + 1 < len(units):
-                    ahead = views(*units[u + 1])
-                gaps(*units[u], terms)
-                u = u + 1
-            nc.vector.tensor_tensor(
-                pages[t][:].indirect(idx2[:, e0 // 16 : e1 // 16]), h[t][:, e0:e1], wg[:, t, e0:e1], ALU.mult
-            )
-            if e1 == S and t < PACK - 1:
-                for part in range(2):
-                    nc.sync.dma_start(stack[part][:, t, :], pages[t][:, part * HALF : (part + 1) * HALF])
+        for u in EARLY_UNITS:
+            products(u, 0)
+        finish_products(0)
+        term(0, 0)
+        term(0, 1)
+        finish_products(1)
+        for u in range(len(units)):
+            term(u + 1, 0)
+            gaps(u)
+            term(u + 1, 1)
+            finish_products(u + 2)
 
-        w8 = keep.tile([P, N], I32, name="w8", tag="v0", align_bytes=64)
+        pages = pages + [pages[0]]
+        stack = [
+            keep.tile([P, PACK, HALF], F32, name="stack%d" % part, tag="v%d" % part, align_bytes=64) for part in range(2)
+        ]
+        for t, e0, e1 in SCATTERS:
+            nc.vector.tensor_tensor(
+                pages[t][:].indirect(idx2[:, e0 // 16 : e1 // 16]), h[t][:, e0:e1], wg[t][:, e0:e1], ALU.mult
+            )
+            if e1 == S and t != 1:
+                for full in (0, 1) if t == 0 else (t,):
+                    for lo, hi in ((0, HALF), (HALF, T2)) if full < PACK - 1 else LAST_COPIES:
+                        part, at = divmod(lo, HALF)
+                        nc.scalar.copy(stack[part][:, full, at : at + hi - lo], pages[full][:, lo:hi])
+
+        w8 = keep.tile([P, N], I32, name="w8", tag="w1_codes", align_bytes=64)
         nc.sync.dma_start(w8[:], w8_words[0].rearrange("p c i -> p (c i)").bitcast(I32))
-        w8_plane = keep.tile([P, N], U8, name="w8_plane", tag="grouped0", align_bytes=64)
-        nc.vector.memset(w8_plane[:].bitcast(I32), 0)
+        w8_plane = planes[:, 0:N]
         for q in range(P // QUAD):
             nc.sync.dma_start(
-                w8_plane[QUAD * q : QUAD * q + 4, :].bitcast(I32), w8_scales[0, 4 * q : 4 * q + 4, :].bitcast(I32)
+                planes[QUAD * q : QUAD * q + 4, 0:N].bitcast(I32), w8_scales[0, 4 * q : 4 * q + 4, :].bitcast(I32)
             )
-        st.append(keep.tile([P, PACK, T2 // 2], F32, name="st1", tag="v1", align_bytes=64))
-        nc.sync.dma_start(st[1][:], state_rows[:, :, T2 // 2 : T2])
         starts = [sum(NODE_CHUNKS[:c]) for c in range(len(NODE_CHUNKS))]
-        for lo, hi in ((0, 128), (128, 256), (256, 512), (512, 1024), (1024, 2048)):
-            part, at = divmod(lo, HALF)
-            nc.scalar.copy(stack[part][:, PACK - 1, at : at + hi - lo], pages[PACK - 1][:, lo:hi])
 
         def maximum(c):
             n0, width = starts[c], NODE_CHUNKS[c]
@@ -248,7 +291,7 @@ def tile_list_neighbour_gap_message_kernel(
                     )
                 o_sb = outs.tile([P, BANK], F32, name="o_sb", align_bytes=64)
                 used = per_bank * width
-                if c == len(NODE_CHUNKS) - 1 and b0 > 0:
+                if c == len(NODE_CHUNKS) - 1:
                     nc.vector.tensor_copy(o_sb[:, :used], o_ps[:, :used])
                 else:
                     nc.scalar.copy(o_sb[:, :used], o_ps[:, :used])

@@ -30,6 +30,7 @@ FIRST = 256
 SCATTERS = ((0, 0, 256), (1, 0, 256), (0, 256, 768), (1, 256, 1024), (0, 768, 1024), (2, 0, 1024), (3, 0, 1024))
 NODE_CHUNKS = (128, 128, 256, 256, 256, 256, 256, 256, 128, 128)
 LAST_COPIES = ((0, 128), (128, 256), (256, 512), (512, 1024), (1024, 2048))
+KIB = 1024
 HALF = T2 // 2
 PAIR = 2
 EARLY_UNITS = (0, 2)
@@ -49,12 +50,11 @@ def tile_list_neighbour_gap_message_kernel(
 
         idx = keep.tile([P, S // 16], U16, name="idx")
         idx2 = keep.tile([P, S // 16], U16, name="idx2")
-        tsc = keep.tile([P, T], U8, name="tsc", align_bytes=64)
+        tsc = keep.tile([P, T], U8, name="tsc", tag="tsc", align_bytes=64)
         w4s_raw = keep.tile([P, H], U8, name="w4s_raw", align_bytes=64)
         planes = keep.tile([P, PASSES * PLANE], U8, name="planes", align_bytes=64)
-        tab = [laid.tile([P, T], I32, name="tab%d" % a, offset=(2 + 4 * a) * 4 * S, align_bytes=64) for a in range(PASSES)]
-        w4_raw = keep.tile([P, PASSES, 2 * H], U8, name="w4_raw", align_bytes=64)
-        pages = [keep.tile([P, T2], F32, name="page0", align_bytes=64)]
+        tab = [laid.tile([P, T], I32, name="tab%d" % a, offset=(16 + 16 * a) * KIB, align_bytes=64) for a in range(PASSES)]
+        w4_raw = keep.tile([P, PASSES, 2 * H], U8, name="w4_raw", tag="w4_raw", align_bytes=64)
         ident = keep.tile([P, P], F32, name="ident", align_bytes=64)
 
         live = PASSES * ROWS
@@ -63,7 +63,6 @@ def tile_list_neighbour_gap_message_kernel(
             nc.vector.memset(w4s_raw[lo:hi, :].bitcast(I32), 0)
         nc.vector.memset(planes[:, PLANE:].bitcast(I32), 0)
         make_identity(nc, ident[:])
-        nc.gpsimd.memset(pages[0][:].bitcast(I32), 0)
 
         w1_rows = w1.rearrange("(a p j) c -> a p j c", a=PASSES, j=PACK)
         nc.sync.dma_start(idx[:], offs)
@@ -83,15 +82,18 @@ def tile_list_neighbour_gap_message_kernel(
         )
         nc.vector.tensor_copy(gsc[:], tsc[:].indirect(idx[:]))
         nc.vector.tensor_copy(planes[:, 0:S].bitcast(I32), gsc[:].bitcast(I32))
-        for a in range(PASSES):
-            for q in range(P // QUAD):
-                src = ROWS * a + 4 * q
-                if src > 0:
-                    queue = nc.gpsimd if src == live - 4 else nc.scalar
-                    queue.dma_start(
-                        planes[QUAD * q : QUAD * q + 4, a * PLANE : (a + 1) * PLANE].bitcast(I32),
-                        planes[src : src + 4, 0:PLANE].bitcast(I32),
-                    )
+
+        def carry(a, q, queue):
+            src = ROWS * a + 4 * q
+            queue.dma_start(
+                planes[QUAD * q : QUAD * q + 4, a * PLANE : (a + 1) * PLANE].bitcast(I32),
+                planes[src : src + 4, 0:PLANE].bitcast(I32),
+            )
+
+        groups = [(a, q) for a in range(PASSES) for q in range(P // QUAD)]
+        for a, q in groups[1:-1]:
+            carry(a, q, nc.scalar)
+        carry(*groups[-1], nc.sync)
         w4 = keep.tile([P, PASSES, 2 * H], U8, name="w4", align_bytes=64)
         nc.vector.tensor_copy(
             w4[:].bitcast(U16).rearrange("p a (t m) -> p a t m", t=PACK),
@@ -99,13 +101,13 @@ def tile_list_neighbour_gap_message_kernel(
         )
 
         v = [keep.tile([P, S], U32, name="v%d" % a, tag="v%d" % a, align_bytes=64) for a in range(PASSES)]
-        for a in range(PASSES):
-            nc.vector.tensor_copy(v[a][:], tab[a][:].bitcast(U32).indirect(idx[:]))
+        nc.vector.tensor_copy(v[0][:], tab[0][:].bitcast(U32).indirect(idx[:]))
 
-        w1_raw.append(laid.tile([P, PACK, H], F32, name="w1_raw1", offset=2 * 4 * S, align_bytes=64))
+        w1_raw.append(laid.tile([P, PACK, H], F32, name="w1_raw1", offset=10 * KIB, align_bytes=64))
         nc.sync.dma_start(w1_raw[1][:], w1_rows[1])
+        nc.vector.tensor_copy(v[1][:], tab[1][:].bitcast(U32).indirect(idx[:]))
         wgs_rows = wgs.rearrange("(q t) j -> q t j", t=PACK)
-        wg = [laid.tile([P, S], F32, name="wg%d" % t, offset=(4 + t) * 4 * S, align_bytes=64) for t in range(PACK)]
+        wg = [laid.tile([P, S], F32, name="wg%d" % t, offset=(20, 24, 32, 36)[t] * KIB, align_bytes=64) for t in range(PACK)]
         for t, e0, e1 in ((0, 0, FIRST), (1, 0, FIRST), (0, FIRST, S), (1, FIRST, S), (2, 0, S), (3, 0, S)):
             for g in QUAD_ORDER:
                 nc.sync.dma_start(wg[t][g * QUAD : (g + 1) * QUAD, e0:e1], wgs_rows[:, t, e0:e1])
@@ -146,9 +148,12 @@ def tile_list_neighbour_gap_message_kernel(
             keep.tile([P, PACK, HALF], F32, name="st0", tag="w1_raw0", align_bytes=64),
             laid.tile([P, PACK, HALF], F32, name="st1", offset=0, align_bytes=64),
         ]
-        for a in range(PASSES):
-            pages.append(keep.tile([P, T2], F32, name="page%d" % (a + 1), tag="grouped%d" % a, align_bytes=64))
-            nc.gpsimd.memset(pages[a + 1][:].bitcast(I32), 0)
+        pages = [
+            keep.tile([P, T2], F32, name="page%d" % t, tag=tag, align_bytes=64)
+            for t, tag in enumerate(("page0", "tsc", "w4_raw"))
+        ]
+        for page in pages:
+            nc.vector.memset(page[:].bitcast(I32), 0)
         for part in range(2):
             nc.sync.dma_start(st[part][:], state_rows[:, :, part * HALF : (part + 1) * HALF])
 

@@ -27,7 +27,10 @@ W4_AT = S
 PLANE = S + H
 FIRST = 256
 
-SCATTERS = ((0, 0, 256), (1, 0, 256), (0, 256, 768), (1, 256, 1024), (0, 768, 1024), (2, 0, 1024), (3, 0, 1024))
+SCATTERS = (
+    (0, 0, 256), (1, 0, 256), (0, 256, 768), (1, 256, 768), (0, 768, 1024), (1, 768, 1024),
+    (2, 0, 512), (3, 0, 256), (2, 512, 1024), (3, 256, 1024),
+)
 NODE_CHUNKS = (128, 128, 256, 256, 256, 256, 256, 256, 128, 128)
 LAST_COPIES = ((0, 128), (128, 256), (256, 512), (512, 1024), (1024, 2048))
 KIB = 1024
@@ -107,10 +110,18 @@ def tile_list_neighbour_gap_message_kernel(
         nc.sync.dma_start(w1_raw[1][:], w1_rows[1])
         nc.vector.tensor_copy(v[1][:], tab[1][:].bitcast(U32).indirect(idx[:]))
         wgs_rows = wgs.rearrange("(q t) j -> q t j", t=PACK)
-        wg = [laid.tile([P, S], F32, name="wg%d" % t, offset=(20, 24, 32, 36)[t] * KIB, align_bytes=64) for t in range(PACK)]
-        for t, e0, e1 in ((0, 0, FIRST), (1, 0, FIRST), (0, FIRST, S), (1, FIRST, S), (2, 0, S), (3, 0, S)):
+        wg = [laid.tile([P, 2, S], F32, name="wg%d" % k, offset=(20 + 12 * k) * KIB, align_bytes=64) for k in range(2)]
+        for k, e0, e1 in ((0, 0, FIRST), (0, FIRST, S), (1, 0, S)):
             for g in QUAD_ORDER:
-                nc.sync.dma_start(wg[t][g * QUAD : (g + 1) * QUAD, e0:e1], wgs_rows[:, t, e0:e1])
+                nc.sync.dma_start(wg[k][g * QUAD : (g + 1) * QUAD, :, e0:e1], wgs_rows[:, 2 * k : 2 * k + 2, e0:e1])
+        w8 = laid.tile([P, N], I32, name="w8", offset=40 * KIB, align_bytes=64)
+        w8_plane = laid.tile([P, N], U8, name="w8_plane", offset=42 * KIB, align_bytes=64)
+        nc.vector.memset(w8_plane[:].bitcast(I32), 0)
+        nc.sync.dma_start(w8[:], w8_words[0].rearrange("p c i -> p (c i)").bitcast(I32))
+        for q in range(P // QUAD):
+            nc.sync.dma_start(
+                w8_plane[QUAD * q : QUAD * q + 4, :].bitcast(I32), w8_scales[0, 4 * q : 4 * q + 4, :].bitcast(I32)
+            )
 
         w1_codes = keep.tile([P, PASSES, H], U32, name="w1_codes", tag="w1_codes", align_bytes=64)
         w1_scales = keep.tile([P, PASSES, H], U8, name="w1_scales", align_bytes=64)
@@ -137,7 +148,8 @@ def tile_list_neighbour_gap_message_kernel(
         quantise_w1(0, 0, 1)
         cast(1, 0, 1, nc.vector.tensor_copy)
         quantise_w1(1, 0, 1)
-        cast(1, 1, PACK, nc.vector.tensor_copy)
+        cast(1, 2, PACK, nc.scalar.copy)
+        cast(1, 1, 2, nc.vector.tensor_copy)
         for a in range(PASSES):
             quantise_w1(a, 1, 2)
         for a in range(PASSES):
@@ -150,10 +162,10 @@ def tile_list_neighbour_gap_message_kernel(
         ]
         pages = [
             keep.tile([P, T2], F32, name="page%d" % t, tag=tag, align_bytes=64)
-            for t, tag in enumerate(("page0", "tsc", "w4_raw"))
+            for t, tag in enumerate(("page0", "tsc", "grouped0", "grouped1"))
         ]
-        for page in pages:
-            nc.vector.memset(page[:].bitcast(I32), 0)
+        for t, page in enumerate(pages):
+            (nc.vector if t < 2 else nc.gpsimd).memset(page[:].bitcast(I32), 0)
         for part in range(2):
             nc.sync.dma_start(st[part][:], state_rows[:, :, part * HALF : (part + 1) * HALF])
 
@@ -234,27 +246,19 @@ def tile_list_neighbour_gap_message_kernel(
             term(u + 1, 1)
             finish_products(u + 2)
 
-        pages = pages + [pages[0]]
         stack = [
-            keep.tile([P, PACK, HALF], F32, name="stack%d" % part, tag="v%d" % part, align_bytes=64) for part in range(2)
+            keep.tile([P, PACK, HALF], F32, name="stack%d" % part, align_bytes=64) for part in range(2)
         ]
         for t, e0, e1 in SCATTERS:
             nc.vector.tensor_tensor(
-                pages[t][:].indirect(idx2[:, e0 // 16 : e1 // 16]), h[t][:, e0:e1], wg[t][:, e0:e1], ALU.mult
+                pages[t][:].indirect(idx2[:, e0 // 16 : e1 // 16]), h[t][:, e0:e1], wg[t // 2][:, t % 2, e0:e1], ALU.mult
             )
-            if e1 == S and t != 1:
-                for full in (0, 1) if t == 0 else (t,):
-                    for lo, hi in ((0, HALF), (HALF, T2)) if full < PACK - 1 else LAST_COPIES:
-                        part, at = divmod(lo, HALF)
-                        nc.scalar.copy(stack[part][:, full, at : at + hi - lo], pages[full][:, lo:hi])
+            if e1 == S:
+                move = nc.sync.dma_start if t < PACK - 1 else nc.scalar.copy
+                for lo, hi in ((0, HALF), (HALF, T2)) if t < PACK - 1 else LAST_COPIES:
+                    part, at = divmod(lo, HALF)
+                    move(stack[part][:, t, at : at + hi - lo], pages[t][:, lo:hi])
 
-        w8 = keep.tile([P, N], I32, name="w8", tag="w1_codes", align_bytes=64)
-        nc.sync.dma_start(w8[:], w8_words[0].rearrange("p c i -> p (c i)").bitcast(I32))
-        w8_plane = planes[:, 0:N]
-        for q in range(P // QUAD):
-            nc.sync.dma_start(
-                planes[QUAD * q : QUAD * q + 4, 0:N].bitcast(I32), w8_scales[0, 4 * q : 4 * q + 4, :].bitcast(I32)
-            )
         starts = [sum(NODE_CHUNKS[:c]) for c in range(len(NODE_CHUNKS))]
 
         def maximum(c):

@@ -72,7 +72,6 @@ def tile_list_neighbour_gap_message_kernel(
         nc.sync.dma_start(tsc[0:live, :].bitcast(I32), tab_scales.rearrange("a q t -> (a q) t").bitcast(I32))
         nc.sync.dma_start(w4s_raw[0:live, :].bitcast(I32), w4_scales.rearrange("a q c -> (a q) c").bitcast(I32))
         nc.sync.dma_start(idx2[:], offs2)
-        nc.sync.dma_start(w4_raw[:].bitcast(I32), w4_words.rearrange("a p b -> p a b").bitcast(I32))
         for a in range(PASSES):
             nc.sync.dma_start(tab[a][:], tab_words[a].rearrange("p t i -> p (t i)").bitcast(I32))
         w1_raw = [keep.tile([P, PACK, H], F32, name="w1_raw0", tag="w1_raw0", align_bytes=64)]
@@ -98,20 +97,24 @@ def tile_list_neighbour_gap_message_kernel(
             carry(a, q, nc.scalar)
         carry(*groups[-1], nc.sync)
         w4 = keep.tile([P, PASSES, 2 * H], U8, name="w4", align_bytes=64)
-        nc.vector.tensor_copy(
-            w4[:].bitcast(U16).rearrange("p a (t m) -> p a t m", t=PACK),
-            w4_raw[:].bitcast(U16).rearrange("p a (m t) -> p a t m", t=PACK),
-        )
+
+        def order_w4(t0, t1):
+            nc.vector.tensor_copy(
+                w4[:].bitcast(U16).rearrange("p a (t m) -> p a t m", t=PACK)[:, :, t0:t1, :],
+                w4_raw[:].bitcast(U16).rearrange("p a (m t) -> p a t m", t=PACK)[:, :, t0:t1, :],
+            )
+
 
         v = [keep.tile([P, S], U32, name="v%d" % a, tag="v%d" % a, align_bytes=64) for a in range(PASSES)]
         nc.vector.tensor_copy(v[0][:], tab[0][:].bitcast(U32).indirect(idx[:]))
 
-        w1_raw.append(laid.tile([P, PACK, H], F32, name="w1_raw1", offset=10 * KIB, align_bytes=64))
+        w1_raw.append(laid.tile([P, PACK, H], F32, name="w1_raw1", offset=0, align_bytes=64))
         nc.sync.dma_start(w1_raw[1][:], w1_rows[1])
+        nc.sync.dma_start(w4_raw[:].bitcast(I32), w4_words.rearrange("a p b -> p a b").bitcast(I32))
         nc.vector.tensor_copy(v[1][:], tab[1][:].bitcast(U32).indirect(idx[:]))
         wgs_rows = wgs.rearrange("(q t) j -> q t j", t=PACK)
         wg = [laid.tile([P, 2, S], F32, name="wg%d" % k, offset=(20 + 12 * k) * KIB, align_bytes=64) for k in range(2)]
-        for k, e0, e1 in ((0, 0, FIRST), (0, FIRST, S), (1, 0, S)):
+        for k, e0, e1 in ((0, 0, FIRST), (0, FIRST, S - FIRST), (0, S - FIRST, S), (1, 0, S)):
             for g in QUAD_ORDER:
                 nc.sync.dma_start(wg[k][g * QUAD : (g + 1) * QUAD, :, e0:e1], wgs_rows[:, 2 * k : 2 * k + 2, e0:e1])
         w8 = laid.tile([P, N], I32, name="w8", offset=40 * KIB, align_bytes=64)
@@ -147,11 +150,14 @@ def tile_list_neighbour_gap_message_kernel(
         cast(0, 1, PACK, nc.scalar.copy)
         quantise_w1(0, 0, 1)
         cast(1, 0, 1, nc.vector.tensor_copy)
+        order_w4(0, 1)
         quantise_w1(1, 0, 1)
         cast(1, 2, PACK, nc.scalar.copy)
         cast(1, 1, 2, nc.vector.tensor_copy)
+        order_w4(1, 2)
         for a in range(PASSES):
             quantise_w1(a, 1, 2)
+        order_w4(2, PACK)
         for a in range(PASSES):
             quantise_w1(a, 2, PACK)
 
@@ -174,14 +180,15 @@ def tile_list_neighbour_gap_message_kernel(
         sums = {}
         terms = {}
 
-        def products(u, a):
+        def products(u, a, sides=(0, 1)):
             t, e0, e1 = units[u]
             blocks = (e1 - e0) // P
-            if a == 0:
+            if u not in sums:
                 a_ps = psum.tile([P, BANK], F32, name="a_ps", tag="bank")
                 b_ps = psum.tile([P, BANK], F32, name="b_ps", tag="bank")
                 sums.setdefault(u, (a_ps, b_ps))
-            for k, acc in enumerate(sums[u]):
+            for k in sides:
+                acc = sums[u][k]
                 if k == 0:
                     rhs = w1_codes[:, a, t * P : (t + 1) * P].bitcast(FP8X4)
                     rhs_scale = w1_scales[:, a, t * P : (t + 1) * P]
@@ -204,8 +211,10 @@ def tile_list_neighbour_gap_message_kernel(
         def finish_products(u):
             if u < len(units):
                 if u not in EARLY_UNITS:
-                    products(u, 0)
-                products(u, 1)
+                    products(u, 0, (0,))
+                products(u, 1, (0,))
+                for a in range(PASSES):
+                    products(u, a, (1,))
 
         def term(u, k):
             if u < len(units):
@@ -235,7 +244,7 @@ def tile_list_neighbour_gap_message_kernel(
             nc.scalar.activation(h[t][:, e0:e1], d_ps[:, :width], ACT.Abs)
 
         for u in EARLY_UNITS:
-            products(u, 0)
+            products(u, 0, (0,))
         finish_products(0)
         term(0, 0)
         term(0, 1)
@@ -247,14 +256,14 @@ def tile_list_neighbour_gap_message_kernel(
             finish_products(u + 2)
 
         stack = [
-            keep.tile([P, PACK, HALF], F32, name="stack%d" % part, align_bytes=64) for part in range(2)
+            keep.tile([P, PACK, HALF], F32, name="stack%d" % part, tag="v%d" % part, align_bytes=64) for part in range(2)
         ]
         for t, e0, e1 in SCATTERS:
             nc.vector.tensor_tensor(
                 pages[t][:].indirect(idx2[:, e0 // 16 : e1 // 16]), h[t][:, e0:e1], wg[t // 2][:, t % 2, e0:e1], ALU.mult
             )
             if e1 == S:
-                move = nc.sync.dma_start if t < PACK - 1 else nc.scalar.copy
+                move = nc.sync.dma_start if t == PACK - 2 else nc.scalar.copy
                 for lo, hi in ((0, HALF), (HALF, T2)) if t < PACK - 1 else LAST_COPIES:
                     part, at = divmod(lo, HALF)
                     move(stack[part][:, t, at : at + hi - lo], pages[t][:, lo:hi])

@@ -72,6 +72,7 @@ def tile_list_neighbour_gap_message_kernel(
         nc.sync.dma_start(tsc[0:live, :].bitcast(I32), tab_scales.rearrange("a q t -> (a q) t").bitcast(I32))
         nc.sync.dma_start(w4s_raw[0:live, :].bitcast(I32), w4_scales.rearrange("a q c -> (a q) c").bitcast(I32))
         nc.sync.dma_start(idx2[:], offs2)
+        nc.sync.dma_start(w4_raw[:].bitcast(I32), w4_words.rearrange("a p b -> p a b").bitcast(I32))
         for a in range(PASSES):
             nc.sync.dma_start(tab[a][:], tab_words[a].rearrange("p t i -> p (t i)").bitcast(I32))
         w1_raw = [keep.tile([P, PACK, H], F32, name="w1_raw0", tag="w1_raw0", align_bytes=64)]
@@ -105,12 +106,13 @@ def tile_list_neighbour_gap_message_kernel(
             )
 
 
+        order_w4(0, PACK)
+
         v = [keep.tile([P, S], U32, name="v%d" % a, tag="v%d" % a, align_bytes=64) for a in range(PASSES)]
         nc.vector.tensor_copy(v[0][:], tab[0][:].bitcast(U32).indirect(idx[:]))
 
         w1_raw.append(laid.tile([P, PACK, H], F32, name="w1_raw1", offset=0, align_bytes=64))
         nc.sync.dma_start(w1_raw[1][:], w1_rows[1])
-        nc.sync.dma_start(w4_raw[:].bitcast(I32), w4_words.rearrange("a p b -> p a b").bitcast(I32))
         nc.vector.tensor_copy(v[1][:], tab[1][:].bitcast(U32).indirect(idx[:]))
         wgs_rows = wgs.rearrange("(q t) j -> q t j", t=PACK)
         wg = [laid.tile([P, 2, S], F32, name="wg%d" % k, offset=(20 + 12 * k) * KIB, align_bytes=64) for k in range(2)]
@@ -128,14 +130,11 @@ def tile_list_neighbour_gap_message_kernel(
 
         w1_codes = keep.tile([P, PASSES, H], U32, name="w1_codes", tag="w1_codes", align_bytes=64)
         w1_scales = keep.tile([P, PASSES, H], U8, name="w1_scales", align_bytes=64)
-        grouped = [
-            keep.tile([P, H * PACK], BF16, name="grouped%d" % a, tag="grouped%d" % a, align_bytes=64)
-            for a in range(PASSES)
-        ]
+        grouped = laid.tile([P, PASSES, H * PACK], BF16, name="grouped", offset=52 * KIB, align_bytes=64)
 
         def cast(a, t0, t1, copy):
             copy(
-                grouped[a][:, t0 * BANK : t1 * BANK].rearrange("p (t m j) -> p m t j", t=t1 - t0, j=PACK),
+                grouped[:, a, t0 * BANK : t1 * BANK].rearrange("p (t m j) -> p m t j", t=t1 - t0, j=PACK),
                 w1_raw[a][:].rearrange("p j (m t) -> p m t j", t=PACK)[:, :, t0:t1, :],
             )
 
@@ -143,35 +142,24 @@ def tile_list_neighbour_gap_message_kernel(
             nc.vector.quantize_mx(
                 out=w1_codes[:, a, t0 * P : t1 * P].bitcast(FP8X4),
                 scales=w1_scales[:, a, t0 * P : t1 * P],
-                in_=grouped[a][:, t0 * BANK : t1 * BANK],
+                in_=grouped[:, a, t0 * BANK : t1 * BANK],
             )
 
         cast(0, 0, 1, nc.vector.tensor_copy)
         cast(0, 1, PACK, nc.scalar.copy)
         quantise_w1(0, 0, 1)
         cast(1, 0, 1, nc.vector.tensor_copy)
-        order_w4(0, 1)
         quantise_w1(1, 0, 1)
         cast(1, 2, PACK, nc.scalar.copy)
         cast(1, 1, 2, nc.vector.tensor_copy)
-        order_w4(1, 2)
         for a in range(PASSES):
             quantise_w1(a, 1, 2)
-        order_w4(2, PACK)
-        for a in range(PASSES):
-            quantise_w1(a, 2, PACK)
 
         state_rows = state.rearrange("(p t) n -> p t n", t=PACK)
         st = [
             keep.tile([P, PACK, HALF], F32, name="st0", tag="w1_raw0", align_bytes=64),
             laid.tile([P, PACK, HALF], F32, name="st1", offset=0, align_bytes=64),
         ]
-        pages = [
-            keep.tile([P, T2], F32, name="page%d" % t, tag=tag, align_bytes=64)
-            for t, tag in enumerate(("page0", "tsc", "grouped0", "grouped1"))
-        ]
-        for t, page in enumerate(pages):
-            (nc.vector if t < 2 else nc.gpsimd).memset(page[:].bitcast(I32), 0)
         for part in range(2):
             nc.sync.dma_start(st[part][:], state_rows[:, :, part * HALF : (part + 1) * HALF])
 
@@ -180,15 +168,14 @@ def tile_list_neighbour_gap_message_kernel(
         sums = {}
         terms = {}
 
-        def products(u, a, sides=(0, 1)):
+        def products(u, a):
             t, e0, e1 = units[u]
             blocks = (e1 - e0) // P
             if u not in sums:
                 a_ps = psum.tile([P, BANK], F32, name="a_ps", tag="bank")
                 b_ps = psum.tile([P, BANK], F32, name="b_ps", tag="bank")
                 sums.setdefault(u, (a_ps, b_ps))
-            for k in sides:
-                acc = sums[u][k]
+            for k, acc in enumerate(sums[u]) if u > 1 else reversed(list(enumerate(sums[u]))):
                 if k == 0:
                     rhs = w1_codes[:, a, t * P : (t + 1) * P].bitcast(FP8X4)
                     rhs_scale = w1_scales[:, a, t * P : (t + 1) * P]
@@ -198,12 +185,17 @@ def tile_list_neighbour_gap_message_kernel(
                     rhs_scale = planes[:, at : at + P]
                 for b in range(blocks):
                     e = e0 + b * P
+                    sides = [
+                        (v[a][:, e : e + P].bitcast(FP8X4), planes[:, a * PLANE + e : a * PLANE + e + P]),
+                        (rhs, rhs_scale),
+                    ]
+                    still, moving = sides if u > 1 else reversed(sides)
                     nc.tensor.matmul_mx(
                         out=acc[:, b * P : (b + 1) * P],
-                        lhsT=v[a][:, e : e + P].bitcast(FP8X4),
-                        lhsT_scale=planes[:, a * PLANE + e : a * PLANE + e + P],
-                        rhs=rhs,
-                        rhs_scale=rhs_scale,
+                        lhsT=still[0],
+                        lhsT_scale=still[1],
+                        rhs=moving[0],
+                        rhs_scale=moving[1],
                         start=(a == 0 and b == 0),
                         stop=(a == PASSES - 1 and b == blocks - 1),
                     )
@@ -211,10 +203,8 @@ def tile_list_neighbour_gap_message_kernel(
         def finish_products(u):
             if u < len(units):
                 if u not in EARLY_UNITS:
-                    products(u, 0, (0,))
-                products(u, 1, (0,))
-                for a in range(PASSES):
-                    products(u, a, (1,))
+                    products(u, 0)
+                products(u, 1)
 
         def term(u, k):
             if u < len(units):
@@ -244,17 +234,31 @@ def tile_list_neighbour_gap_message_kernel(
             nc.scalar.activation(h[t][:, e0:e1], d_ps[:, :width], ACT.Abs)
 
         for u in EARLY_UNITS:
-            products(u, 0, (0,))
-        finish_products(0)
-        term(0, 0)
-        term(0, 1)
-        finish_products(1)
-        for u in range(len(units)):
+            products(u, 0)
+        for u in range(2):
+            finish_products(u)
+            b_first = keep.tile([P, FIRST], F32, name="b_first%d" % u, align_bytes=64)
+            d_first = keep.tile([P, FIRST], F32, name="d_first%d" % u, align_bytes=64)
+            nc.scalar.copy(b_first[:], sums[u][1][:, :FIRST])
+            nc.vector.scalar_tensor_tensor(d_first[:], sums[u][0][:, :FIRST], 0.0, b_first[:], ALU.max, ALU.subtract)
+            nc.scalar.activation(h[u][:, :FIRST], d_first[:], ACT.Abs)
+        for a in range(PASSES):
+            quantise_w1(a, 2, PACK)
+        finish_products(2)
+        term(2, 0)
+        term(2, 1)
+        finish_products(3)
+        for u in range(2, len(units)):
             term(u + 1, 0)
             gaps(u)
             term(u + 1, 1)
             finish_products(u + 2)
 
+        pages = [
+            keep.tile([P, T2], F32, name="page%d" % t, tag=tag, align_bytes=64) for t, tag in enumerate(("page0", "tsc"))
+        ] + [laid.tile([P, T2], F32, name="page%d" % t, offset=(32 + 8 * t) * KIB, align_bytes=64) for t in (2, 3)]
+        for t, page in enumerate(pages):
+            (nc.vector if t < 2 else nc.gpsimd).memset(page[:].bitcast(I32), 0)
         stack = [
             keep.tile([P, PACK, HALF], F32, name="stack%d" % part, tag="v%d" % part, align_bytes=64) for part in range(2)
         ]

@@ -26,9 +26,9 @@ ROWS = 16
 W4_AT = S
 PLANE = S + H
 FIRST = 256
+PIECES = ((0, FIRST), (FIRST, S - FIRST), (S - FIRST, S))
 
-SCATTERS = (
-    (0, 0, 256), (1, 0, 256), (0, 256, 768), (1, 256, 768), (0, 768, 1024), (1, 768, 1024),
+SCATTERS = tuple((t, e0, e1) for e0, e1 in PIECES for t in (0, 1)) + (
     (2, 0, 512), (3, 0, 256), (2, 512, 1024), (3, 256, 1024),
 )
 NODE_CHUNKS = (128, 128, 256, 256, 256, 256, 256, 256, 128, 128)
@@ -36,8 +36,10 @@ LAST_COPIES = ((0, 128), (128, 256), (256, 512), (512, 1024), (1024, 2048))
 KIB = 1024
 HALF = T2 // 2
 PAIR = 2
-EARLY_UNITS = (0, 2)
+EARLY_UNITS = 3
 QUAD_ORDER = (0, 2, 1, 3)
+DIRECT = 2
+WG_LOADS = ((0, 1, 0, FIRST), (1, 2, 0, FIRST), (0, 1, FIRST, S - FIRST), (1, 2, FIRST, S - FIRST), (0, 2, S - FIRST, S), (2, 4, 0, S))
 
 
 def tile_list_neighbour_gap_message_kernel(
@@ -56,27 +58,30 @@ def tile_list_neighbour_gap_message_kernel(
         tsc = keep.tile([P, T], U8, name="tsc", tag="tsc", align_bytes=64)
         w4s_raw = keep.tile([P, H], U8, name="w4s_raw", align_bytes=64)
         planes = keep.tile([P, PASSES * PLANE], U8, name="planes", align_bytes=64)
-        tab = [laid.tile([P, T], I32, name="tab%d" % a, offset=(16 + 16 * a) * KIB, align_bytes=64) for a in range(PASSES)]
-        w4_raw = keep.tile([P, PASSES, 2 * H], U8, name="w4_raw", tag="w4_raw", align_bytes=64)
+        tab = [
+            keep.tile([P, T], I32, name="tab0", tag="tab0", align_bytes=64),
+            laid.tile([P, T], I32, name="tab1", offset=0, align_bytes=64),
+        ]
+        w4_raw = keep.tile([P, PASSES, 2 * H], U8, name="w4_raw", align_bytes=64)
+        w1_raw = keep.tile([P, PASSES, PACK * H], F32, name="w1_raw", tag="w1_raw", align_bytes=64)
         ident = keep.tile([P, P], F32, name="ident", align_bytes=64)
 
         live = PASSES * ROWS
         for lo, hi in ((QUAD, 2 * QUAD), (2 * QUAD, P)):
-            nc.vector.memset(tsc[lo:hi, :].bitcast(I32), 0)
-            nc.vector.memset(w4s_raw[lo:hi, :].bitcast(I32), 0)
+            nc.gpsimd.memset(tsc[lo:hi, :].bitcast(I32), 0)
+            nc.gpsimd.memset(w4s_raw[lo:hi, :].bitcast(I32), 0)
         nc.vector.memset(planes[:, PLANE:].bitcast(I32), 0)
         make_identity(nc, ident[:])
+        pages = {}
 
-        w1_rows = w1.rearrange("(a p j) c -> a p j c", a=PASSES, j=PACK)
         nc.sync.dma_start(idx[:], offs)
         nc.sync.dma_start(tsc[0:live, :].bitcast(I32), tab_scales.rearrange("a q t -> (a q) t").bitcast(I32))
         nc.sync.dma_start(w4s_raw[0:live, :].bitcast(I32), w4_scales.rearrange("a q c -> (a q) c").bitcast(I32))
         nc.sync.dma_start(idx2[:], offs2)
         nc.sync.dma_start(w4_raw[:].bitcast(I32), w4_words.rearrange("a p b -> p a b").bitcast(I32))
-        for a in range(PASSES):
-            nc.sync.dma_start(tab[a][:], tab_words[a].rearrange("p t i -> p (t i)").bitcast(I32))
-        w1_raw = [keep.tile([P, PACK, H], F32, name="w1_raw0", tag="w1_raw0", align_bytes=64)]
-        nc.sync.dma_start(w1_raw[0][:], w1_rows[0])
+        nc.sync.dma_start(w1_raw[:], w1.rearrange("(a p j) c -> p a (j c)", a=PASSES, j=PACK))
+        tab_rows = tab_words.rearrange("a p t i -> a p (t i)").bitcast(I32)
+        nc.sync.dma_start(tab[0][:], tab_rows[0])
 
         gsc = keep.tile([P, S], U8, name="gsc", align_bytes=64)
         nc.vector.tensor_copy(
@@ -95,32 +100,22 @@ def tile_list_neighbour_gap_message_kernel(
 
         groups = [(a, q) for a in range(PASSES) for q in range(P // QUAD)]
         for a, q in groups[1:-1]:
-            carry(a, q, nc.scalar)
+            carry(a, q, nc.sync)
+        nc.sync.dma_start(tab[1][:], tab_rows[1])
         carry(*groups[-1], nc.sync)
         w4 = keep.tile([P, PASSES, 2 * H], U8, name="w4", align_bytes=64)
+        nc.vector.tensor_copy(
+            w4[:].bitcast(U16).rearrange("p a (t m) -> p a t m", t=PACK),
+            w4_raw[:].bitcast(U16).rearrange("p a (m t) -> p a t m", t=PACK),
+        )
 
-        def order_w4(t0, t1):
-            nc.vector.tensor_copy(
-                w4[:].bitcast(U16).rearrange("p a (t m) -> p a t m", t=PACK)[:, :, t0:t1, :],
-                w4_raw[:].bitcast(U16).rearrange("p a (m t) -> p a t m", t=PACK)[:, :, t0:t1, :],
-            )
-
-
-        order_w4(0, PACK)
-
-        v = [keep.tile([P, S], U32, name="v%d" % a, tag="v%d" % a, align_bytes=64) for a in range(PASSES)]
-        nc.vector.tensor_copy(v[0][:], tab[0][:].bitcast(U32).indirect(idx[:]))
-
-        w1_raw.append(laid.tile([P, PACK, H], F32, name="w1_raw1", offset=0, align_bytes=64))
-        nc.sync.dma_start(w1_raw[1][:], w1_rows[1])
-        nc.vector.tensor_copy(v[1][:], tab[1][:].bitcast(U32).indirect(idx[:]))
         wgs_rows = wgs.rearrange("(q t) j -> q t j", t=PACK)
-        wg = [laid.tile([P, 2, S], F32, name="wg%d" % k, offset=(20 + 12 * k) * KIB, align_bytes=64) for k in range(2)]
-        for k, e0, e1 in ((0, 0, FIRST), (0, FIRST, S - FIRST), (0, S - FIRST, S), (1, 0, S)):
+        wg = keep.tile([P, PACK, S], F32, name="wg", align_bytes=64)
+        for t0, t1, e0, e1 in WG_LOADS:
             for g in QUAD_ORDER:
-                nc.sync.dma_start(wg[k][g * QUAD : (g + 1) * QUAD, :, e0:e1], wgs_rows[:, 2 * k : 2 * k + 2, e0:e1])
-        w8 = laid.tile([P, N], I32, name="w8", offset=40 * KIB, align_bytes=64)
-        w8_plane = laid.tile([P, N], U8, name="w8_plane", offset=42 * KIB, align_bytes=64)
+                nc.sync.dma_start(wg[g * QUAD : (g + 1) * QUAD, t0:t1, e0:e1], wgs_rows[:, t0:t1, e0:e1])
+        w8 = keep.tile([P, N], I32, name="w8", align_bytes=64)
+        w8_plane = keep.tile([P, N], U8, name="w8_plane", align_bytes=64)
         nc.vector.memset(w8_plane[:].bitcast(I32), 0)
         nc.sync.dma_start(w8[:], w8_words[0].rearrange("p c i -> p (c i)").bitcast(I32))
         for q in range(P // QUAD):
@@ -130,35 +125,46 @@ def tile_list_neighbour_gap_message_kernel(
 
         w1_codes = keep.tile([P, PASSES, H], U32, name="w1_codes", tag="w1_codes", align_bytes=64)
         w1_scales = keep.tile([P, PASSES, H], U8, name="w1_scales", align_bytes=64)
-        grouped = laid.tile([P, PASSES, H * PACK], BF16, name="grouped", offset=52 * KIB, align_bytes=64)
-
-        def cast(a, t0, t1, copy):
+        grouped = keep.tile([P, PASSES, H * PACK], BF16, name="grouped", tag="grouped", align_bytes=64)
+        for a, t0, t1, copy in (
+            (0, 0, PACK, nc.vector.tensor_copy),
+            (1, 0, PACK, nc.scalar.copy),
+        ):
             copy(
                 grouped[:, a, t0 * BANK : t1 * BANK].rearrange("p (t m j) -> p m t j", t=t1 - t0, j=PACK),
-                w1_raw[a][:].rearrange("p j (m t) -> p m t j", t=PACK)[:, :, t0:t1, :],
+                w1_raw[:, a, :].rearrange("p (j m t) -> p m t j", j=PACK, t=PACK)[:, :, t0:t1, :],
             )
-
-        def quantise_w1(a, t0, t1):
-            nc.vector.quantize_mx(
-                out=w1_codes[:, a, t0 * P : t1 * P].bitcast(FP8X4),
-                scales=w1_scales[:, a, t0 * P : t1 * P],
-                in_=grouped[:, a, t0 * BANK : t1 * BANK],
-            )
-
-        cast(0, 0, 1, nc.vector.tensor_copy)
-        cast(0, 1, PACK, nc.scalar.copy)
-        quantise_w1(0, 0, 1)
-        cast(1, 0, 1, nc.vector.tensor_copy)
-        quantise_w1(1, 0, 1)
-        cast(1, 2, PACK, nc.scalar.copy)
-        cast(1, 1, 2, nc.vector.tensor_copy)
+        pages.setdefault(0, keep.tile([P, T2], F32, name="page0", align_bytes=64))
+        nc.vector.memset(pages[0][:].bitcast(I32), 0)
         for a in range(PASSES):
-            quantise_w1(a, 1, 2)
+            nc.vector.quantize_mx(
+                out=w1_codes[:, a, :].bitcast(FP8X4), scales=w1_scales[:, a, :], in_=grouped[:, a, :]
+            )
+        pages.setdefault(1, keep.tile([P, T2], F32, name="page1", tag="tsc", align_bytes=64))
+        nc.vector.memset(pages[1][:].bitcast(I32), 0)
+
+        v0 = keep.tile([P, S], U32, name="v0", tag="v0", align_bytes=64)
+        nc.vector.tensor_copy(v0[:], tab[0][:].bitcast(U32).indirect(idx[:]))
+        v1 = {}
+
+        def gather_last_pass(e0, e1, tag):
+            piece = keep.tile([P, e1 - e0], U32, name="v1_%d" % e0, tag=tag, align_bytes=64)
+            nc.vector.tensor_copy(piece[:], tab[1][:].bitcast(U32).indirect(idx[:, e0 // 16 : e1 // 16]))
+            v1.setdefault(e0, piece)
+
+        def looked_up(a, e0, e1):
+            if a == 0:
+                return v0[:, e0:e1]
+            lo = max(start for start in v1 if start <= e0)
+            return v1[lo][:, e0 - lo : e1 - lo]
+
+        for e0, e1 in PIECES[:2]:
+            gather_last_pass(e0, e1, "v1_%d" % e0)
 
         state_rows = state.rearrange("(p t) n -> p t n", t=PACK)
         st = [
-            keep.tile([P, PACK, HALF], F32, name="st0", tag="w1_raw0", align_bytes=64),
-            laid.tile([P, PACK, HALF], F32, name="st1", offset=0, align_bytes=64),
+            keep.tile([P, PACK, HALF], F32, name="st%d" % part, tag=tag, align_bytes=64)
+            for part, tag in enumerate(("w1_raw", "tab0"))
         ]
         for part in range(2):
             nc.sync.dma_start(st[part][:], state_rows[:, :, part * HALF : (part + 1) * HALF])
@@ -168,48 +174,59 @@ def tile_list_neighbour_gap_message_kernel(
         sums = {}
         terms = {}
 
+        def weights(k, a, t):
+            if k == 0:
+                return w1_codes[:, a, t * P : (t + 1) * P].bitcast(FP8X4), w1_scales[:, a, t * P : (t + 1) * P]
+            at = a * PLANE + W4_AT + t * P
+            return w4[:, a, 2 * t * P : 2 * (t + 1) * P].bitcast(FP4X4), planes[:, at : at + P]
+
         def products(u, a):
             t, e0, e1 = units[u]
-            blocks = (e1 - e0) // P
             if u not in sums:
                 a_ps = psum.tile([P, BANK], F32, name="a_ps", tag="bank")
                 b_ps = psum.tile([P, BANK], F32, name="b_ps", tag="bank")
                 sums.setdefault(u, (a_ps, b_ps))
-            for k, acc in enumerate(sums[u]) if u > 1 else reversed(list(enumerate(sums[u]))):
-                if k == 0:
-                    rhs = w1_codes[:, a, t * P : (t + 1) * P].bitcast(FP8X4)
-                    rhs_scale = w1_scales[:, a, t * P : (t + 1) * P]
-                else:
-                    rhs = w4[:, a, 2 * t * P : 2 * (t + 1) * P].bitcast(FP4X4)
-                    at = a * PLANE + W4_AT + t * P
-                    rhs_scale = planes[:, at : at + P]
+            if u < DIRECT:
+                for k in (1, 0):
+                    codes, scales = weights(k, a, t)
+                    nc.tensor.matmul_mx(
+                        out=sums[u][k][:, : e1 - e0],
+                        lhsT=codes,
+                        lhsT_scale=scales,
+                        rhs=looked_up(a, e0, e1).bitcast(FP8X4),
+                        rhs_scale=planes[:, a * PLANE + e0 : a * PLANE + e1],
+                        start=(a == 0),
+                        stop=(a == PASSES - 1),
+                    )
+                return
+            blocks = (e1 - e0) // P
+            for k, acc in enumerate(sums[u]):
+                codes, scales = weights(k, a, t)
                 for b in range(blocks):
                     e = e0 + b * P
-                    sides = [
-                        (v[a][:, e : e + P].bitcast(FP8X4), planes[:, a * PLANE + e : a * PLANE + e + P]),
-                        (rhs, rhs_scale),
-                    ]
-                    still, moving = sides if u > 1 else reversed(sides)
                     nc.tensor.matmul_mx(
                         out=acc[:, b * P : (b + 1) * P],
-                        lhsT=still[0],
-                        lhsT_scale=still[1],
-                        rhs=moving[0],
-                        rhs_scale=moving[1],
+                        lhsT=looked_up(a, e, e + P).bitcast(FP8X4),
+                        lhsT_scale=planes[:, a * PLANE + e : a * PLANE + e + P],
+                        rhs=codes,
+                        rhs_scale=scales,
                         start=(a == 0 and b == 0),
                         stop=(a == PASSES - 1 and b == blocks - 1),
                     )
 
         def finish_products(u):
             if u < len(units):
-                if u not in EARLY_UNITS:
+                if u >= EARLY_UNITS:
                     products(u, 0)
                 products(u, 1)
 
         def term(u, k):
             if u < len(units):
                 width = units[u][2] - units[u][1]
-                sb = ring.tile([P, BANK], F32, name="term%d" % k, tag="term%d" % k, bufs=3, align_bytes=64)
+                if k == 0 and u == DIRECT:
+                    sb = laid.tile([P, width], F32, name="behind", offset=16 * KIB, align_bytes=64)
+                else:
+                    sb = ring.tile([P, BANK], F32, name="term%d" % k, tag="term%d" % k, bufs=3, align_bytes=64)
                 if k == 0:
                     nc.scalar.activation(sb[:, :width], sums[u][0][:, :width], ACT.Relu)
                 else:
@@ -233,38 +250,36 @@ def tile_list_neighbour_gap_message_kernel(
                     )
             nc.scalar.activation(h[t][:, e0:e1], d_ps[:, :width], ACT.Abs)
 
-        for u in EARLY_UNITS:
+        for u in range(EARLY_UNITS):
             products(u, 0)
-        for u in range(2):
+        for u in range(DIRECT):
             finish_products(u)
-            b_first = keep.tile([P, FIRST], F32, name="b_first%d" % u, align_bytes=64)
-            d_first = keep.tile([P, FIRST], F32, name="d_first%d" % u, align_bytes=64)
+            b_first = keep.tile([P, FIRST], F32, name="b_first%d" % u, tag="b_first%d" % u, align_bytes=64)
+            d_first = laid.tile([P, FIRST], F32, name="d_first%d" % u, offset=(17 + u) * KIB, align_bytes=64)
             nc.scalar.copy(b_first[:], sums[u][1][:, :FIRST])
             nc.vector.scalar_tensor_tensor(d_first[:], sums[u][0][:, :FIRST], 0.0, b_first[:], ALU.max, ALU.subtract)
             nc.scalar.activation(h[u][:, :FIRST], d_first[:], ACT.Abs)
-        for a in range(PASSES):
-            quantise_w1(a, 2, PACK)
-        finish_products(2)
-        term(2, 0)
-        term(2, 1)
-        finish_products(3)
-        for u in range(2, len(units)):
+        gather_last_pass(*PIECES[2], "b_first%d" % (DIRECT - 1))
+        for t in (2, 3):
+            pages.setdefault(t, laid.tile([P, T2], F32, name="page%d" % t, offset=(t - 2) * 8 * KIB, align_bytes=64))
+            nc.gpsimd.memset(pages[t][:].bitcast(I32), 0)
+        finish_products(DIRECT)
+        term(DIRECT, 0)
+        term(DIRECT, 1)
+        finish_products(DIRECT + 1)
+        for u in range(DIRECT, len(units)):
             term(u + 1, 0)
             gaps(u)
             term(u + 1, 1)
             finish_products(u + 2)
 
-        pages = [
-            keep.tile([P, T2], F32, name="page%d" % t, tag=tag, align_bytes=64) for t, tag in enumerate(("page0", "tsc"))
-        ] + [laid.tile([P, T2], F32, name="page%d" % t, offset=(32 + 8 * t) * KIB, align_bytes=64) for t in (2, 3)]
-        for t, page in enumerate(pages):
-            (nc.vector if t < 2 else nc.gpsimd).memset(page[:].bitcast(I32), 0)
         stack = [
-            keep.tile([P, PACK, HALF], F32, name="stack%d" % part, tag="v%d" % part, align_bytes=64) for part in range(2)
+            keep.tile([P, PACK, HALF], F32, name="stack%d" % part, tag=tag, align_bytes=64)
+            for part, tag in enumerate(("v0", "w1_codes"))
         ]
         for t, e0, e1 in SCATTERS:
             nc.vector.tensor_tensor(
-                pages[t][:].indirect(idx2[:, e0 // 16 : e1 // 16]), h[t][:, e0:e1], wg[t // 2][:, t % 2, e0:e1], ALU.mult
+                pages[t][:].indirect(idx2[:, e0 // 16 : e1 // 16]), h[t][:, e0:e1], wg[:, t, e0:e1], ALU.mult
             )
             if e1 == S:
                 move = nc.sync.dma_start if t == PACK - 2 else nc.scalar.copy

@@ -26,7 +26,7 @@ ROWS = 16
 W4_AT = S
 PLANE = S + H
 FIRST = 256
-PIECES = ((0, FIRST), (FIRST, S - FIRST), (S - FIRST, S))
+PIECES = ((0, FIRST), (FIRST, 2 * FIRST), (2 * FIRST, S))
 
 SCATTERS = tuple((t, e0, e1) for e0, e1 in PIECES for t in (0, 1)) + (
     (2, 0, 512), (3, 0, 256), (2, 512, 1024), (3, 256, 1024),
@@ -36,10 +36,12 @@ LAST_COPIES = ((0, 128), (128, 256), (256, 512), (512, 1024), (1024, 2048))
 KIB = 1024
 HALF = T2 // 2
 PAIR = 2
-EARLY_UNITS = 3
+EARLY_UNITS = 4
 QUAD_ORDER = (0, 2, 1, 3)
 DIRECT = 2
-WG_LOADS = ((0, 1, 0, FIRST), (1, 2, 0, FIRST), (0, 1, FIRST, S - FIRST), (1, 2, FIRST, S - FIRST), (0, 2, S - FIRST, S), (2, 4, 0, S))
+AHEAD = 5
+TERM_BUFS = (3, AHEAD)
+WG_LOADS = tuple((t, t + 1, e0, e1) for e0, e1 in ((0, FIRST),) for t in (0, 1)) + ((0, 2, FIRST, 2 * FIRST), (0, 2, 2 * FIRST, S), (2, 4, 0, S))
 
 
 def tile_list_neighbour_gap_message_kernel(
@@ -58,12 +60,9 @@ def tile_list_neighbour_gap_message_kernel(
         tsc = keep.tile([P, T], U8, name="tsc", tag="tsc", align_bytes=64)
         w4s_raw = keep.tile([P, H], U8, name="w4s_raw", align_bytes=64)
         planes = keep.tile([P, PASSES * PLANE], U8, name="planes", align_bytes=64)
-        tab = [
-            keep.tile([P, T], I32, name="tab0", tag="tab0", align_bytes=64),
-            laid.tile([P, T], I32, name="tab1", offset=0, align_bytes=64),
-        ]
+        tab = [keep.tile([P, T], I32, name="tab%d" % a, tag="tab%d" % a, align_bytes=64) for a in range(PASSES)]
         w4_raw = keep.tile([P, PASSES, 2 * H], U8, name="w4_raw", align_bytes=64)
-        w1_raw = keep.tile([P, PASSES, PACK * H], F32, name="w1_raw", tag="w1_raw", align_bytes=64)
+        w1_raw = [keep.tile([P, PACK, H], F32, name="w1_raw%d" % a, align_bytes=64) for a in range(PASSES)]
         ident = keep.tile([P, P], F32, name="ident", align_bytes=64)
 
         live = PASSES * ROWS
@@ -79,9 +78,8 @@ def tile_list_neighbour_gap_message_kernel(
         nc.sync.dma_start(w4s_raw[0:live, :].bitcast(I32), w4_scales.rearrange("a q c -> (a q) c").bitcast(I32))
         nc.sync.dma_start(idx2[:], offs2)
         nc.sync.dma_start(w4_raw[:].bitcast(I32), w4_words.rearrange("a p b -> p a b").bitcast(I32))
-        nc.sync.dma_start(w1_raw[:], w1.rearrange("(a p j) c -> p a (j c)", a=PASSES, j=PACK))
-        tab_rows = tab_words.rearrange("a p t i -> a p (t i)").bitcast(I32)
-        nc.sync.dma_start(tab[0][:], tab_rows[0])
+        for a in range(PASSES):
+            nc.sync.dma_start(tab[a][:], tab_words[a].rearrange("p t i -> p (t i)").bitcast(I32))
 
         gsc = keep.tile([P, S], U8, name="gsc", align_bytes=64)
         nc.vector.tensor_copy(
@@ -101,8 +99,10 @@ def tile_list_neighbour_gap_message_kernel(
         groups = [(a, q) for a in range(PASSES) for q in range(P // QUAD)]
         for a, q in groups[1:-1]:
             carry(a, q, nc.sync)
-        nc.sync.dma_start(tab[1][:], tab_rows[1])
+        w1_rows = w1.rearrange("(a p j) c -> a p j c", a=PASSES, j=PACK)
+        nc.sync.dma_start(w1_raw[0][:], w1_rows[0])
         carry(*groups[-1], nc.sync)
+        nc.sync.dma_start(w1_raw[1][:], w1_rows[1])
         w4 = keep.tile([P, PASSES, 2 * H], U8, name="w4", align_bytes=64)
         nc.vector.tensor_copy(
             w4[:].bitcast(U16).rearrange("p a (t m) -> p a t m", t=PACK),
@@ -123,48 +123,34 @@ def tile_list_neighbour_gap_message_kernel(
                 w8_plane[QUAD * q : QUAD * q + 4, :].bitcast(I32), w8_scales[0, 4 * q : 4 * q + 4, :].bitcast(I32)
             )
 
-        w1_codes = keep.tile([P, PASSES, H], U32, name="w1_codes", tag="w1_codes", align_bytes=64)
-        w1_scales = keep.tile([P, PASSES, H], U8, name="w1_scales", align_bytes=64)
-        grouped = keep.tile([P, PASSES, H * PACK], BF16, name="grouped", tag="grouped", align_bytes=64)
-        for a, t0, t1, copy in (
-            (0, 0, PACK, nc.vector.tensor_copy),
-            (1, 0, PACK, nc.scalar.copy),
-        ):
-            copy(
-                grouped[:, a, t0 * BANK : t1 * BANK].rearrange("p (t m j) -> p m t j", t=t1 - t0, j=PACK),
-                w1_raw[:, a, :].rearrange("p (j m t) -> p m t j", j=PACK, t=PACK)[:, :, t0:t1, :],
-            )
-        pages.setdefault(0, keep.tile([P, T2], F32, name="page0", align_bytes=64))
-        nc.vector.memset(pages[0][:].bitcast(I32), 0)
+        for t, tag in enumerate(("page0", "tsc")):
+            pages.setdefault(t, keep.tile([P, T2], F32, name="page%d" % t, tag=tag, align_bytes=64))
+            nc.vector.memset(pages[t][:].bitcast(I32), 0)
+        v = [keep.tile([P, S], U32, name="v%d" % a, tag="v%d" % a, align_bytes=64) for a in range(PASSES)]
         for a in range(PASSES):
-            nc.vector.quantize_mx(
-                out=w1_codes[:, a, :].bitcast(FP8X4), scales=w1_scales[:, a, :], in_=grouped[:, a, :]
+            nc.vector.tensor_copy(v[a][:], tab[a][:].bitcast(U32).indirect(idx[:]))
+
+        w1_codes = keep.tile([P, PASSES, H], U32, name="w1_codes", align_bytes=64)
+        w1_scales = keep.tile([P, PASSES, H], U8, name="w1_scales", align_bytes=64)
+        grouped = laid.tile([P, PASSES, H * PACK], BF16, name="grouped", offset=20 * KIB, align_bytes=64)
+
+        def cast(a, t0, t1, copy):
+            copy(
+                grouped[:, a, t0 * BANK : t1 * BANK].rearrange("p (t m j) -> p m j t", t=t1 - t0, j=PACK),
+                w1_raw[a][:].rearrange("p j (m t) -> p m j t", t=PACK)[:, :, :, t0:t1],
             )
-        pages.setdefault(1, keep.tile([P, T2], F32, name="page1", tag="tsc", align_bytes=64))
-        nc.vector.memset(pages[1][:].bitcast(I32), 0)
 
-        v0 = keep.tile([P, S], U32, name="v0", tag="v0", align_bytes=64)
-        nc.vector.tensor_copy(v0[:], tab[0][:].bitcast(U32).indirect(idx[:]))
-        v1 = {}
-
-        def gather_last_pass(e0, e1, tag):
-            piece = keep.tile([P, e1 - e0], U32, name="v1_%d" % e0, tag=tag, align_bytes=64)
-            nc.vector.tensor_copy(piece[:], tab[1][:].bitcast(U32).indirect(idx[:, e0 // 16 : e1 // 16]))
-            v1.setdefault(e0, piece)
-
-        def looked_up(a, e0, e1):
-            if a == 0:
-                return v0[:, e0:e1]
-            lo = max(start for start in v1 if start <= e0)
-            return v1[lo][:, e0 - lo : e1 - lo]
-
-        for e0, e1 in PIECES[:2]:
-            gather_last_pass(e0, e1, "v1_%d" % e0)
+        def quantise_w1(a, t0, t1):
+            nc.vector.quantize_mx(
+                out=w1_codes[:, a, t0 * P : t1 * P].bitcast(FP8X4),
+                scales=w1_scales[:, a, t0 * P : t1 * P],
+                in_=grouped[:, a, t0 * BANK : t1 * BANK],
+            )
 
         state_rows = state.rearrange("(p t) n -> p t n", t=PACK)
         st = [
             keep.tile([P, PACK, HALF], F32, name="st%d" % part, tag=tag, align_bytes=64)
-            for part, tag in enumerate(("w1_raw", "tab0"))
+            for part, tag in enumerate(("tab0", "tab1"))
         ]
         for part in range(2):
             nc.sync.dma_start(st[part][:], state_rows[:, :, part * HALF : (part + 1) * HALF])
@@ -180,65 +166,56 @@ def tile_list_neighbour_gap_message_kernel(
             at = a * PLANE + W4_AT + t * P
             return w4[:, a, 2 * t * P : 2 * (t + 1) * P].bitcast(FP4X4), planes[:, at : at + P]
 
-        def products(u, a):
+        def product(u, k, a):
             t, e0, e1 = units[u]
-            if u not in sums:
-                a_ps = psum.tile([P, BANK], F32, name="a_ps", tag="bank")
-                b_ps = psum.tile([P, BANK], F32, name="b_ps", tag="bank")
-                sums.setdefault(u, (a_ps, b_ps))
-            if u < DIRECT:
-                for k in (1, 0):
-                    codes, scales = weights(k, a, t)
-                    nc.tensor.matmul_mx(
-                        out=sums[u][k][:, : e1 - e0],
-                        lhsT=codes,
-                        lhsT_scale=scales,
-                        rhs=looked_up(a, e0, e1).bitcast(FP8X4),
-                        rhs_scale=planes[:, a * PLANE + e0 : a * PLANE + e1],
-                        start=(a == 0),
-                        stop=(a == PASSES - 1),
-                    )
-                return
-            blocks = (e1 - e0) // P
-            for k, acc in enumerate(sums[u]):
-                codes, scales = weights(k, a, t)
-                for b in range(blocks):
-                    e = e0 + b * P
-                    nc.tensor.matmul_mx(
-                        out=acc[:, b * P : (b + 1) * P],
-                        lhsT=looked_up(a, e, e + P).bitcast(FP8X4),
-                        lhsT_scale=planes[:, a * PLANE + e : a * PLANE + e + P],
-                        rhs=codes,
-                        rhs_scale=scales,
-                        start=(a == 0 and b == 0),
-                        stop=(a == PASSES - 1 and b == blocks - 1),
-                    )
-
-        def finish_products(u):
-            if u < len(units):
-                if u >= EARLY_UNITS:
-                    products(u, 0)
-                products(u, 1)
+            if (u, k) not in sums:
+                sums.setdefault((u, k), psum.tile([P, BANK], F32, name="sum%d" % k, tag="bank"))
+            looked_up = [
+                (v[a][:, lo:hi].bitcast(FP8X4), planes[:, a * PLANE + lo : a * PLANE + hi])
+                for lo, hi in ([(e0, e1)] if u < DIRECT else [(e, e + P) for e in range(e0, e1, P)])
+            ]
+            for b, edges in enumerate(looked_up):
+                still, moving = (weights(k, a, t), edges) if u < DIRECT else (edges, weights(k, a, t))
+                width = e1 - e0 if u < DIRECT else P
+                nc.tensor.matmul_mx(
+                    out=sums[u, k][:, b * width : (b + 1) * width],
+                    lhsT=still[0],
+                    lhsT_scale=still[1],
+                    rhs=moving[0],
+                    rhs_scale=moving[1],
+                    start=(a == 0 and b == 0),
+                    stop=(a == PASSES - 1 and b == len(looked_up) - 1),
+                )
 
         def term(u, k):
+            width = units[u][2] - units[u][1]
+            if (u, k) == (DIRECT, 0):
+                sb = keep.tile([P, width], F32, name="term_behind", tag="d_first0", align_bytes=64)
+            else:
+                sb = ring.tile([P, BANK], F32, name="term%d" % k, tag="term%d" % k, bufs=TERM_BUFS[k], align_bytes=64)
+            if k == 0:
+                nc.scalar.activation(sb[:, :width], sums[u, 0][:, :width], ACT.Relu)
+            else:
+                nc.scalar.activation(sb[:, :width], sums[u, 1][:, :width], ACT.Copy, scale=-1.0)
+            terms.setdefault((u, k), sb)
+
+        def linear_view(u):
             if u < len(units):
-                width = units[u][2] - units[u][1]
-                if k == 0 and u == DIRECT:
-                    sb = laid.tile([P, width], F32, name="behind", offset=16 * KIB, align_bytes=64)
-                else:
-                    sb = ring.tile([P, BANK], F32, name="term%d" % k, tag="term%d" % k, bufs=3, align_bytes=64)
-                if k == 0:
-                    nc.scalar.activation(sb[:, :width], sums[u][0][:, :width], ACT.Relu)
-                else:
-                    nc.scalar.activation(sb[:, :width], sums[u][1][:, :width], ACT.Copy, scale=-1.0)
-                terms.setdefault(u, []).append(sb)
+                for a in range(PASSES):
+                    product(u, 1, a)
+                term(u, 1)
+
+        def rectified_view(u):
+            if u < len(units):
+                for a in range(0 if u >= EARLY_UNITS else 1, PASSES):
+                    product(u, 0, a)
 
         def gaps(u):
             t, e0, e1 = units[u]
             width = e1 - e0
             blocks = width // P
             d_ps = psum.tile([P, BANK], F32, name="d_ps", tag="bank")
-            for k, sb in enumerate(terms[u]):
+            for k, sb in enumerate((terms[u, 1], terms[u, 0])):
                 for b in range(blocks):
                     nc.tensor.matmul(
                         d_ps[:, b * P : (b + 1) * P],
@@ -250,32 +227,38 @@ def tile_list_neighbour_gap_message_kernel(
                     )
             nc.scalar.activation(h[t][:, e0:e1], d_ps[:, :width], ACT.Abs)
 
+        for u in range(AHEAD):
+            linear_view(u)
+        cast(0, 0, PACK, nc.vector.tensor_copy)
+        quantise_w1(0, 0, PACK)
         for u in range(EARLY_UNITS):
-            products(u, 0)
+            product(u, 0, 0)
+        cast(1, 0, 2, nc.vector.tensor_copy)
+        cast(1, 2, PACK, nc.scalar.copy)
         for u in range(DIRECT):
-            finish_products(u)
-            b_first = keep.tile([P, FIRST], F32, name="b_first%d" % u, tag="b_first%d" % u, align_bytes=64)
-            d_first = laid.tile([P, FIRST], F32, name="d_first%d" % u, offset=(17 + u) * KIB, align_bytes=64)
-            nc.scalar.copy(b_first[:], sums[u][1][:, :FIRST])
-            nc.vector.scalar_tensor_tensor(d_first[:], sums[u][0][:, :FIRST], 0.0, b_first[:], ALU.max, ALU.subtract)
+            quantise_w1(1, u, u + 1)
+        for u in range(DIRECT):
+            rectified_view(u)
+            d_first = keep.tile([P, FIRST], F32, name="d_first%d" % u, tag="d_first%d" % u, align_bytes=64)
+            nc.vector.scalar_tensor_tensor(d_first[:], sums[u, 0][:, :FIRST], 0.0, terms[u, 1][:, :FIRST], ALU.max, ALU.add)
             nc.scalar.activation(h[u][:, :FIRST], d_first[:], ACT.Abs)
-        gather_last_pass(*PIECES[2], "b_first%d" % (DIRECT - 1))
+        quantise_w1(1, 2, PACK)
         for t in (2, 3):
-            pages.setdefault(t, laid.tile([P, T2], F32, name="page%d" % t, offset=(t - 2) * 8 * KIB, align_bytes=64))
+            pages.setdefault(t, laid.tile([P, T2], F32, name="page%d" % t, offset=t * 8 * KIB, align_bytes=64))
             nc.gpsimd.memset(pages[t][:].bitcast(I32), 0)
-        finish_products(DIRECT)
+        rectified_view(DIRECT)
         term(DIRECT, 0)
-        term(DIRECT, 1)
-        finish_products(DIRECT + 1)
+        rectified_view(DIRECT + 1)
         for u in range(DIRECT, len(units)):
-            term(u + 1, 0)
+            if u + 1 < len(units):
+                term(u + 1, 0)
             gaps(u)
-            term(u + 1, 1)
-            finish_products(u + 2)
+            rectified_view(u + 2)
+            linear_view(u + AHEAD - DIRECT)
 
         stack = [
             keep.tile([P, PACK, HALF], F32, name="stack%d" % part, tag=tag, align_bytes=64)
-            for part, tag in enumerate(("v0", "w1_codes"))
+            for part, tag in enumerate(("v0", "v1"))
         ]
         for t, e0, e1 in SCATTERS:
             nc.vector.tensor_tensor(
@@ -292,7 +275,7 @@ def tile_list_neighbour_gap_message_kernel(
         def maximum(c):
             n0, width = starts[c], NODE_CHUNKS[c]
             part, at = divmod(n0, HALF)
-            woven = ring.tile([P, PACK * BANK], BF16, name="woven", bufs=3, align_bytes=64)
+            woven = ring.tile([P, PACK * max(NODE_CHUNKS)], BF16, name="woven", bufs=3, align_bytes=64)
             nc.vector.tensor_tensor(
                 woven[:, : PACK * width].rearrange("p (c i t) -> p c t i", i=PAIR, t=PACK),
                 stack[part][:, :, at : at + width].rearrange("p t (c i) -> p c t i", i=PAIR),
@@ -303,8 +286,8 @@ def tile_list_neighbour_gap_message_kernel(
 
         def quantise(c, woven):
             width = NODE_CHUNKS[c]
-            z_codes = ring.tile([P, BANK], U32, name="z_codes", align_bytes=64)
-            z_scales = ring.tile([P, BANK], U8, name="z_scales", align_bytes=64)
+            z_codes = ring.tile([P, max(NODE_CHUNKS)], U32, name="z_codes", align_bytes=64)
+            z_scales = ring.tile([P, max(NODE_CHUNKS)], U8, name="z_scales", align_bytes=64)
             nc.vector.quantize_mx(
                 out=z_codes[:, :width].bitcast(FP8X4), scales=z_scales[:, :width], in_=woven[:, : PACK * width]
             )

@@ -76,7 +76,6 @@ def tile_list_neighbour_gap_message_kernel(
         nc.sync.dma_start(idx[:], offs)
         nc.sync.dma_start(tsc[0:live, :].bitcast(I32), tab_scales.rearrange("a q t -> (a q) t").bitcast(I32))
         nc.sync.dma_start(w4s_raw[0:live, :].bitcast(I32), w4_scales.rearrange("a q c -> (a q) c").bitcast(I32))
-        nc.sync.dma_start(idx2[:], offs2)
         nc.sync.dma_start(w4_raw[:].bitcast(I32), w4_words.rearrange("a p b -> p a b").bitcast(I32))
         for a in range(PASSES):
             nc.sync.dma_start(tab[a][:], tab_words[a].rearrange("p t i -> p (t i)").bitcast(I32))
@@ -96,13 +95,14 @@ def tile_list_neighbour_gap_message_kernel(
                 planes[src : src + 4, 0:PLANE].bitcast(I32),
             )
 
-        groups = [(a, q) for a in range(PASSES) for q in range(P // QUAD)]
+        groups = [(a, q) for a in range(PASSES) for q in QUAD_ORDER]
         for a, q in groups[1:-1]:
             carry(a, q, nc.sync)
         w1_rows = w1.rearrange("(a p j) c -> a p j c", a=PASSES, j=PACK)
         nc.sync.dma_start(w1_raw[0][:], w1_rows[0])
         carry(*groups[-1], nc.sync)
         nc.sync.dma_start(w1_raw[1][:], w1_rows[1])
+        nc.sync.dma_start(idx2[:], offs2)
         w4 = keep.tile([P, PASSES, 2 * H], U8, name="w4", align_bytes=64)
         nc.vector.tensor_copy(
             w4[:].bitcast(U16).rearrange("p a (t m) -> p a t m", t=PACK),
@@ -229,8 +229,10 @@ def tile_list_neighbour_gap_message_kernel(
 
         for u in range(AHEAD):
             linear_view(u)
-        cast(0, 0, PACK, nc.vector.tensor_copy)
-        quantise_w1(0, 0, PACK)
+        cast(0, 0, 2, nc.vector.tensor_copy)
+        cast(0, 2, PACK, nc.scalar.copy)
+        quantise_w1(0, 0, 2)
+        quantise_w1(0, 2, PACK)
         for u in range(EARLY_UNITS):
             product(u, 0, 0)
         cast(1, 0, 2, nc.vector.tensor_copy)

@@ -39,6 +39,7 @@ PAIR = 2
 EARLY_UNITS = 4
 QUAD_ORDER = (0, 2, 1, 3)
 DIRECT = 2
+LEAD = 96
 AHEAD = 5
 TERM_BUFS = (3, AHEAD)
 WG_LOADS = tuple((t, t + 1, e0, e1) for e0, e1 in ((0, FIRST),) for t in (0, 1)) + ((0, 2, FIRST, 2 * FIRST), (0, 2, 2 * FIRST, S), (2, 4, 0, S))
@@ -274,17 +275,18 @@ def tile_list_neighbour_gap_message_kernel(
 
         starts = [sum(NODE_CHUNKS[:c]) for c in range(len(NODE_CHUNKS))]
 
-        def maximum(c):
-            n0, width = starts[c], NODE_CHUNKS[c]
-            part, at = divmod(n0, HALF)
-            woven = ring.tile([P, PACK * max(NODE_CHUNKS)], BF16, name="woven", bufs=3, align_bytes=64)
+        wovens = {}
+
+        def maximum(c, lo, hi):
+            part, at = divmod(starts[c], HALF)
+            if c not in wovens:
+                wovens.setdefault(c, ring.tile([P, PACK * max(NODE_CHUNKS)], BF16, name="woven", bufs=3, align_bytes=64))
             nc.vector.tensor_tensor(
-                woven[:, : PACK * width].rearrange("p (c i t) -> p c t i", i=PAIR, t=PACK),
-                stack[part][:, :, at : at + width].rearrange("p t (c i) -> p c t i", i=PAIR),
-                st[part][:, :, at : at + width].rearrange("p t (c i) -> p c t i", i=PAIR),
+                wovens[c][:, PACK * lo : PACK * hi].rearrange("p (c i t) -> p c t i", i=PAIR, t=PACK),
+                stack[part][:, :, at + lo : at + hi].rearrange("p t (c i) -> p c t i", i=PAIR),
+                st[part][:, :, at + lo : at + hi].rearrange("p t (c i) -> p c t i", i=PAIR),
                 ALU.max,
             )
-            return woven
 
         def quantise(c, woven):
             width = NODE_CHUNKS[c]
@@ -322,10 +324,9 @@ def tile_list_neighbour_gap_message_kernel(
                     o_sb[:, :used].rearrange("p (k n) -> p k n", k=per_bank),
                 )
 
-        ahead = maximum(0)
-        for c in range(len(NODE_CHUNKS)):
-            woven = ahead
+        for c, width in enumerate(NODE_CHUNKS):
+            maximum(c, LEAD if c > 0 else 0, width)
             if c + 1 < len(NODE_CHUNKS):
-                ahead = maximum(c + 1)
-            z_codes, z_scales = quantise(c, woven)
+                maximum(c + 1, 0, LEAD)
+            z_codes, z_scales = quantise(c, wovens[c])
             messages(c, z_codes, z_scales)

@@ -36,12 +36,14 @@ LAST_COPIES = ((0, 128), (128, 256), (256, 512), (512, 1024), (1024, 2048))
 KIB = 1024
 HALF = T2 // 2
 PAIR = 2
-EARLY_UNITS = 4
+BANKS = 8
+EARLY_UNITS = (4, 2)
 QUAD_ORDER = (0, 2, 1, 3)
 DIRECT = 2
 LEAD = 96
-AHEAD = 5
-TERM_BUFS = (3, AHEAD)
+HELD = 4
+LATE_UNIT = 6
+TERM_BUFS = (3, 3)
 WG_LOADS = tuple((t, t + 1, e0, e1) for e0, e1 in ((0, FIRST),) for t in (0, 1)) + ((0, 2, FIRST, 2 * FIRST), (0, 2, 2 * FIRST, S), (2, 4, 0, S))
 
 
@@ -54,7 +56,7 @@ def tile_list_neighbour_gap_message_kernel(
         laid = ctx.enter_context(tc.tile_pool(name="laid", bufs=1))
         ring = ctx.enter_context(tc.tile_pool(name="ring", bufs=2))
         outs = ctx.enter_context(tc.tile_pool(name="outs", bufs=12))
-        psum = ctx.enter_context(tc.psum_pool(name="psum", bufs=8))
+        psum = ctx.enter_context(tc.psum_pool(name="psum", bufs=1))
 
         idx = keep.tile([P, S // 16], U16, name="idx")
         idx2 = keep.tile([P, S // 16], U16, name="idx2")
@@ -62,7 +64,7 @@ def tile_list_neighbour_gap_message_kernel(
         w4s_raw = keep.tile([P, H], U8, name="w4s_raw", align_bytes=64)
         planes = keep.tile([P, PASSES * PLANE], U8, name="planes", align_bytes=64)
         tab = [keep.tile([P, T], I32, name="tab%d" % a, tag="tab%d" % a, align_bytes=64) for a in range(PASSES)]
-        w4_raw = keep.tile([P, PASSES, 2 * H], U8, name="w4_raw", align_bytes=64)
+        w4_raw = [keep.tile([P, 2 * H], U8, name="w4_raw%d" % a, align_bytes=64) for a in range(PASSES)]
         w1_raw = [keep.tile([P, PACK, H], F32, name="w1_raw%d" % a, align_bytes=64) for a in range(PASSES)]
         ident = keep.tile([P, P], F32, name="ident", align_bytes=64)
 
@@ -77,7 +79,7 @@ def tile_list_neighbour_gap_message_kernel(
         nc.sync.dma_start(idx[:], offs)
         nc.sync.dma_start(tsc[0:live, :].bitcast(I32), tab_scales.rearrange("a q t -> (a q) t").bitcast(I32))
         nc.sync.dma_start(w4s_raw[0:live, :].bitcast(I32), w4_scales.rearrange("a q c -> (a q) c").bitcast(I32))
-        nc.sync.dma_start(w4_raw[:].bitcast(I32), w4_words.rearrange("a p b -> p a b").bitcast(I32))
+        nc.sync.dma_start(w4_raw[0][:].bitcast(I32), w4_words[0].bitcast(I32))
         for a in range(PASSES):
             nc.sync.dma_start(tab[a][:], tab_words[a].rearrange("p t i -> p (t i)").bitcast(I32))
 
@@ -103,12 +105,17 @@ def tile_list_neighbour_gap_message_kernel(
         nc.sync.dma_start(w1_raw[0][:], w1_rows[0])
         carry(*groups[-1], nc.sync)
         nc.sync.dma_start(w1_raw[1][:], w1_rows[1])
+        nc.sync.dma_start(w4_raw[1][:].bitcast(I32), w4_words[1].bitcast(I32))
         nc.sync.dma_start(idx2[:], offs2)
-        w4 = keep.tile([P, PASSES, 2 * H], U8, name="w4", align_bytes=64)
-        nc.vector.tensor_copy(
-            w4[:].bitcast(U16).rearrange("p a (t m) -> p a t m", t=PACK),
-            w4_raw[:].bitcast(U16).rearrange("p a (m t) -> p a t m", t=PACK),
-        )
+        w4 = [keep.tile([P, 2 * H], U8, name="w4_%d" % a, align_bytes=64) for a in range(PASSES)]
+
+        def order_w4(a, t0, t1, copy):
+            copy(
+                w4[a][:, 2 * t0 * P : 2 * t1 * P].bitcast(U16).rearrange("p (t m) -> p t m", m=P),
+                w4_raw[a][:].bitcast(U16).rearrange("p (m t) -> p t m", t=PACK)[:, t0:t1, :],
+            )
+
+        order_w4(0, 0, PACK, nc.vector.tensor_copy)
 
         wgs_rows = wgs.rearrange("(q t) j -> q t j", t=PACK)
         wg = keep.tile([P, PACK, S], F32, name="wg", align_bytes=64)
@@ -135,17 +142,25 @@ def tile_list_neighbour_gap_message_kernel(
         w1_scales = keep.tile([P, PASSES, H], U8, name="w1_scales", align_bytes=64)
         grouped = laid.tile([P, PASSES, H * PACK], BF16, name="grouped", offset=20 * KIB, align_bytes=64)
 
+        def rounded(a, t0, t1):
+            return late["grouped"][:] if (a, t0) == (1, 2) else grouped[:, a, t0 * BANK : t1 * BANK]
+
+        def codes(a, t0, t1):
+            return late["codes"][:, (t0 - 2) * P : (t1 - 2) * P] if a == 1 and t0 >= 2 else w1_codes[:, a, t0 * P : t1 * P]
+
+        late = {}
+
         def cast(a, t0, t1, copy):
             copy(
-                grouped[:, a, t0 * BANK : t1 * BANK].rearrange("p (t m j) -> p m j t", t=t1 - t0, j=PACK),
+                rounded(a, t0, t1).rearrange("p (t m j) -> p m j t", t=t1 - t0, j=PACK),
                 w1_raw[a][:].rearrange("p j (m t) -> p m j t", t=PACK)[:, :, :, t0:t1],
             )
 
         def quantise_w1(a, t0, t1):
             nc.vector.quantize_mx(
-                out=w1_codes[:, a, t0 * P : t1 * P].bitcast(FP8X4),
+                out=codes(a, t0, t1).bitcast(FP8X4),
                 scales=w1_scales[:, a, t0 * P : t1 * P],
-                in_=grouped[:, a, t0 * BANK : t1 * BANK],
+                in_=rounded(a, t0, t1),
             )
 
         state_rows = state.rearrange("(p t) n -> p t n", t=PACK)
@@ -158,19 +173,30 @@ def tile_list_neighbour_gap_message_kernel(
 
         h = [keep.tile([P, S], F32, name="h%d" % t, align_bytes=64) for t in range(PACK)]
         units = [(t, lo, min(lo + BANK, e1)) for t, e0, e1 in SCATTERS for lo in range(e0, e1, BANK)]
+        h_held = keep.tile([P, FIRST], F32, name="h_held", tag="late_codes", align_bytes=64)
+
+        def gap(t, e0, e1):
+            return h_held[:] if (t, e0, e1) == SCATTERS[HELD - 1] else h[t][:, e0:e1]
+
         sums = {}
         terms = {}
 
+        def bank(b, name):
+            return psum.tile([P, BANK], F32, name=name, tag="bank%d" % b)
+
+        def sum_bank(u, k):
+            return u % EARLY_UNITS[0] if k == 0 else EARLY_UNITS[0] + u % EARLY_UNITS[1]
+
         def weights(k, a, t):
             if k == 0:
-                return w1_codes[:, a, t * P : (t + 1) * P].bitcast(FP8X4), w1_scales[:, a, t * P : (t + 1) * P]
+                return codes(a, t, t + 1).bitcast(FP8X4), w1_scales[:, a, t * P : (t + 1) * P]
             at = a * PLANE + W4_AT + t * P
-            return w4[:, a, 2 * t * P : 2 * (t + 1) * P].bitcast(FP4X4), planes[:, at : at + P]
+            return w4[a][:, 2 * t * P : 2 * (t + 1) * P].bitcast(FP4X4), planes[:, at : at + P]
 
         def product(u, k, a):
             t, e0, e1 = units[u]
             if (u, k) not in sums:
-                sums.setdefault((u, k), psum.tile([P, BANK], F32, name="sum%d" % k, tag="bank"))
+                sums.setdefault((u, k), bank(sum_bank(u, k), "sum%d" % k))
             looked_up = [
                 (v[a][:, lo:hi].bitcast(FP8X4), planes[:, a * PLANE + lo : a * PLANE + hi])
                 for lo, hi in ([(e0, e1)] if u < DIRECT else [(e, e + P) for e in range(e0, e1, P)])
@@ -190,8 +216,10 @@ def tile_list_neighbour_gap_message_kernel(
 
         def term(u, k):
             width = units[u][2] - units[u][1]
-            if (u, k) == (DIRECT, 0):
-                sb = keep.tile([P, width], F32, name="term_behind", tag="d_first0", align_bytes=64)
+            if u == DIRECT:
+                sb = keep.tile([P, width], F32, name="term_behind", tag="d_first%d" % k, align_bytes=64)
+            elif (u, k) == (DIRECT + 1, 0):
+                sb = keep.tile([P, width], F32, name="term_ahead", tag="late_cast", align_bytes=64)
             else:
                 sb = ring.tile([P, BANK], F32, name="term%d" % k, tag="term%d" % k, bufs=TERM_BUFS[k], align_bytes=64)
             if k == 0:
@@ -201,21 +229,19 @@ def tile_list_neighbour_gap_message_kernel(
             terms.setdefault((u, k), sb)
 
         def linear_view(u):
-            if u < len(units):
-                for a in range(PASSES):
-                    product(u, 1, a)
-                term(u, 1)
+            for a in range(0 if u >= EARLY_UNITS[1] else 1, PASSES):
+                product(u, 1, a)
+            term(u, 1)
 
         def rectified_view(u):
-            if u < len(units):
-                for a in range(0 if u >= EARLY_UNITS else 1, PASSES):
-                    product(u, 0, a)
+            for a in range(0 if u >= EARLY_UNITS[0] else 1, PASSES):
+                product(u, 0, a)
 
         def gaps(u):
             t, e0, e1 = units[u]
             width = e1 - e0
             blocks = width // P
-            d_ps = psum.tile([P, BANK], F32, name="d_ps", tag="bank")
+            d_ps = bank(sum(EARLY_UNITS) + u % 2, "d_ps")
             for k, sb in enumerate((terms[u, 1], terms[u, 0])):
                 for b in range(blocks):
                     nc.tensor.matmul(
@@ -226,47 +252,56 @@ def tile_list_neighbour_gap_message_kernel(
                         start=(k == 0 and b == 0),
                         stop=(k == 1 and b == blocks - 1),
                     )
-            nc.scalar.activation(h[t][:, e0:e1], d_ps[:, :width], ACT.Abs)
+            nc.scalar.activation(gap(t, e0, e1), d_ps[:, :width], ACT.Abs)
 
-        for u in range(AHEAD):
-            linear_view(u)
         cast(0, 0, 2, nc.vector.tensor_copy)
         cast(0, 2, PACK, nc.scalar.copy)
         quantise_w1(0, 0, 2)
         quantise_w1(0, 2, PACK)
-        for u in range(EARLY_UNITS):
-            product(u, 0, 0)
+        for k in (1, 0):
+            for u in range(EARLY_UNITS[k]):
+                product(u, k, 0)
         cast(1, 0, 2, nc.vector.tensor_copy)
-        cast(1, 2, PACK, nc.scalar.copy)
+        order_w4(1, 0, 2, nc.scalar.copy)
+        for t in range(2):
+            quantise_w1(1, t, t + 1)
         for u in range(DIRECT):
-            quantise_w1(1, u, u + 1)
-        for u in range(DIRECT):
+            linear_view(u)
             rectified_view(u)
+        for u in range(DIRECT):
             d_first = keep.tile([P, FIRST], F32, name="d_first%d" % u, tag="d_first%d" % u, align_bytes=64)
             nc.vector.scalar_tensor_tensor(d_first[:], sums[u, 0][:, :FIRST], 0.0, terms[u, 1][:, :FIRST], ALU.max, ALU.add)
             nc.scalar.activation(h[u][:, :FIRST], d_first[:], ACT.Abs)
-        quantise_w1(1, 2, PACK)
         for t in (2, 3):
             pages.setdefault(t, laid.tile([P, T2], F32, name="page%d" % t, offset=t * 8 * KIB, align_bytes=64))
             nc.gpsimd.memset(pages[t][:].bitcast(I32), 0)
-        rectified_view(DIRECT)
-        term(DIRECT, 0)
-        rectified_view(DIRECT + 1)
+        def scatter(t, e0, e1):
+            nc.vector.tensor_tensor(
+                pages[t][:].indirect(idx2[:, e0 // 16 : e1 // 16]), gap(t, e0, e1), wg[:, t, e0:e1], ALU.mult
+            )
+
         for u in range(DIRECT, len(units)):
-            if u + 1 < len(units):
-                term(u + 1, 0)
-            gaps(u)
-            rectified_view(u + 2)
-            linear_view(u + AHEAD - DIRECT)
+            if u == LATE_UNIT:
+                for piece in SCATTERS[:HELD]:
+                    scatter(*piece)
+                late.setdefault("grouped", keep.tile([P, 2 * BANK], BF16, name="late_grouped", tag="late_cast", align_bytes=64))
+                late.setdefault("codes", keep.tile([P, 2 * P], U32, name="late_codes", tag="late_codes", align_bytes=64))
+                cast(1, 2, PACK, nc.scalar.copy)
+                quantise_w1(1, 2, PACK)
+                order_w4(1, 2, PACK, nc.scalar.copy)
+            rectified_view(u)
+            term(u, 0)
+            linear_view(u)
+            if u > DIRECT:
+                gaps(u - 1)
+        gaps(len(units) - 1)
 
         stack = [
             keep.tile([P, PACK, HALF], F32, name="stack%d" % part, tag=tag, align_bytes=64)
             for part, tag in enumerate(("v0", "v1"))
         ]
-        for t, e0, e1 in SCATTERS:
-            nc.vector.tensor_tensor(
-                pages[t][:].indirect(idx2[:, e0 // 16 : e1 // 16]), h[t][:, e0:e1], wg[:, t, e0:e1], ALU.mult
-            )
+        for t, e0, e1 in SCATTERS[HELD:]:
+            scatter(t, e0, e1)
             if e1 == S:
                 move = nc.sync.dma_start if t == PACK - 2 else nc.scalar.copy
                 for lo, hi in ((0, HALF), (HALF, T2)) if t < PACK - 1 else LAST_COPIES:
@@ -276,6 +311,7 @@ def tile_list_neighbour_gap_message_kernel(
         starts = [sum(NODE_CHUNKS[:c]) for c in range(len(NODE_CHUNKS))]
 
         wovens = {}
+        stored = []
 
         def maximum(c, lo, hi):
             part, at = divmod(starts[c], HALF)
@@ -301,7 +337,8 @@ def tile_list_neighbour_gap_message_kernel(
             n0, width = starts[c], NODE_CHUNKS[c]
             per_bank = 2 if c == len(NODE_CHUNKS) - 1 else BANK // width
             for b0 in range(0, N // P, per_bank):
-                o_ps = psum.tile([P, BANK], F32, name="o_ps", tag="bank")
+                o_ps = bank(len(stored) % BANKS, "o_ps")
+                stored.append((c, b0))
                 for k in range(per_bank):
                     b = b0 + k
                     nc.tensor.matmul_mx(

@@ -37,13 +37,11 @@ KIB = 1024
 HALF = T2 // 2
 PAIR = 2
 BANKS = 8
-EARLY_UNITS = (4, 2)
+EARLY_UNITS = ((0, 1, 2, 3), (0, 1, 4, 5))
 QUAD_ORDER = (0, 2, 1, 3)
 DIRECT = 2
 LEAD = 96
-HELD = 4
-LATE_UNIT = 6
-TERM_BUFS = (3, 3)
+TERM_BUFS = (3, 2)
 WG_LOADS = tuple((t, t + 1, e0, e1) for e0, e1 in ((0, FIRST),) for t in (0, 1)) + ((0, 2, FIRST, 2 * FIRST), (0, 2, 2 * FIRST, S), (2, 4, 0, S))
 
 
@@ -79,9 +77,9 @@ def tile_list_neighbour_gap_message_kernel(
         nc.sync.dma_start(idx[:], offs)
         nc.sync.dma_start(tsc[0:live, :].bitcast(I32), tab_scales.rearrange("a q t -> (a q) t").bitcast(I32))
         nc.sync.dma_start(w4s_raw[0:live, :].bitcast(I32), w4_scales.rearrange("a q c -> (a q) c").bitcast(I32))
-        nc.sync.dma_start(w4_raw[0][:].bitcast(I32), w4_words[0].bitcast(I32))
         for a in range(PASSES):
             nc.sync.dma_start(tab[a][:], tab_words[a].rearrange("p t i -> p (t i)").bitcast(I32))
+        nc.sync.dma_start(w4_raw[0][:].bitcast(I32), w4_words[0].bitcast(I32))
 
         gsc = keep.tile([P, S], U8, name="gsc", align_bytes=64)
         nc.vector.tensor_copy(
@@ -99,23 +97,27 @@ def tile_list_neighbour_gap_message_kernel(
             )
 
         groups = [(a, q) for a in range(PASSES) for q in QUAD_ORDER]
-        for a, q in groups[1:-1]:
+        for a, q in groups[1:PACK]:
             carry(a, q, nc.sync)
-        w1_rows = w1.rearrange("(a p j) c -> a p j c", a=PASSES, j=PACK)
-        nc.sync.dma_start(w1_raw[0][:], w1_rows[0])
-        carry(*groups[-1], nc.sync)
-        nc.sync.dma_start(w1_raw[1][:], w1_rows[1])
-        nc.sync.dma_start(w4_raw[1][:].bitcast(I32), w4_words[1].bitcast(I32))
         nc.sync.dma_start(idx2[:], offs2)
-        w4 = [keep.tile([P, 2 * H], U8, name="w4_%d" % a, align_bytes=64) for a in range(PASSES)]
+        w1_rows = w1.rearrange("(a p j) c -> a p j c", a=PASSES, j=PACK)
+        for a in range(PASSES):
+            nc.sync.dma_start(w1_raw[a][:], w1_rows[a])
+        nc.sync.dma_start(w4_raw[1][:].bitcast(I32), w4_words[1].bitcast(I32))
+        for a, q in groups[PACK:]:
+            carry(a, q, nc.sync)
+        w4 = {}
 
-        def order_w4(a, t0, t1, copy):
+        def order_w4(a, t0, t1, copy, tag):
+            words = keep.tile([P, 2 * (t1 - t0) * P], U8, name="w4_%d%d" % (a, t0), tag=tag, align_bytes=64)
+            for t in range(t0, t1):
+                w4.setdefault((a, t), words[:, 2 * (t - t0) * P : 2 * (t - t0 + 1) * P])
             copy(
-                w4[a][:, 2 * t0 * P : 2 * t1 * P].bitcast(U16).rearrange("p (t m) -> p t m", m=P),
+                words[:].bitcast(U16).rearrange("p (t m) -> p t m", m=P),
                 w4_raw[a][:].bitcast(U16).rearrange("p (m t) -> p t m", t=PACK)[:, t0:t1, :],
             )
 
-        order_w4(0, 0, PACK, nc.vector.tensor_copy)
+        order_w4(0, 0, PACK, nc.vector.tensor_copy, "w4_first")
 
         wgs_rows = wgs.rearrange("(q t) j -> q t j", t=PACK)
         wg = keep.tile([P, PACK, S], F32, name="wg", align_bytes=64)
@@ -142,25 +144,17 @@ def tile_list_neighbour_gap_message_kernel(
         w1_scales = keep.tile([P, PASSES, H], U8, name="w1_scales", align_bytes=64)
         grouped = laid.tile([P, PASSES, H * PACK], BF16, name="grouped", offset=20 * KIB, align_bytes=64)
 
-        def rounded(a, t0, t1):
-            return late["grouped"][:] if (a, t0) == (1, 2) else grouped[:, a, t0 * BANK : t1 * BANK]
-
-        def codes(a, t0, t1):
-            return late["codes"][:, (t0 - 2) * P : (t1 - 2) * P] if a == 1 and t0 >= 2 else w1_codes[:, a, t0 * P : t1 * P]
-
-        late = {}
-
-        def cast(a, t0, t1, copy):
+        def cast(a, t0, t1, copy, m0=0, m1=P):
             copy(
-                rounded(a, t0, t1).rearrange("p (t m j) -> p m j t", t=t1 - t0, j=PACK),
-                w1_raw[a][:].rearrange("p j (m t) -> p m j t", t=PACK)[:, :, :, t0:t1],
+                grouped[:, a, t0 * BANK : t1 * BANK].rearrange("p (t m j) -> p m j t", t=t1 - t0, j=PACK)[:, m0:m1],
+                w1_raw[a][:].rearrange("p j (m t) -> p m j t", t=PACK)[:, m0:m1, :, t0:t1],
             )
 
         def quantise_w1(a, t0, t1):
             nc.vector.quantize_mx(
-                out=codes(a, t0, t1).bitcast(FP8X4),
+                out=w1_codes[:, a, t0 * P : t1 * P].bitcast(FP8X4),
                 scales=w1_scales[:, a, t0 * P : t1 * P],
-                in_=rounded(a, t0, t1),
+                in_=grouped[:, a, t0 * BANK : t1 * BANK],
             )
 
         state_rows = state.rearrange("(p t) n -> p t n", t=PACK)
@@ -173,11 +167,6 @@ def tile_list_neighbour_gap_message_kernel(
 
         h = [keep.tile([P, S], F32, name="h%d" % t, align_bytes=64) for t in range(PACK)]
         units = [(t, lo, min(lo + BANK, e1)) for t, e0, e1 in SCATTERS for lo in range(e0, e1, BANK)]
-        h_held = keep.tile([P, FIRST], F32, name="h_held", tag="late_codes", align_bytes=64)
-
-        def gap(t, e0, e1):
-            return h_held[:] if (t, e0, e1) == SCATTERS[HELD - 1] else h[t][:, e0:e1]
-
         sums = {}
         terms = {}
 
@@ -185,13 +174,13 @@ def tile_list_neighbour_gap_message_kernel(
             return psum.tile([P, BANK], F32, name=name, tag="bank%d" % b)
 
         def sum_bank(u, k):
-            return u % EARLY_UNITS[0] if k == 0 else EARLY_UNITS[0] + u % EARLY_UNITS[1]
+            return u % 4 if k == 0 else 4 + u % 2 + 2 * ((max(u // 2, 1) + 1) % 2)
 
         def weights(k, a, t):
             if k == 0:
-                return codes(a, t, t + 1).bitcast(FP8X4), w1_scales[:, a, t * P : (t + 1) * P]
+                return w1_codes[:, a, t * P : (t + 1) * P].bitcast(FP8X4), w1_scales[:, a, t * P : (t + 1) * P]
             at = a * PLANE + W4_AT + t * P
-            return w4[a][:, 2 * t * P : 2 * (t + 1) * P].bitcast(FP4X4), planes[:, at : at + P]
+            return w4[a, t].bitcast(FP4X4), planes[:, at : at + P]
 
         def product(u, k, a):
             t, e0, e1 = units[u]
@@ -219,7 +208,7 @@ def tile_list_neighbour_gap_message_kernel(
             if u == DIRECT:
                 sb = keep.tile([P, width], F32, name="term_behind", tag="d_first%d" % k, align_bytes=64)
             elif (u, k) == (DIRECT + 1, 0):
-                sb = keep.tile([P, width], F32, name="term_ahead", tag="late_cast", align_bytes=64)
+                sb = keep.tile([P, width], F32, name="term_ahead", tag="w4_late", align_bytes=64)
             else:
                 sb = ring.tile([P, BANK], F32, name="term%d" % k, tag="term%d" % k, bufs=TERM_BUFS[k], align_bytes=64)
             if k == 0:
@@ -229,19 +218,19 @@ def tile_list_neighbour_gap_message_kernel(
             terms.setdefault((u, k), sb)
 
         def linear_view(u):
-            for a in range(0 if u >= EARLY_UNITS[1] else 1, PASSES):
+            for a in range(1 if u in EARLY_UNITS[1] else 0, PASSES):
                 product(u, 1, a)
             term(u, 1)
 
         def rectified_view(u):
-            for a in range(0 if u >= EARLY_UNITS[0] else 1, PASSES):
+            for a in range(1 if u in EARLY_UNITS[0] else 0, PASSES):
                 product(u, 0, a)
 
         def gaps(u):
             t, e0, e1 = units[u]
             width = e1 - e0
             blocks = width // P
-            d_ps = bank(sum(EARLY_UNITS) + u % 2, "d_ps")
+            d_ps = bank(sum_bank(u, 0), "d_ps")
             for k, sb in enumerate((terms[u, 1], terms[u, 0])):
                 for b in range(blocks):
                     nc.tensor.matmul(
@@ -252,56 +241,50 @@ def tile_list_neighbour_gap_message_kernel(
                         start=(k == 0 and b == 0),
                         stop=(k == 1 and b == blocks - 1),
                     )
-            nc.scalar.activation(gap(t, e0, e1), d_ps[:, :width], ACT.Abs)
+            nc.scalar.activation(h[t][:, e0:e1], d_ps[:, :width], ACT.Abs)
 
         cast(0, 0, 2, nc.vector.tensor_copy)
         cast(0, 2, PACK, nc.scalar.copy)
         quantise_w1(0, 0, 2)
         quantise_w1(0, 2, PACK)
         for k in (1, 0):
-            for u in range(EARLY_UNITS[k]):
+            for u in EARLY_UNITS[k]:
                 product(u, k, 0)
         cast(1, 0, 2, nc.vector.tensor_copy)
-        order_w4(1, 0, 2, nc.scalar.copy)
+        order_w4(1, 0, 2, nc.scalar.copy, "w4_second")
+        for m0 in (0, P // 2):
+            cast(1, 2, PACK, nc.scalar.copy, m0, m0 + P // 2)
         for t in range(2):
             quantise_w1(1, t, t + 1)
-        for u in range(DIRECT):
-            linear_view(u)
-            rectified_view(u)
+        for view in (linear_view, rectified_view):
+            for u in range(DIRECT):
+                view(u)
         for u in range(DIRECT):
             d_first = keep.tile([P, FIRST], F32, name="d_first%d" % u, tag="d_first%d" % u, align_bytes=64)
             nc.vector.scalar_tensor_tensor(d_first[:], sums[u, 0][:, :FIRST], 0.0, terms[u, 1][:, :FIRST], ALU.max, ALU.add)
             nc.scalar.activation(h[u][:, :FIRST], d_first[:], ACT.Abs)
+        quantise_w1(1, 2, PACK)
         for t in (2, 3):
             pages.setdefault(t, laid.tile([P, T2], F32, name="page%d" % t, offset=t * 8 * KIB, align_bytes=64))
             nc.gpsimd.memset(pages[t][:].bitcast(I32), 0)
-        def scatter(t, e0, e1):
-            nc.vector.tensor_tensor(
-                pages[t][:].indirect(idx2[:, e0 // 16 : e1 // 16]), gap(t, e0, e1), wg[:, t, e0:e1], ALU.mult
-            )
-
         for u in range(DIRECT, len(units)):
-            if u == LATE_UNIT:
-                for piece in SCATTERS[:HELD]:
-                    scatter(*piece)
-                late.setdefault("grouped", keep.tile([P, 2 * BANK], BF16, name="late_grouped", tag="late_cast", align_bytes=64))
-                late.setdefault("codes", keep.tile([P, 2 * P], U32, name="late_codes", tag="late_codes", align_bytes=64))
-                cast(1, 2, PACK, nc.scalar.copy)
-                quantise_w1(1, 2, PACK)
-                order_w4(1, 2, PACK, nc.scalar.copy)
             rectified_view(u)
             term(u, 0)
             linear_view(u)
             if u > DIRECT:
                 gaps(u - 1)
+            if u == DIRECT + 2:
+                order_w4(1, 2, PACK, nc.scalar.copy, "w4_late")
         gaps(len(units) - 1)
 
         stack = [
             keep.tile([P, PACK, HALF], F32, name="stack%d" % part, tag=tag, align_bytes=64)
             for part, tag in enumerate(("v0", "v1"))
         ]
-        for t, e0, e1 in SCATTERS[HELD:]:
-            scatter(t, e0, e1)
+        for t, e0, e1 in SCATTERS:
+            nc.vector.tensor_tensor(
+                pages[t][:].indirect(idx2[:, e0 // 16 : e1 // 16]), h[t][:, e0:e1], wg[:, t, e0:e1], ALU.mult
+            )
             if e1 == S:
                 move = nc.sync.dma_start if t == PACK - 2 else nc.scalar.copy
                 for lo, hi in ((0, HALF), (HALF, T2)) if t < PACK - 1 else LAST_COPIES:

@@ -31,8 +31,14 @@ PIECES = ((0, FIRST), (FIRST, 2 * FIRST), (2 * FIRST, S))
 SCATTERS = tuple((t, e0, e1) for e0, e1 in PIECES for t in (0, 1)) + (
     (2, 0, 512), (3, 0, 256), (2, 512, 1024), (3, 256, 1024),
 )
-NODE_CHUNKS = (128, 128, 256, 256, 256, 256, 256, 256, 128, 128)
-LAST_COPIES = ((0, 128), (128, 256), (256, 512), (512, 1024), (1024, 2048))
+TURNED = 256
+TURNED_AT = T2 - TURNED
+NODE_CHUNKS = (128, 128, 384, 384, 384, 384)
+TURNED_AFTER = 2
+NEAR = sum(NODE_CHUNKS[: TURNED_AFTER + 1])
+TURN_AT_UNIT = 6
+EXCESS_BANK = 3
+LAST_COPIES = ((0, 128), (128, 256), (256, 640))
 KIB = 1024
 HALF = T2 // 2
 PAIR = 2
@@ -53,7 +59,7 @@ def tile_list_neighbour_gap_message_kernel(
         keep = ctx.enter_context(tc.tile_pool(name="keep", bufs=1))
         laid = ctx.enter_context(tc.tile_pool(name="laid", bufs=1))
         ring = ctx.enter_context(tc.tile_pool(name="ring", bufs=2))
-        outs = ctx.enter_context(tc.tile_pool(name="outs", bufs=12))
+        outs = ctx.enter_context(tc.tile_pool(name="outs", bufs=3))
         psum = ctx.enter_context(tc.psum_pool(name="psum", bufs=1))
 
         idx = keep.tile([P, S // 16], U16, name="idx")
@@ -63,7 +69,9 @@ def tile_list_neighbour_gap_message_kernel(
         planes = keep.tile([P, PASSES * PLANE], U8, name="planes", align_bytes=64)
         tab = [keep.tile([P, T], I32, name="tab%d" % a, tag="tab%d" % a, align_bytes=64) for a in range(PASSES)]
         w4_raw = [keep.tile([P, 2 * H], U8, name="w4_raw%d" % a, align_bytes=64) for a in range(PASSES)]
-        w1_raw = [keep.tile([P, PACK, H], F32, name="w1_raw%d" % a, align_bytes=64) for a in range(PASSES)]
+        w1_raw = [
+            keep.tile([P, PACK, H], F32, name="w1_raw%d" % a, tag="w1_raw%d" % a, align_bytes=64) for a in range(PASSES)
+        ]
         ident = keep.tile([P, P], F32, name="ident", align_bytes=64)
 
         live = PASSES * ROWS
@@ -158,12 +166,15 @@ def tile_list_neighbour_gap_message_kernel(
             )
 
         state_rows = state.rearrange("(p t) n -> p t n", t=PACK)
+        st_cuts = ((0, NEAR), (NEAR, TURNED_AT))
         st = [
-            keep.tile([P, PACK, HALF], F32, name="st%d" % part, tag=tag, align_bytes=64)
-            for part, tag in enumerate(("tab0", "tab1"))
+            keep.tile([P, PACK, hi - lo], F32, name="st%d" % part, tag="tab%d" % part, align_bytes=64)
+            for part, (lo, hi) in enumerate(st_cuts)
         ]
-        for part in range(2):
-            nc.sync.dma_start(st[part][:], state_rows[:, :, part * HALF : (part + 1) * HALF])
+        st_turned = keep.tile([P, PACK, TURNED], F32, name="st_turned", align_bytes=64)
+        nc.sync.dma_start(st_turned[:], state_rows[:, :, TURNED_AT:])
+        for part, (lo, hi) in enumerate(st_cuts):
+            nc.sync.dma_start(st[part][:], state_rows[:, :, lo:hi])
 
         h = [keep.tile([P, S], F32, name="h%d" % t, align_bytes=64) for t in range(PACK)]
         units = [(t, lo, min(lo + BANK, e1)) for t, e0, e1 in SCATTERS for lo in range(e0, e1, BANK)]
@@ -174,6 +185,8 @@ def tile_list_neighbour_gap_message_kernel(
             return psum.tile([P, BANK], F32, name=name, tag="bank%d" % b)
 
         def sum_bank(u, k):
+            if k == 1 and u >= TURN_AT_UNIT:
+                return 4 + u % 2
             return u % 4 if k == 0 else 4 + u % 2 + 2 * ((max(u // 2, 1) + 1) % 2)
 
         def weights(k, a, t):
@@ -230,7 +243,7 @@ def tile_list_neighbour_gap_message_kernel(
             t, e0, e1 = units[u]
             width = e1 - e0
             blocks = width // P
-            d_ps = bank(sum_bank(u, 0), "d_ps")
+            d_ps = bank(sum_bank(u, 0) if u < len(units) - 1 else EXCESS_BANK, "d_ps")
             for k, sb in enumerate((terms[u, 1], terms[u, 0])):
                 for b in range(blocks):
                     nc.tensor.matmul(
@@ -242,6 +255,48 @@ def tile_list_neighbour_gap_message_kernel(
                         stop=(k == 1 and b == blocks - 1),
                     )
             nc.scalar.activation(h[t][:, e0:e1], d_ps[:, :width], ACT.Abs)
+
+        blocks = TURNED // P
+        s_turned = keep.tile([P, blocks, PACK, P], F32, name="s_turned", tag="w1_raw0", align_bytes=64)
+        s_minus = keep.tile([P, blocks, PACK, P], F32, name="s_minus", tag="w1_raw1", align_bytes=64)
+        z_sums = []
+
+        def turn(dst, src, start, stop):
+            nc.tensor.matmul(dst, lhsT=src, rhs=ident[:], is_transpose=True, start=start, stop=stop)
+
+        def turned_state():
+            for b in range(blocks):
+                ps = bank(BANKS - blocks + b, "s_ps")
+                for t in range(PACK):
+                    turn(ps[:, t * P : (t + 1) * P], st_turned[:, t, b * P : (b + 1) * P], t == 0, t == PACK - 1)
+                nc.scalar.activation(s_turned[:, b].rearrange("p t n -> p (t n)"), ps[:], ACT.Relu)
+            for b in range(blocks):
+                ps = bank(BANKS - blocks + b, "m_ps")
+                for t in range(PACK):
+                    turn(ps[:, t * P : (t + 1) * P], s_turned[:, b, t, :], t == 0, t == PACK - 1)
+                nc.scalar.activation(s_minus[:, b].rearrange("p t n -> p (t n)"), ps[:], ACT.Copy, scale=-1.0)
+            for b in range(blocks):
+                z_sums.append(bank(BANKS - blocks + b, "z_ps"))
+                for t in range(PACK):
+                    turn(z_sums[b][:, t * P : (t + 1) * P], s_turned[:, b, t, :], t == 0, False)
+
+        def excess(slots, in_bank):
+            ps = bank(in_bank, "r_ps")
+            cells = [(i, t, b) for i, t in enumerate(slots) for b in range(blocks)]
+            for n, (i, t, b) in enumerate(cells):
+                turn(ps[:, n * P : (n + 1) * P], s_minus[:, b, t, :], n == 0, False)
+            for n, (i, t, b) in enumerate(cells):
+                at = TURNED_AT + b * P
+                turn(ps[:, n * P : (n + 1) * P], pages[t][:, at : at + P], False, n == len(cells) - 1)
+            for i, t in enumerate(slots):
+                if t == PACK - 2:
+                    r_turned = stack[0][:, PACK - 1, :TURNED]
+                else:
+                    r_tile = keep.tile([P, TURNED], F32, name="r_turned%d" % t, align_bytes=64)
+                    r_turned = r_tile[:]
+                nc.scalar.activation(r_turned, ps[:, i * TURNED : (i + 1) * TURNED], ACT.Relu)
+                for b in range(blocks):
+                    turn(z_sums[b][:, t * P : (t + 1) * P], r_turned[:, b * P : (b + 1) * P], False, t == PACK - 1)
 
         cast(0, 0, 2, nc.vector.tensor_copy)
         cast(0, 2, PACK, nc.scalar.copy)
@@ -267,7 +322,16 @@ def tile_list_neighbour_gap_message_kernel(
         for t in (2, 3):
             pages.setdefault(t, laid.tile([P, T2], F32, name="page%d" % t, offset=t * 8 * KIB, align_bytes=64))
             nc.gpsimd.memset(pages[t][:].bitcast(I32), 0)
+        stack = []
+
+        def scatter(t, e0, e1):
+            nc.vector.tensor_tensor(
+                pages[t][:].indirect(idx2[:, e0 // 16 : e1 // 16]), h[t][:, e0:e1], wg[:, t, e0:e1], ALU.mult
+            )
+
         for u in range(DIRECT, len(units)):
+            if u == TURN_AT_UNIT:
+                turned_state()
             rectified_view(u)
             term(u, 0)
             linear_view(u)
@@ -275,21 +339,28 @@ def tile_list_neighbour_gap_message_kernel(
                 gaps(u - 1)
             if u == DIRECT + 2:
                 order_w4(1, 2, PACK, nc.scalar.copy, "w4_late")
+        for t, e0, e1 in SCATTERS[: 2 * len(PIECES)]:
+            scatter(t, e0, e1)
+        excess((0, 1), EXCESS_BANK)
         gaps(len(units) - 1)
 
-        stack = [
+        stack.extend(
             keep.tile([P, PACK, HALF], F32, name="stack%d" % part, tag=tag, align_bytes=64)
             for part, tag in enumerate(("v0", "v1"))
-        ]
+        )
         for t, e0, e1 in SCATTERS:
-            nc.vector.tensor_tensor(
-                pages[t][:].indirect(idx2[:, e0 // 16 : e1 // 16]), h[t][:, e0:e1], wg[:, t, e0:e1], ALU.mult
-            )
+            if t > 1:
+                scatter(t, e0, e1)
             if e1 == S:
-                move = nc.sync.dma_start if t == PACK - 2 else nc.scalar.copy
-                for lo, hi in ((0, HALF), (HALF, T2)) if t < PACK - 1 else LAST_COPIES:
+                move = nc.sync.dma_start if t < PACK - 1 else nc.scalar.copy
+                for lo, hi in ((0, HALF), (HALF, TURNED_AT)) if t < PACK - 1 else LAST_COPIES:
                     part, at = divmod(lo, HALF)
                     move(stack[part][:, t, at : at + hi - lo], pages[t][:, lo:hi])
+                if t == PACK - 1:
+                    nc.sync.dma_start(stack[0][:, t, NEAR:], pages[t][:, NEAR:HALF])
+                    nc.sync.dma_start(stack[1][:, t, : TURNED_AT - HALF], pages[t][:, HALF:TURNED_AT])
+                if t > 1:
+                    excess((t,), EXCESS_BANK)
 
         starts = [sum(NODE_CHUNKS[:c]) for c in range(len(NODE_CHUNKS))]
 
@@ -298,55 +369,75 @@ def tile_list_neighbour_gap_message_kernel(
 
         def maximum(c, lo, hi):
             part, at = divmod(starts[c], HALF)
+            far = c > TURNED_AFTER
+            st_at = starts[c] - (NEAR if far else 0)
             if c not in wovens:
                 wovens.setdefault(c, ring.tile([P, PACK * max(NODE_CHUNKS)], BF16, name="woven", bufs=3, align_bytes=64))
             nc.vector.tensor_tensor(
                 wovens[c][:, PACK * lo : PACK * hi].rearrange("p (c i t) -> p c t i", i=PAIR, t=PACK),
                 stack[part][:, :, at + lo : at + hi].rearrange("p t (c i) -> p c t i", i=PAIR),
-                st[part][:, :, at + lo : at + hi].rearrange("p t (c i) -> p c t i", i=PAIR),
+                st[far][:, :, st_at + lo : st_at + hi].rearrange("p t (c i) -> p c t i", i=PAIR),
                 ALU.max,
             )
 
-        def quantise(c, woven):
-            width = NODE_CHUNKS[c]
-            z_codes = ring.tile([P, max(NODE_CHUNKS)], U32, name="z_codes", align_bytes=64)
-            z_scales = ring.tile([P, max(NODE_CHUNKS)], U8, name="z_scales", align_bytes=64)
+        def quantise(width, woven, turned=False):
+            if turned:
+                z_codes = keep.tile([P, width], U32, name="z_turned", tag="tab0", align_bytes=64)
+            else:
+                z_codes = ring.tile([P, max(NODE_CHUNKS)], U32, name="z_codes", align_bytes=64)
+            z_scales = ring.tile([P, max(NODE_CHUNKS)], U8, name="z_scales", bufs=3, align_bytes=64)
             nc.vector.quantize_mx(
                 out=z_codes[:, :width].bitcast(FP8X4), scales=z_scales[:, :width], in_=woven[:, : PACK * width]
             )
             return z_codes, z_scales
 
-        def messages(c, z_codes, z_scales):
-            n0, width = starts[c], NODE_CHUNKS[c]
-            per_bank = 2 if c == len(NODE_CHUNKS) - 1 else BANK // width
-            for b0 in range(0, N // P, per_bank):
+        wide_places = [dict(offset=0), dict(offset=8 * KIB), dict(tag="w1_raw0"), dict(tag="w1_raw1")]
+
+        def messages(n0, width, z_codes, z_scales, on_vector):
+            total = N // P * width
+            if total > 3 * BANK - 1:
+                place = wide_places.pop(0)
+                o_sb = (laid if "offset" in place else keep).tile([P, total], F32, name="o_wide%d" % n0, align_bytes=64, **place)
+            else:
+                o_sb = outs.tile([P, 2 * BANK], F32, name="o_sb", align_bytes=64)
+            done = 0
+            for q in range(total // BANK):
                 o_ps = bank(len(stored) % BANKS, "o_ps")
-                stored.append((c, b0))
-                for k in range(per_bank):
-                    b = b0 + k
+                stored.append((n0, q))
+                at = q * BANK
+                while at < (q + 1) * BANK:
+                    b, lo = divmod(at, width)
+                    room = min(width - lo, (q + 1) * BANK - at)
+                    hi = lo + (room if room != 3 * P else 2 * P)
                     nc.tensor.matmul_mx(
-                        out=o_ps[:, k * width : (k + 1) * width],
+                        out=o_ps[:, at - q * BANK : at - q * BANK + hi - lo],
                         lhsT=w8[:, b * P : (b + 1) * P].bitcast(FP8X4),
                         lhsT_scale=w8_plane[:, b * P : (b + 1) * P],
-                        rhs=z_codes[:, :width].bitcast(FP8X4),
-                        rhs_scale=z_scales[:, :width],
+                        rhs=z_codes[:, lo:hi].bitcast(FP8X4),
+                        rhs_scale=z_scales[:, lo:hi],
                         start=True,
                         stop=True,
                     )
-                o_sb = outs.tile([P, BANK], F32, name="o_sb", align_bytes=64)
-                used = per_bank * width
-                if c == len(NODE_CHUNKS) - 1:
-                    nc.vector.tensor_copy(o_sb[:, :used], o_ps[:, :used])
-                else:
-                    nc.scalar.copy(o_sb[:, :used], o_ps[:, :used])
+                    at = at + hi - lo
+                copy = nc.vector.tensor_copy if q in on_vector else nc.scalar.copy
+                copy(o_sb[:, q * BANK : (q + 1) * BANK], o_ps[:])
+                whole = (q + 1) * BANK // width
                 nc.sync.dma_start(
-                    out[b0 * P : (b0 + per_bank) * P, n0 : n0 + width].rearrange("(k p) n -> p k n", p=P),
-                    o_sb[:, :used].rearrange("p (k n) -> p k n", k=per_bank),
+                    out[done * P : whole * P, n0 : n0 + width].rearrange("(k p) n -> p k n", p=P),
+                    o_sb[:, done * width : whole * width].rearrange("p (k n) -> p k n", n=width),
                 )
+                done = whole
 
+        woven_turned = keep.tile([P, PACK * TURNED], BF16, name="woven_turned", align_bytes=64)
+        for b in range(blocks):
+            nc.scalar.copy(
+                woven_turned[:, b * BANK : (b + 1) * BANK].rearrange("p (n t) -> p n t", t=PACK),
+                z_sums[b][:].rearrange("p (t n) -> p n t", t=PACK),
+            )
         for c, width in enumerate(NODE_CHUNKS):
-            maximum(c, LEAD if c > 0 else 0, width)
-            if c + 1 < len(NODE_CHUNKS):
+            maximum(c, LEAD if c not in (0, TURNED_AFTER + 1) else 0, width)
+            if c == TURNED_AFTER:
+                messages(TURNED_AT, TURNED, *quantise(TURNED, woven_turned, True), ())
+            elif c + 1 < len(NODE_CHUNKS):
                 maximum(c + 1, 0, LEAD)
-            z_codes, z_scales = quantise(c, wovens[c])
-            messages(c, z_codes, z_scales)
+            messages(starts[c], width, *quantise(width, wovens[c]), (0, 2) if c == len(NODE_CHUNKS) - 1 else ())

@@ -33,12 +33,12 @@ SCATTERS = tuple((t, e0, e1) for e0, e1 in PIECES for t in (0, 1)) + (
 )
 TURNED = 256
 TURNED_AT = T2 - TURNED
-NODE_CHUNKS = (128, 128, 384, 384, 384, 384)
-TURNED_AFTER = 2
+NODE_CHUNKS = (128, 128, 256, 256, 256, 256, 256, 128, 128)
+TURNED_AFTER = 4
 NEAR = sum(NODE_CHUNKS[: TURNED_AFTER + 1])
 TURN_AT_UNIT = 6
 EXCESS_BANK = 3
-LAST_COPIES = ((0, 128), (128, 256), (256, 640))
+LAST_COPIES = ((0, 128), (128, 256), (256, 512), (512, 1024))
 KIB = 1024
 HALF = T2 // 2
 PAIR = 2
@@ -59,7 +59,7 @@ def tile_list_neighbour_gap_message_kernel(
         keep = ctx.enter_context(tc.tile_pool(name="keep", bufs=1))
         laid = ctx.enter_context(tc.tile_pool(name="laid", bufs=1))
         ring = ctx.enter_context(tc.tile_pool(name="ring", bufs=2))
-        outs = ctx.enter_context(tc.tile_pool(name="outs", bufs=3))
+        outs = ctx.enter_context(tc.tile_pool(name="outs", bufs=10))
         psum = ctx.enter_context(tc.psum_pool(name="psum", bufs=1))
 
         idx = keep.tile([P, S // 16], U16, name="idx")
@@ -288,15 +288,10 @@ def tile_list_neighbour_gap_message_kernel(
             for n, (i, t, b) in enumerate(cells):
                 at = TURNED_AT + b * P
                 turn(ps[:, n * P : (n + 1) * P], pages[t][:, at : at + P], False, n == len(cells) - 1)
-            for i, t in enumerate(slots):
-                if t == PACK - 2:
-                    r_turned = stack[0][:, PACK - 1, :TURNED]
-                else:
-                    r_tile = keep.tile([P, TURNED], F32, name="r_turned%d" % t, align_bytes=64)
-                    r_turned = r_tile[:]
-                nc.scalar.activation(r_turned, ps[:, i * TURNED : (i + 1) * TURNED], ACT.Relu)
-                for b in range(blocks):
-                    turn(z_sums[b][:, t * P : (t + 1) * P], r_turned[:, b * P : (b + 1) * P], False, t == PACK - 1)
+            r_turned = keep.tile([P, BANK], F32, name="r_turned%d" % slots[0], align_bytes=64)
+            nc.scalar.activation(r_turned[:], ps[:], ACT.Relu)
+            for n, (i, t, b) in enumerate(cells):
+                turn(z_sums[b][:, t * P : (t + 1) * P], r_turned[:, n * P : (n + 1) * P], False, t == PACK - 1)
 
         cast(0, 0, 2, nc.vector.tensor_copy)
         cast(0, 2, PACK, nc.scalar.copy)
@@ -357,10 +352,8 @@ def tile_list_neighbour_gap_message_kernel(
                     part, at = divmod(lo, HALF)
                     move(stack[part][:, t, at : at + hi - lo], pages[t][:, lo:hi])
                 if t == PACK - 1:
-                    nc.sync.dma_start(stack[0][:, t, NEAR:], pages[t][:, NEAR:HALF])
                     nc.sync.dma_start(stack[1][:, t, : TURNED_AT - HALF], pages[t][:, HALF:TURNED_AT])
-                if t > 1:
-                    excess((t,), EXCESS_BANK)
+                    excess((2, 3), EXCESS_BANK)
 
         starts = [sum(NODE_CHUNKS[:c]) for c in range(len(NODE_CHUNKS))]
 
@@ -391,53 +384,42 @@ def tile_list_neighbour_gap_message_kernel(
             )
             return z_codes, z_scales
 
-        wide_places = [dict(offset=0), dict(offset=8 * KIB), dict(tag="w1_raw0"), dict(tag="w1_raw1")]
-
-        def messages(n0, width, z_codes, z_scales, on_vector):
-            total = N // P * width
-            if total > 3 * BANK - 1:
-                place = wide_places.pop(0)
-                o_sb = (laid if "offset" in place else keep).tile([P, total], F32, name="o_wide%d" % n0, align_bytes=64, **place)
-            else:
-                o_sb = outs.tile([P, 2 * BANK], F32, name="o_sb", align_bytes=64)
-            done = 0
-            for q in range(total // BANK):
+        def messages(n0, width, z_codes, z_scales, left):
+            per_bank = 2 if left == 0 else BANK // width
+            for b0 in range(0, N // P, per_bank):
                 o_ps = bank(len(stored) % BANKS, "o_ps")
-                stored.append((n0, q))
-                at = q * BANK
-                while at < (q + 1) * BANK:
-                    b, lo = divmod(at, width)
-                    room = min(width - lo, (q + 1) * BANK - at)
-                    hi = lo + (room if room != 3 * P else 2 * P)
+                stored.append((n0, b0))
+                for k in range(per_bank):
+                    b = b0 + k
                     nc.tensor.matmul_mx(
-                        out=o_ps[:, at - q * BANK : at - q * BANK + hi - lo],
+                        out=o_ps[:, k * width : (k + 1) * width],
                         lhsT=w8[:, b * P : (b + 1) * P].bitcast(FP8X4),
                         lhsT_scale=w8_plane[:, b * P : (b + 1) * P],
-                        rhs=z_codes[:, lo:hi].bitcast(FP8X4),
-                        rhs_scale=z_scales[:, lo:hi],
+                        rhs=z_codes[:, :width].bitcast(FP8X4),
+                        rhs_scale=z_scales[:, :width],
                         start=True,
                         stop=True,
                     )
-                    at = at + hi - lo
-                copy = nc.vector.tensor_copy if q in on_vector else nc.scalar.copy
-                copy(o_sb[:, q * BANK : (q + 1) * BANK], o_ps[:])
-                whole = (q + 1) * BANK // width
+                o_sb = outs.tile([P, BANK], F32, name="o_sb", align_bytes=64)
+                used = per_bank * width
+                copy = nc.vector.tensor_copy if left == 1 or (left == 0 and b0 > 0) else nc.scalar.copy
+                copy(o_sb[:, :used], o_ps[:, :used])
                 nc.sync.dma_start(
-                    out[done * P : whole * P, n0 : n0 + width].rearrange("(k p) n -> p k n", p=P),
-                    o_sb[:, done * width : whole * width].rearrange("p (k n) -> p k n", n=width),
+                    out[b0 * P : (b0 + per_bank) * P, n0 : n0 + width].rearrange("(k p) n -> p k n", p=P),
+                    o_sb[:, :used].rearrange("p (k n) -> p k n", k=per_bank),
                 )
-                done = whole
 
         woven_turned = keep.tile([P, PACK * TURNED], BF16, name="woven_turned", align_bytes=64)
-        for b in range(blocks):
-            nc.scalar.copy(
-                woven_turned[:, b * BANK : (b + 1) * BANK].rearrange("p (n t) -> p n t", t=PACK),
-                z_sums[b][:].rearrange("p (t n) -> p n t", t=PACK),
-            )
         for c, width in enumerate(NODE_CHUNKS):
             maximum(c, LEAD if c not in (0, TURNED_AFTER + 1) else 0, width)
             if c == TURNED_AFTER:
-                messages(TURNED_AT, TURNED, *quantise(TURNED, woven_turned, True), ())
+                messages(TURNED_AT, TURNED, *quantise(TURNED, woven_turned, True), None)
             elif c + 1 < len(NODE_CHUNKS):
                 maximum(c + 1, 0, LEAD)
-            messages(starts[c], width, *quantise(width, wovens[c]), (0, 2) if c == len(NODE_CHUNKS) - 1 else ())
+            messages(starts[c], width, *quantise(width, wovens[c]), len(NODE_CHUNKS) - 1 - c)
+            if c == TURNED_AFTER - 2:
+                for b in range(blocks):
+                    nc.scalar.copy(
+                        woven_turned[:, b * BANK : (b + 1) * BANK].rearrange("p (n t) -> p n t", t=PACK),
+                        z_sums[b][:].rearrange("p (t n) -> p n t", t=PACK),
+                    )

@@ -129,7 +129,11 @@ def tile_list_neighbour_gap_message_kernel(
 
         wgs_rows = wgs.rearrange("(q t) j -> q t j", t=PACK)
         wg = keep.tile([P, PACK, S], F32, name="wg", align_bytes=64)
+        state_rows = state.rearrange("(p t) n -> p t n", t=PACK)
+        st_turned = keep.tile([P, PACK, TURNED], F32, name="st_turned", align_bytes=64)
         for t0, t1, e0, e1 in WG_LOADS:
+            if t0 == 2:
+                nc.sync.dma_start(st_turned[:], state_rows[:, :, TURNED_AT:])
             for g in QUAD_ORDER:
                 nc.sync.dma_start(wg[g * QUAD : (g + 1) * QUAD, t0:t1, e0:e1], wgs_rows[:, t0:t1, e0:e1])
         w8 = keep.tile([P, N], I32, name="w8", align_bytes=64)
@@ -165,14 +169,11 @@ def tile_list_neighbour_gap_message_kernel(
                 in_=grouped[:, a, t0 * BANK : t1 * BANK],
             )
 
-        state_rows = state.rearrange("(p t) n -> p t n", t=PACK)
         st_cuts = ((0, NEAR), (NEAR, TURNED_AT))
         st = [
             keep.tile([P, PACK, hi - lo], F32, name="st%d" % part, tag="tab%d" % part, align_bytes=64)
             for part, (lo, hi) in enumerate(st_cuts)
         ]
-        st_turned = keep.tile([P, PACK, TURNED], F32, name="st_turned", align_bytes=64)
-        nc.sync.dma_start(st_turned[:], state_rows[:, :, TURNED_AT:])
         for part, (lo, hi) in enumerate(st_cuts):
             nc.sync.dma_start(st[part][:], state_rows[:, :, lo:hi])
 
@@ -220,6 +221,8 @@ def tile_list_neighbour_gap_message_kernel(
             width = units[u][2] - units[u][1]
             if u == DIRECT:
                 sb = keep.tile([P, width], F32, name="term_behind", tag="d_first%d" % k, align_bytes=64)
+            elif u == len(units) - 1:
+                sb = keep.tile([P, width], F32, name="term_last", tag="v%d" % k, align_bytes=64)
             elif (u, k) == (DIRECT + 1, 0):
                 sb = keep.tile([P, width], F32, name="term_ahead", tag="w4_late", align_bytes=64)
             else:
@@ -347,7 +350,7 @@ def tile_list_neighbour_gap_message_kernel(
             if t > 1:
                 scatter(t, e0, e1)
             if e1 == S:
-                move = nc.sync.dma_start if t < PACK - 1 else nc.scalar.copy
+                move = nc.sync.dma_start if t == PACK - 2 else nc.scalar.copy
                 for lo, hi in ((0, HALF), (HALF, TURNED_AT)) if t < PACK - 1 else LAST_COPIES:
                     part, at = divmod(lo, HALF)
                     move(stack[part][:, t, at : at + hi - lo], pages[t][:, lo:hi])

@@ -64,15 +64,15 @@ def tile_list_neighbour_gap_message_kernel(
 
         idx = keep.tile([P, S // 16], U16, name="idx")
         idx2 = keep.tile([P, S // 16], U16, name="idx2")
-        tsc = keep.tile([P, T], U8, name="tsc", tag="tsc", align_bytes=64)
-        w4s_raw = keep.tile([P, H], U8, name="w4s_raw", align_bytes=64)
-        planes = keep.tile([P, PASSES * PLANE], U8, name="planes", align_bytes=64)
-        tab = [keep.tile([P, T], I32, name="tab%d" % a, tag="tab%d" % a, align_bytes=64) for a in range(PASSES)]
-        w4_raw = [keep.tile([P, 2 * H], U8, name="w4_raw%d" % a, align_bytes=64) for a in range(PASSES)]
+        tsc = keep.tile([P, T], U8, name="tsc", tag="tsc", align_bytes=256)
+        w4s_raw = keep.tile([P, H], U8, name="w4s_raw", align_bytes=256)
+        planes = keep.tile([P, PASSES * PLANE], U8, name="planes", align_bytes=256)
+        tab = [keep.tile([P, T], I32, name="tab%d" % a, tag="tab%d" % a, align_bytes=256) for a in range(PASSES)]
+        w4_raw = [keep.tile([P, 2 * H], U8, name="w4_raw%d" % a, align_bytes=256) for a in range(PASSES)]
         w1_raw = [
-            keep.tile([P, PACK, H], F32, name="w1_raw%d" % a, tag="w1_raw%d" % a, align_bytes=64) for a in range(PASSES)
+            keep.tile([P, PACK, H], F32, name="w1_raw%d" % a, tag="w1_raw%d" % a, align_bytes=256) for a in range(PASSES)
         ]
-        ident = keep.tile([P, P], F32, name="ident", align_bytes=64)
+        ident = keep.tile([P, P], F32, name="ident", align_bytes=256)
 
         live = PASSES * ROWS
         for lo, hi in ((QUAD, 2 * QUAD), (2 * QUAD, P)):
@@ -89,7 +89,7 @@ def tile_list_neighbour_gap_message_kernel(
             nc.sync.dma_start(tab[a][:], tab_words[a].rearrange("p t i -> p (t i)").bitcast(I32))
         nc.sync.dma_start(w4_raw[0][:].bitcast(I32), w4_words[0].bitcast(I32))
 
-        gsc = keep.tile([P, S], U8, name="gsc", align_bytes=64)
+        gsc = keep.tile([P, S], U8, name="gsc", align_bytes=256)
         nc.vector.tensor_copy(
             planes[:, W4_AT:PLANE].rearrange("p (t m) -> p t m", t=PACK),
             w4s_raw[:].rearrange("p (m t) -> p t m", t=PACK),
@@ -117,7 +117,7 @@ def tile_list_neighbour_gap_message_kernel(
         w4 = {}
 
         def order_w4(a, t0, t1, copy, tag):
-            words = keep.tile([P, 2 * (t1 - t0) * P], U8, name="w4_%d%d" % (a, t0), tag=tag, align_bytes=64)
+            words = keep.tile([P, 2 * (t1 - t0) * P], U8, name="w4_%d%d" % (a, t0), tag=tag, align_bytes=256)
             for t in range(t0, t1):
                 w4.setdefault((a, t), words[:, 2 * (t - t0) * P : 2 * (t - t0 + 1) * P])
             copy(
@@ -128,16 +128,16 @@ def tile_list_neighbour_gap_message_kernel(
         order_w4(0, 0, PACK, nc.vector.tensor_copy, "w4_first")
 
         wgs_rows = wgs.rearrange("(q t) j -> q t j", t=PACK)
-        wg = keep.tile([P, PACK, S], F32, name="wg", align_bytes=64)
+        wg = keep.tile([P, PACK, S], F32, name="wg", align_bytes=256)
         state_rows = state.rearrange("(p t) n -> p t n", t=PACK)
-        st_turned = keep.tile([P, PACK, TURNED], F32, name="st_turned", align_bytes=64)
+        st_turned = keep.tile([P, PACK, TURNED], F32, name="st_turned", align_bytes=256)
         for t0, t1, e0, e1 in WG_LOADS:
             if t0 == 2:
                 nc.sync.dma_start(st_turned[:], state_rows[:, :, TURNED_AT:])
             for g in QUAD_ORDER:
                 nc.sync.dma_start(wg[g * QUAD : (g + 1) * QUAD, t0:t1, e0:e1], wgs_rows[:, t0:t1, e0:e1])
-        w8 = keep.tile([P, N], I32, name="w8", align_bytes=64)
-        w8_plane = keep.tile([P, N], U8, name="w8_plane", align_bytes=64)
+        w8 = keep.tile([P, N], I32, name="w8", align_bytes=256)
+        w8_plane = keep.tile([P, N], U8, name="w8_plane", align_bytes=256)
         nc.vector.memset(w8_plane[:].bitcast(I32), 0)
         nc.sync.dma_start(w8[:], w8_words[0].rearrange("p c i -> p (c i)").bitcast(I32))
         for q in range(P // QUAD):
@@ -146,15 +146,15 @@ def tile_list_neighbour_gap_message_kernel(
             )
 
         for t, tag in enumerate(("page0", "tsc")):
-            pages.setdefault(t, keep.tile([P, T2], F32, name="page%d" % t, tag=tag, align_bytes=64))
+            pages.setdefault(t, keep.tile([P, T2], F32, name="page%d" % t, tag=tag, align_bytes=256))
             nc.vector.memset(pages[t][:].bitcast(I32), 0)
-        v = [keep.tile([P, S], U32, name="v%d" % a, tag="v%d" % a, align_bytes=64) for a in range(PASSES)]
+        v = [keep.tile([P, S], U32, name="v%d" % a, tag="v%d" % a, align_bytes=256) for a in range(PASSES)]
         for a in range(PASSES):
             nc.vector.tensor_copy(v[a][:], tab[a][:].bitcast(U32).indirect(idx[:]))
 
-        w1_codes = keep.tile([P, PASSES, H], U32, name="w1_codes", align_bytes=64)
-        w1_scales = keep.tile([P, PASSES, H], U8, name="w1_scales", align_bytes=64)
-        grouped = laid.tile([P, PASSES, H * PACK], BF16, name="grouped", offset=20 * KIB, align_bytes=64)
+        w1_codes = keep.tile([P, PASSES, H], U32, name="w1_codes", align_bytes=256)
+        w1_scales = keep.tile([P, PASSES, H], U8, name="w1_scales", align_bytes=256)
+        grouped = laid.tile([P, PASSES, H * PACK], BF16, name="grouped", offset=20 * KIB, align_bytes=256)
 
         def cast(a, t0, t1, copy, m0=0, m1=P):
             copy(
@@ -171,13 +171,13 @@ def tile_list_neighbour_gap_message_kernel(
 
         st_cuts = ((0, NEAR), (NEAR, TURNED_AT))
         st = [
-            keep.tile([P, PACK, hi - lo], F32, name="st%d" % part, tag="tab%d" % part, align_bytes=64)
+            keep.tile([P, PACK, hi - lo], F32, name="st%d" % part, tag="tab%d" % part, align_bytes=256)
             for part, (lo, hi) in enumerate(st_cuts)
         ]
         for part, (lo, hi) in enumerate(st_cuts):
             nc.sync.dma_start(st[part][:], state_rows[:, :, lo:hi])
 
-        h = [keep.tile([P, S], F32, name="h%d" % t, align_bytes=64) for t in range(PACK)]
+        h = [keep.tile([P, S], F32, name="h%d" % t, align_bytes=256) for t in range(PACK)]
         units = [(t, lo, min(lo + BANK, e1)) for t, e0, e1 in SCATTERS for lo in range(e0, e1, BANK)]
         sums = {}
         terms = {}
@@ -220,13 +220,13 @@ def tile_list_neighbour_gap_message_kernel(
         def term(u, k):
             width = units[u][2] - units[u][1]
             if u == DIRECT:
-                sb = keep.tile([P, width], F32, name="term_behind", tag="d_first%d" % k, align_bytes=64)
+                sb = keep.tile([P, width], F32, name="term_behind", tag="d_first%d" % k, align_bytes=256)
             elif u == len(units) - 1:
-                sb = keep.tile([P, width], F32, name="term_last", tag="v%d" % k, align_bytes=64)
+                sb = keep.tile([P, width], F32, name="term_last", tag="v%d" % k, align_bytes=256)
             elif (u, k) == (DIRECT + 1, 0):
-                sb = keep.tile([P, width], F32, name="term_ahead", tag="w4_late", align_bytes=64)
+                sb = keep.tile([P, width], F32, name="term_ahead", tag="w4_late", align_bytes=256)
             else:
-                sb = ring.tile([P, BANK], F32, name="term%d" % k, tag="term%d" % k, bufs=TERM_BUFS[k], align_bytes=64)
+                sb = ring.tile([P, BANK], F32, name="term%d" % k, tag="term%d" % k, bufs=TERM_BUFS[k], align_bytes=256)
             if k == 0:
                 nc.scalar.activation(sb[:, :width], sums[u, 0][:, :width], ACT.Relu)
             else:
@@ -260,8 +260,8 @@ def tile_list_neighbour_gap_message_kernel(
             nc.scalar.activation(h[t][:, e0:e1], d_ps[:, :width], ACT.Abs)
 
         blocks = TURNED // P
-        s_turned = keep.tile([P, blocks, PACK, P], F32, name="s_turned", tag="w1_raw0", align_bytes=64)
-        s_minus = keep.tile([P, blocks, PACK, P], F32, name="s_minus", tag="w1_raw1", align_bytes=64)
+        s_turned = keep.tile([P, blocks, PACK, P], F32, name="s_turned", tag="w1_raw0", align_bytes=256)
+        s_minus = keep.tile([P, blocks, PACK, P], F32, name="s_minus", tag="w1_raw1", align_bytes=256)
         z_sums = []
 
         def turn(dst, src, start, stop):
@@ -291,7 +291,10 @@ def tile_list_neighbour_gap_message_kernel(
             for n, (i, t, b) in enumerate(cells):
                 at = TURNED_AT + b * P
                 turn(ps[:, n * P : (n + 1) * P], pages[t][:, at : at + P], False, n == len(cells) - 1)
-            r_turned = keep.tile([P, BANK], F32, name="r_turned%d" % slots[0], align_bytes=64)
+            return ps, cells
+
+        def rectify(ps, cells, tag):
+            r_turned = keep.tile([P, BANK], F32, name="r_turned", tag=tag, align_bytes=256)
             nc.scalar.activation(r_turned[:], ps[:], ACT.Relu)
             for n, (i, t, b) in enumerate(cells):
                 turn(z_sums[b][:, t * P : (t + 1) * P], r_turned[:, n * P : (n + 1) * P], False, t == PACK - 1)
@@ -313,12 +316,12 @@ def tile_list_neighbour_gap_message_kernel(
             for u in range(DIRECT):
                 view(u)
         for u in range(DIRECT):
-            d_first = keep.tile([P, FIRST], F32, name="d_first%d" % u, tag="d_first%d" % u, align_bytes=64)
+            d_first = keep.tile([P, FIRST], F32, name="d_first%d" % u, tag="d_first%d" % u, align_bytes=256)
             nc.vector.scalar_tensor_tensor(d_first[:], sums[u, 0][:, :FIRST], 0.0, terms[u, 1][:, :FIRST], ALU.max, ALU.add)
             nc.scalar.activation(h[u][:, :FIRST], d_first[:], ACT.Abs)
         quantise_w1(1, 2, PACK)
         for t in (2, 3):
-            pages.setdefault(t, laid.tile([P, T2], F32, name="page%d" % t, offset=t * 8 * KIB, align_bytes=64))
+            pages.setdefault(t, laid.tile([P, T2], F32, name="page%d" % t, offset=t * 8 * KIB, align_bytes=256))
             nc.gpsimd.memset(pages[t][:].bitcast(I32), 0)
         stack = []
 
@@ -339,24 +342,23 @@ def tile_list_neighbour_gap_message_kernel(
                 order_w4(1, 2, PACK, nc.scalar.copy, "w4_late")
         for t, e0, e1 in SCATTERS[: 2 * len(PIECES)]:
             scatter(t, e0, e1)
-        excess((0, 1), EXCESS_BANK)
+        rectify(*excess((0, 1), EXCESS_BANK), "r_early")
         gaps(len(units) - 1)
 
         stack.extend(
-            keep.tile([P, PACK, HALF], F32, name="stack%d" % part, tag=tag, align_bytes=64)
+            keep.tile([P, PACK, HALF], F32, name="stack%d" % part, tag=tag, align_bytes=256)
             for part, tag in enumerate(("v0", "v1"))
         )
         for t, e0, e1 in SCATTERS:
             if t > 1:
                 scatter(t, e0, e1)
             if e1 == S:
-                move = nc.sync.dma_start if t == PACK - 2 else nc.scalar.copy
                 for lo, hi in ((0, HALF), (HALF, TURNED_AT)) if t < PACK - 1 else LAST_COPIES:
                     part, at = divmod(lo, HALF)
-                    move(stack[part][:, t, at : at + hi - lo], pages[t][:, lo:hi])
+                    nc.scalar.copy(stack[part][:, t, at : at + hi - lo], pages[t][:, lo:hi])
                 if t == PACK - 1:
                     nc.sync.dma_start(stack[1][:, t, : TURNED_AT - HALF], pages[t][:, HALF:TURNED_AT])
-                    excess((2, 3), EXCESS_BANK)
+                    late = excess((2, 3), EXCESS_BANK)
 
         starts = [sum(NODE_CHUNKS[:c]) for c in range(len(NODE_CHUNKS))]
 
@@ -368,7 +370,7 @@ def tile_list_neighbour_gap_message_kernel(
             far = c > TURNED_AFTER
             st_at = starts[c] - (NEAR if far else 0)
             if c not in wovens:
-                wovens.setdefault(c, ring.tile([P, PACK * max(NODE_CHUNKS)], BF16, name="woven", bufs=3, align_bytes=64))
+                wovens.setdefault(c, ring.tile([P, PACK * max(NODE_CHUNKS)], BF16, name="woven", bufs=3, align_bytes=256))
             nc.vector.tensor_tensor(
                 wovens[c][:, PACK * lo : PACK * hi].rearrange("p (c i t) -> p c t i", i=PAIR, t=PACK),
                 stack[part][:, :, at + lo : at + hi].rearrange("p t (c i) -> p c t i", i=PAIR),
@@ -376,12 +378,12 @@ def tile_list_neighbour_gap_message_kernel(
                 ALU.max,
             )
 
-        def quantise(width, woven, turned=False):
-            if turned:
-                z_codes = keep.tile([P, width], U32, name="z_turned", tag="tab0", align_bytes=64)
+        def quantise(width, woven, tag=None):
+            if tag is not None:
+                z_codes = keep.tile([P, width], U32, name="z_own", tag=tag, align_bytes=256)
             else:
-                z_codes = ring.tile([P, max(NODE_CHUNKS)], U32, name="z_codes", align_bytes=64)
-            z_scales = ring.tile([P, max(NODE_CHUNKS)], U8, name="z_scales", bufs=3, align_bytes=64)
+                z_codes = ring.tile([P, max(NODE_CHUNKS)], U32, name="z_codes", align_bytes=256)
+            z_scales = ring.tile([P, max(NODE_CHUNKS)], U8, name="z_scales", bufs=3, align_bytes=256)
             nc.vector.quantize_mx(
                 out=z_codes[:, :width].bitcast(FP8X4), scales=z_scales[:, :width], in_=woven[:, : PACK * width]
             )
@@ -403,7 +405,7 @@ def tile_list_neighbour_gap_message_kernel(
                         start=True,
                         stop=True,
                     )
-                o_sb = outs.tile([P, BANK], F32, name="o_sb", align_bytes=64)
+                o_sb = outs.tile([P, BANK], F32, name="o_sb", align_bytes=256)
                 used = per_bank * width
                 copy = nc.vector.tensor_copy if left == 1 or (left == 0 and b0 > 0) else nc.scalar.copy
                 copy(o_sb[:, :used], o_ps[:, :used])
@@ -412,17 +414,19 @@ def tile_list_neighbour_gap_message_kernel(
                     o_sb[:, :used].rearrange("p (k n) -> p k n", k=per_bank),
                 )
 
-        woven_turned = keep.tile([P, PACK * TURNED], BF16, name="woven_turned", align_bytes=64)
         for c, width in enumerate(NODE_CHUNKS):
             maximum(c, LEAD if c not in (0, TURNED_AFTER + 1) else 0, width)
             if c == TURNED_AFTER:
-                messages(TURNED_AT, TURNED, *quantise(TURNED, woven_turned, True), None)
+                messages(TURNED_AT, TURNED, *quantise(TURNED, woven_turned, "tab0"), None)
             elif c + 1 < len(NODE_CHUNKS):
                 maximum(c + 1, 0, LEAD)
-            messages(starts[c], width, *quantise(width, wovens[c]), len(NODE_CHUNKS) - 1 - c)
-            if c == TURNED_AFTER - 2:
+            messages(starts[c], width, *quantise(width, wovens[c], "z_first%d" % c if c < 2 else None), len(NODE_CHUNKS) - 1 - c)
+            if c == 0:
+                rectify(*late, "z_first0")
+            if c == 1:
+                woven_turned = keep.tile([P, PACK * TURNED], BF16, name="woven_turned", tag="z_first1", align_bytes=256)
                 for b in range(blocks):
                     nc.scalar.copy(
-                        woven_turned[:, b * BANK : (b + 1) * BANK].rearrange("p (n t) -> p n t", t=PACK),
-                        z_sums[b][:].rearrange("p (t n) -> p n t", t=PACK),
+                        woven_turned[:, b * BANK : (b + 1) * BANK].rearrange("p (c i t) -> p c t i", i=PAIR, t=PACK),
+                        z_sums[b][:].rearrange("p (t c i) -> p c t i", i=PAIR, t=PACK),
                     )

@@ -32,10 +32,10 @@ SCATTERS = tuple((t, e0, e1) for e0, e1 in PIECES for t in (0, 1)) + (
     (2, 0, 512), (3, 0, 256), (2, 512, 1024), (3, 256, 1024),
 )
 TURNED = 256
-TURNED_AT = T2 - TURNED
-NODE_CHUNKS = (128, 128, 256, 256, 256, 256, 256, 128, 128)
+TURNED_AT = T2 // 2
+FAR = TURNED_AT + TURNED
+NODE_CHUNKS = (128, 128, 256, 256, 256, 256, 256, 256)
 TURNED_AFTER = 4
-NEAR = sum(NODE_CHUNKS[: TURNED_AFTER + 1])
 TURN_AT_UNIT = 6
 EXCESS_BANK = 3
 LAST_COPIES = ((0, 128), (128, 256), (256, 512), (512, 1024))
@@ -133,7 +133,7 @@ def tile_list_neighbour_gap_message_kernel(
         st_turned = keep.tile([P, PACK, TURNED], F32, name="st_turned", align_bytes=256)
         for t0, t1, e0, e1 in WG_LOADS:
             if t0 == 2:
-                nc.sync.dma_start(st_turned[:], state_rows[:, :, TURNED_AT:])
+                nc.sync.dma_start(st_turned[:], state_rows[:, :, TURNED_AT:FAR])
             for g in QUAD_ORDER:
                 nc.sync.dma_start(wg[g * QUAD : (g + 1) * QUAD, t0:t1, e0:e1], wgs_rows[:, t0:t1, e0:e1])
         w8 = keep.tile([P, N], I32, name="w8", align_bytes=256)
@@ -169,7 +169,7 @@ def tile_list_neighbour_gap_message_kernel(
                 in_=grouped[:, a, t0 * BANK : t1 * BANK],
             )
 
-        st_cuts = ((0, NEAR), (NEAR, TURNED_AT))
+        st_cuts = ((0, TURNED_AT), (FAR, T2))
         st = [
             keep.tile([P, PACK, hi - lo], F32, name="st%d" % part, tag="tab%d" % part, align_bytes=256)
             for part, (lo, hi) in enumerate(st_cuts)
@@ -353,14 +353,15 @@ def tile_list_neighbour_gap_message_kernel(
             if t > 1:
                 scatter(t, e0, e1)
             if e1 == S:
-                for lo, hi in ((0, HALF), (HALF, TURNED_AT)) if t < PACK - 1 else LAST_COPIES:
+                for lo, hi in ((0, TURNED_AT), (FAR, T2)) if t < PACK - 1 else LAST_COPIES:
                     part, at = divmod(lo, HALF)
                     nc.scalar.copy(stack[part][:, t, at : at + hi - lo], pages[t][:, lo:hi])
                 if t == PACK - 1:
-                    nc.sync.dma_start(stack[1][:, t, : TURNED_AT - HALF], pages[t][:, HALF:TURNED_AT])
+                    nc.sync.dma_start(stack[1][:, t, FAR - HALF :], pages[t][:, FAR:])
                     late = excess((2, 3), EXCESS_BANK)
 
-        starts = [sum(NODE_CHUNKS[:c]) for c in range(len(NODE_CHUNKS))]
+        starts = [sum(NODE_CHUNKS[:c]) + (TURNED if c > TURNED_AFTER else 0) for c in range(len(NODE_CHUNKS))]
+        last = len(NODE_CHUNKS) - 1
 
         wovens = {}
         stored = []
@@ -368,7 +369,9 @@ def tile_list_neighbour_gap_message_kernel(
         def maximum(c, lo, hi):
             part, at = divmod(starts[c], HALF)
             far = c > TURNED_AFTER
-            st_at = starts[c] - (NEAR if far else 0)
+            st_at = starts[c] - (FAR if far else 0)
+            if c == last and c not in wovens:
+                wovens.setdefault(c, keep.tile([P, PACK * NODE_CHUNKS[c]], BF16, name="woven", tag="woven_last", align_bytes=256))
             if c not in wovens:
                 wovens.setdefault(c, ring.tile([P, PACK * max(NODE_CHUNKS)], BF16, name="woven", bufs=3, align_bytes=256))
             nc.vector.tensor_tensor(
@@ -378,19 +381,26 @@ def tile_list_neighbour_gap_message_kernel(
                 ALU.max,
             )
 
-        def quantise(width, woven, tag=None):
+        def quantise(parts, tag=None):
+            total = sum(width for width, woven in parts)
             if tag is not None:
-                z_codes = keep.tile([P, width], U32, name="z_own", tag=tag, align_bytes=256)
+                z_codes = keep.tile([P, total], U32, name="z_own", tag=tag, align_bytes=256)
             else:
-                z_codes = ring.tile([P, max(NODE_CHUNKS)], U32, name="z_codes", align_bytes=256)
-            z_scales = ring.tile([P, max(NODE_CHUNKS)], U8, name="z_scales", bufs=3, align_bytes=256)
-            nc.vector.quantize_mx(
-                out=z_codes[:, :width].bitcast(FP8X4), scales=z_scales[:, :width], in_=woven[:, : PACK * width]
-            )
-            return z_codes, z_scales
+                z_codes = ring.tile([P, total], U32, name="z_codes", align_bytes=256)
+            z_scales = ring.tile([P, BANK], U8, name="z_scales", bufs=3, align_bytes=256)
+            end = total
+            for width, woven in parts[::-1]:
+                nc.vector.quantize_mx(
+                    out=z_codes[:, end - width : end].bitcast(FP8X4),
+                    scales=z_scales[:, end - width : end],
+                    in_=woven[:, : PACK * width],
+                )
+                end = end - width
+            return total, z_codes, z_scales
 
-        def messages(n0, width, z_codes, z_scales, left):
-            per_bank = 2 if left == 0 else BANK // width
+        def messages(c, width, z_codes, z_scales):
+            n0 = starts[c]
+            per_bank = BANK // width
             for b0 in range(0, N // P, per_bank):
                 o_ps = bank(len(stored) % BANKS, "o_ps")
                 stored.append((n0, b0))
@@ -405,22 +415,31 @@ def tile_list_neighbour_gap_message_kernel(
                         start=True,
                         stop=True,
                     )
-                o_sb = outs.tile([P, BANK], F32, name="o_sb", align_bytes=256)
+                if c == last - 1 and b0 > 0:
+                    o_sb = keep.tile([P, BANK], F32, name="o_late", tag="woven_last", align_bytes=256)
+                else:
+                    o_sb = outs.tile([P, BANK], F32, name="o_sb", align_bytes=256)
                 used = per_bank * width
-                copy = nc.vector.tensor_copy if left == 1 or (left == 0 and b0 > 0) else nc.scalar.copy
+                copy = nc.vector.tensor_copy if c >= last - 1 and b0 > 0 else nc.scalar.copy
                 copy(o_sb[:, :used], o_ps[:, :used])
                 nc.sync.dma_start(
                     out[b0 * P : (b0 + per_bank) * P, n0 : n0 + width].rearrange("(k p) n -> p k n", p=P),
                     o_sb[:, :used].rearrange("p (k n) -> p k n", k=per_bank),
                 )
 
+        made = {}
         for c, width in enumerate(NODE_CHUNKS):
             maximum(c, LEAD if c not in (0, TURNED_AFTER + 1) else 0, width)
             if c == TURNED_AFTER:
-                messages(TURNED_AT, TURNED, *quantise(TURNED, woven_turned, "tab0"), None)
-            elif c + 1 < len(NODE_CHUNKS):
-                maximum(c + 1, 0, LEAD)
-            messages(starts[c], width, *quantise(width, wovens[c], "z_first%d" % c if c < 2 else None), len(NODE_CHUNKS) - 1 - c)
+                made.setdefault(c, quantise([(width, wovens[c]), (TURNED, woven_turned)], "tab0"))
+            else:
+                if c < last:
+                    maximum(c + 1, 0, LEAD)
+                made.setdefault(c, quantise([(width, wovens[c])], "z_first%d" % c if c < 2 else None))
+            if c != last - 1:
+                if c == last:
+                    messages(c - 1, *made[c - 1])
+                messages(c, *made[c])
             if c == 0:
                 rectify(*late, "z_first0")
             if c == 1:

@@ -32,13 +32,13 @@ SCATTERS = tuple((t, e0, e1) for e0, e1 in PIECES for t in (0, 1)) + (
     (2, 0, 512), (3, 0, 256), (2, 512, 1024), (3, 256, 1024),
 )
 TURNED = 256
-TURNED_AT = T2 // 2
-FAR = TURNED_AT + TURNED
-NODE_CHUNKS = (128, 128, 256, 256, 256, 256, 256, 256)
-TURNED_AFTER = 4
+FAR = T2 // 2
+TURNED_AT = FAR - TURNED
+NODE_CHUNKS = (128, 128, 256, 256, 256, 256, 256, 128, 128)
+TURNED_AFTER = 3
 TURN_AT_UNIT = 6
 EXCESS_BANK = 3
-LAST_COPIES = ((0, 128), (128, 256), (256, 512), (512, 1024))
+LAST_COPIES = ((0, 128), (128, 256), (256, 512), (512, TURNED_AT))
 KIB = 1024
 HALF = T2 // 2
 PAIR = 2
@@ -59,7 +59,7 @@ def tile_list_neighbour_gap_message_kernel(
         keep = ctx.enter_context(tc.tile_pool(name="keep", bufs=1))
         laid = ctx.enter_context(tc.tile_pool(name="laid", bufs=1))
         ring = ctx.enter_context(tc.tile_pool(name="ring", bufs=2))
-        outs = ctx.enter_context(tc.tile_pool(name="outs", bufs=10))
+        outs = ctx.enter_context(tc.tile_pool(name="outs", bufs=9))
         psum = ctx.enter_context(tc.psum_pool(name="psum", bufs=1))
 
         idx = keep.tile([P, S // 16], U16, name="idx")
@@ -177,7 +177,7 @@ def tile_list_neighbour_gap_message_kernel(
         for part, (lo, hi) in enumerate(st_cuts):
             nc.sync.dma_start(st[part][:], state_rows[:, :, lo:hi])
 
-        h = [keep.tile([P, S], F32, name="h%d" % t, align_bytes=256) for t in range(PACK)]
+        h = [keep.tile([P, S], F32, name="h%d" % t, tag="h%d" % t, align_bytes=256) for t in range(PACK)]
         units = [(t, lo, min(lo + BANK, e1)) for t, e0, e1 in SCATTERS for lo in range(e0, e1, BANK)]
         sums = {}
         terms = {}
@@ -294,8 +294,8 @@ def tile_list_neighbour_gap_message_kernel(
             return ps, cells
 
         def rectify(ps, cells, tag):
-            r_turned = keep.tile([P, BANK], F32, name="r_turned", tag=tag, align_bytes=256)
-            nc.scalar.activation(r_turned[:], ps[:], ACT.Relu)
+            r_turned = keep.tile([P, len(cells) * P], F32, name="r_turned", tag=tag, align_bytes=256)
+            nc.scalar.activation(r_turned[:], ps[:, : len(cells) * P], ACT.Relu)
             for n, (i, t, b) in enumerate(cells):
                 turn(z_sums[b][:, t * P : (t + 1) * P], r_turned[:, n * P : (n + 1) * P], False, t == PACK - 1)
 
@@ -355,10 +355,13 @@ def tile_list_neighbour_gap_message_kernel(
             if e1 == S:
                 for lo, hi in ((0, TURNED_AT), (FAR, T2)) if t < PACK - 1 else LAST_COPIES:
                     part, at = divmod(lo, HALF)
+                    if t == PACK - 1 and hi == TURNED_AT:
+                        rectify(*excess((t,), EXCESS_BANK + 1), "r_last")
                     nc.scalar.copy(stack[part][:, t, at : at + hi - lo], pages[t][:, lo:hi])
+                if t == PACK - 2:
+                    rectify(*excess((t,), EXCESS_BANK), "r_early")
                 if t == PACK - 1:
                     nc.sync.dma_start(stack[1][:, t, FAR - HALF :], pages[t][:, FAR:])
-                    late = excess((2, 3), EXCESS_BANK)
 
         starts = [sum(NODE_CHUNKS[:c]) + (TURNED if c > TURNED_AFTER else 0) for c in range(len(NODE_CHUNKS))]
         last = len(NODE_CHUNKS) - 1
@@ -386,7 +389,7 @@ def tile_list_neighbour_gap_message_kernel(
             if tag is not None:
                 z_codes = keep.tile([P, total], U32, name="z_own", tag=tag, align_bytes=256)
             else:
-                z_codes = ring.tile([P, total], U32, name="z_codes", align_bytes=256)
+                z_codes = ring.tile([P, total], U32, name="z_codes", bufs=3, align_bytes=256)
             z_scales = ring.tile([P, BANK], U8, name="z_scales", bufs=3, align_bytes=256)
             end = total
             for width, woven in parts[::-1]:
@@ -400,7 +403,7 @@ def tile_list_neighbour_gap_message_kernel(
 
         def messages(c, width, z_codes, z_scales):
             n0 = starts[c]
-            per_bank = BANK // width
+            per_bank = 2 if c == last else BANK // width
             for b0 in range(0, N // P, per_bank):
                 o_ps = bank(len(stored) % BANKS, "o_ps")
                 stored.append((n0, b0))
@@ -415,37 +418,42 @@ def tile_list_neighbour_gap_message_kernel(
                         start=True,
                         stop=True,
                     )
-                if c == last - 1 and b0 > 0:
+                if c == last - 1:
                     o_sb = keep.tile([P, BANK], F32, name="o_late", tag="woven_last", align_bytes=256)
                 else:
                     o_sb = outs.tile([P, BANK], F32, name="o_sb", align_bytes=256)
                 used = per_bank * width
-                copy = nc.vector.tensor_copy if c >= last - 1 and b0 > 0 else nc.scalar.copy
+                copy = nc.vector.tensor_copy if c == last - 1 or (c == last and b0 > 0) else nc.scalar.copy
                 copy(o_sb[:, :used], o_ps[:, :used])
                 nc.sync.dma_start(
                     out[b0 * P : (b0 + per_bank) * P, n0 : n0 + width].rearrange("(k p) n -> p k n", p=P),
                     o_sb[:, :used].rearrange("p (k n) -> p k n", k=per_bank),
                 )
 
+        turned = []
+
+        def weave(b, tag):
+            woven = keep.tile([P, BANK], BF16, name="woven_turned", tag=tag, align_bytes=256)
+            nc.scalar.copy(
+                woven[:].rearrange("p (c i t) -> p c t i", i=PAIR, t=PACK),
+                z_sums[b][:].rearrange("p (t c i) -> p c t i", i=PAIR, t=PACK),
+            )
+            turned.append((P, woven))
+
+        weave(0, "woven_turned")
         made = {}
         for c, width in enumerate(NODE_CHUNKS):
             maximum(c, LEAD if c not in (0, TURNED_AFTER + 1) else 0, width)
             if c == TURNED_AFTER:
-                made.setdefault(c, quantise([(width, wovens[c]), (TURNED, woven_turned)], "tab0"))
+                made.setdefault(c, quantise([(width, wovens[c])] + turned, "h0"))
             else:
                 if c < last:
                     maximum(c + 1, 0, LEAD)
                 made.setdefault(c, quantise([(width, wovens[c])], "z_first%d" % c if c < 2 else None))
-            if c != last - 1:
-                if c == last:
-                    messages(c - 1, *made[c - 1])
+            if c < last - 1:
                 messages(c, *made[c])
+            if c == last:
+                for d in range(last - 1, last + 1):
+                    messages(d, *made[d])
             if c == 0:
-                rectify(*late, "z_first0")
-            if c == 1:
-                woven_turned = keep.tile([P, PACK * TURNED], BF16, name="woven_turned", tag="z_first1", align_bytes=256)
-                for b in range(blocks):
-                    nc.scalar.copy(
-                        woven_turned[:, b * BANK : (b + 1) * BANK].rearrange("p (c i t) -> p c t i", i=PAIR, t=PACK),
-                        z_sums[b][:].rearrange("p (t c i) -> p c t i", i=PAIR, t=PACK),
-                    )
+                weave(1, "z_first0")

@@ -59,7 +59,7 @@ def tile_list_neighbour_gap_message_kernel(
         keep = ctx.enter_context(tc.tile_pool(name="keep", bufs=1))
         laid = ctx.enter_context(tc.tile_pool(name="laid", bufs=1))
         ring = ctx.enter_context(tc.tile_pool(name="ring", bufs=2))
-        outs = ctx.enter_context(tc.tile_pool(name="outs", bufs=9))
+        outs = ctx.enter_context(tc.tile_pool(name="outs", bufs=8))
         psum = ctx.enter_context(tc.psum_pool(name="psum", bufs=1))
 
         idx = keep.tile([P, S // 16], U16, name="idx")
@@ -401,6 +401,12 @@ def tile_list_neighbour_gap_message_kernel(
                 end = end - width
             return total, z_codes, z_scales
 
+        joint = []
+
+        def store(b0, n0, rows):
+            count, width = rows.shape[1:]
+            nc.sync.dma_start(out[b0 * P : (b0 + count) * P, n0 : n0 + width].rearrange("(k p) n -> p k n", p=P), rows)
+
         def messages(c, width, z_codes, z_scales):
             n0 = starts[c]
             per_bank = 2 if c == last else BANK // width
@@ -418,17 +424,20 @@ def tile_list_neighbour_gap_message_kernel(
                         start=True,
                         stop=True,
                     )
-                if c == last - 1:
-                    o_sb = keep.tile([P, BANK], F32, name="o_late", tag="woven_last", align_bytes=256)
-                else:
-                    o_sb = outs.tile([P, BANK], F32, name="o_sb", align_bytes=256)
                 used = per_bank * width
-                copy = nc.vector.tensor_copy if c == last - 1 or (c == last and b0 > 0) else nc.scalar.copy
-                copy(o_sb[:, :used], o_ps[:, :used])
-                nc.sync.dma_start(
-                    out[b0 * P : (b0 + per_bank) * P, n0 : n0 + width].rearrange("(k p) n -> p k n", p=P),
-                    o_sb[:, :used].rearrange("p (k n) -> p k n", k=per_bank),
-                )
+                if c < last - 1:
+                    o_sb = outs.tile([P, BANK], F32, name="o_sb", align_bytes=256)
+                    nc.scalar.copy(o_sb[:, :used], o_ps[:, :used])
+                    store(b0, n0, o_sb[:, :used].rearrange("p (k n) -> p k n", k=per_bank))
+                    continue
+                sums_out = o_ps[:, :used].rearrange("p (k n) -> p k n", k=per_bank)
+                if c < last:
+                    joint.append(keep.tile([P, N // P, 2 * width], F32, name="joint", tag="woven_last", align_bytes=256))
+                    nc.vector.tensor_copy(joint[0][:, :, :width], sums_out)
+                else:
+                    copy = nc.vector.tensor_copy if b0 > 0 else nc.scalar.copy
+                    copy(joint[0][:, b0 : b0 + per_bank, width:], sums_out)
+                    store(b0, starts[c - 1], joint[0][:, b0 : b0 + per_bank, :])
 
         turned = []
 

from contextlib import ExitStack

import concourse.mybir as mybir
from concourse.masks import make_identity

K, T, S, T2, H, N = 1024, 4096, 1024, 2048, 512, 512
FLOPS = 2 * (2 * K * H * S + H * N * T2)

F32 = mybir.dt.float32
BF16 = mybir.dt.bfloat16
I32 = mybir.dt.int32
U32 = mybir.dt.uint32
U16 = mybir.dt.uint16
U8 = mybir.dt.uint8
FP8X4 = mybir.dt.float8_e4m3fn_x4
FP4X4 = mybir.dt.float4_e2m1fn_x4
ALU = mybir.AluOpType
ACT = mybir.ActivationFunctionType

P = 128
PACK = 4
PASSES = K // (P * PACK)
BANK = 512
QUAD = 32
ROWS = 16
W4_AT = S
PLANE = S + H
FIRST = 256
PIECES = ((0, FIRST), (FIRST, 2 * FIRST), (2 * FIRST, S))

SCATTERS = tuple((t, e0, e1) for e0, e1 in PIECES for t in (0, 1)) + (
    (2, 0, 512), (3, 0, 256), (2, 512, 1024), (3, 256, 1024),
)
TURNED = 256
FAR = T2 // 2
TURNED_AT = FAR - TURNED
NODE_CHUNKS = (128, 128, 256, 256, 256, 256, 256, 128, 128)
TURNED_AFTER = 3
TURN_AT_UNIT = 6
EXCESS_BANK = 3
LAST_COPIES = ((0, 128), (128, 256), (256, 512), (512, TURNED_AT))
KIB = 1024
HALF = T2 // 2
PAIR = 2
BANKS = 8
EARLY_UNITS = ((0, 1, 2, 3), (0, 1, 4, 5))
QUAD_ORDER = (0, 2, 1, 3)
DIRECT = 2
LEAD = 96
TERM_BUFS = (3, 2)
WG_LOADS = tuple((t, t + 1, e0, e1) for e0, e1 in ((0, FIRST),) for t in (0, 1)) + ((0, 2, FIRST, 2 * FIRST), (0, 2, 2 * FIRST, S), (2, 4, 0, S))


def tile_list_neighbour_gap_message_kernel(
    tc, tab_words, tab_scales, offs, w1, w4_words, w4_scales, wgs, offs2, state, w8_words, w8_scales, out
):
    nc = tc.nc
    with ExitStack() as ctx:
        keep = ctx.enter_context(tc.tile_pool(name="keep", bufs=1))
        laid = ctx.enter_context(tc.tile_pool(name="laid", bufs=1))
        ring = ctx.enter_context(tc.tile_pool(name="ring", bufs=2))
        outs = ctx.enter_context(tc.tile_pool(name="outs", bufs=8))
        psum = ctx.enter_context(tc.psum_pool(name="psum", bufs=1))

        idx = keep.tile([P, S // 16], U16, name="idx")
        idx2 = keep.tile([P, S // 16], U16, name="idx2")
        tsc = keep.tile([P, T], U8, name="tsc", tag="tsc", align_bytes=256)
        w4s_raw = keep.tile([P, H], U8, name="w4s_raw", align_bytes=256)
        planes = keep.tile([P, PASSES * PLANE], U8, name="planes", align_bytes=256)
        tab = [keep.tile([P, T], I32, name="tab%d" % a, tag="tab%d" % a, align_bytes=256) for a in range(PASSES)]
        w4_raw = [keep.tile([P, 2 * H], U8, name="w4_raw%d" % a, align_bytes=256) for a in range(PASSES)]
        w1_raw = [
            keep.tile([P, PACK, H], F32, name="w1_raw%d" % a, tag="w1_raw%d" % a, align_bytes=256) for a in range(PASSES)
        ]
        ident = keep.tile([P, P], F32, name="ident", align_bytes=256)

        live = PASSES * ROWS
        for lo, hi in ((QUAD, 2 * QUAD), (2 * QUAD, P)):
            nc.gpsimd.memset(tsc[lo:hi, :].bitcast(I32), 0)
            nc.gpsimd.memset(w4s_raw[lo:hi, :].bitcast(I32), 0)
        nc.vector.memset(planes[:, PLANE:].bitcast(I32), 0)
        make_identity(nc, ident[:])
        pages = {}

        nc.sync.dma_start(idx[:], offs)
        nc.sync.dma_start(tsc[0:live, :].bitcast(I32), tab_scales.rearrange("a q t -> (a q) t").bitcast(I32))
        nc.sync.dma_start(w4s_raw[0:live, :].bitcast(I32), w4_scales.rearrange("a q c -> (a q) c").bitcast(I32))
        for a in range(PASSES):
            nc.sync.dma_start(tab[a][:], tab_words[a].rearrange("p t i -> p (t i)").bitcast(I32))
        nc.sync.dma_start(w4_raw[0][:].bitcast(I32), w4_words[0].bitcast(I32))

        gsc = keep.tile([P, S], U8, name="gsc", align_bytes=256)
        nc.vector.tensor_copy(
            planes[:, W4_AT:PLANE].rearrange("p (t m) -> p t m", t=PACK),
            w4s_raw[:].rearrange("p (m t) -> p t m", t=PACK),
        )
        nc.vector.tensor_copy(gsc[:], tsc[:].indirect(idx[:]))
        nc.vector.tensor_copy(planes[:, 0:S].bitcast(I32), gsc[:].bitcast(I32))

        def carry(a, q, queue):
            src = ROWS * a + 4 * q
            queue.dma_start(
                planes[QUAD * q : QUAD * q + 4, a * PLANE : (a + 1) * PLANE].bitcast(I32),
                planes[src : src + 4, 0:PLANE].bitcast(I32),
            )

        groups = [(a, q) for a in range(PASSES) for q in QUAD_ORDER]
        for a, q in groups[1:PACK]:
            carry(a, q, nc.sync)
        nc.sync.dma_start(idx2[:], offs2)
        w1_rows = w1.rearrange("(a p j) c -> a p j c", a=PASSES, j=PACK)
        for a in range(PASSES):
            nc.sync.dma_start(w1_raw[a][:], w1_rows[a])
        nc.sync.dma_start(w4_raw[1][:].bitcast(I32), w4_words[1].bitcast(I32))
        for a, q in groups[PACK:]:
            carry(a, q, nc.sync)
        w4 = {}

        def order_w4(a, t0, t1, copy, tag):
            words = keep.tile([P, 2 * (t1 - t0) * P], U8, name="w4_%d%d" % (a, t0), tag=tag, align_bytes=256)
            for t in range(t0, t1):
                w4.setdefault((a, t), words[:, 2 * (t - t0) * P : 2 * (t - t0 + 1) * P])
            copy(
                words[:].bitcast(U16).rearrange("p (t m) -> p t m", m=P),
                w4_raw[a][:].bitcast(U16).rearrange("p (m t) -> p t m", t=PACK)[:, t0:t1, :],
            )

        order_w4(0, 0, PACK, nc.vector.tensor_copy, "w4_first")

        wgs_rows = wgs.rearrange("(q t) j -> q t j", t=PACK)
        wg = keep.tile([P, PACK, S], F32, name="wg", align_bytes=256)
        state_rows = state.rearrange("(p t) n -> p t n", t=PACK)
        st_turned = keep.tile([P, PACK, TURNED], F32, name="st_turned", align_bytes=256)
        for t0, t1, e0, e1 in WG_LOADS:
            if t0 == 2:
                nc.sync.dma_start(st_turned[:], state_rows[:, :, TURNED_AT:FAR])
            for g in QUAD_ORDER:
                nc.sync.dma_start(wg[g * QUAD : (g + 1) * QUAD, t0:t1, e0:e1], wgs_rows[:, t0:t1, e0:e1])
        w8 = keep.tile([P, N], I32, name="w8", align_bytes=256)
        w8_plane = keep.tile([P, N], U8, name="w8_plane", align_bytes=256)
        nc.vector.memset(w8_plane[:].bitcast(I32), 0)
        nc.sync.dma_start(w8[:], w8_words[0].rearrange("p c i -> p (c i)").bitcast(I32))
        for q in range(P // QUAD):
            nc.sync.dma_start(
                w8_plane[QUAD * q : QUAD * q + 4, :].bitcast(I32), w8_scales[0, 4 * q : 4 * q + 4, :].bitcast(I32)
            )

        for t, tag in enumerate(("page0", "tsc")):
            pages.setdefault(t, keep.tile([P, T2], F32, name="page%d" % t, tag=tag, align_bytes=256))
            nc.vector.memset(pages[t][:].bitcast(I32), 0)
        v = [keep.tile([P, S], U32, name="v%d" % a, tag="v%d" % a, align_bytes=256) for a in range(PASSES)]
        for a in range(PASSES):
            nc.vector.tensor_copy(v[a][:], tab[a][:].bitcast(U32).indirect(idx[:]))

        w1_codes = keep.tile([P, PASSES, H], U32, name="w1_codes", align_bytes=256)
        w1_scales = keep.tile([P, PASSES, H], U8, name="w1_scales", align_bytes=256)
        grouped = laid.tile([P, PASSES, H * PACK], BF16, name="grouped", offset=20 * KIB, align_bytes=256)

        def cast(a, t0, t1, copy, m0=0, m1=P):
            copy(
                grouped[:, a, t0 * BANK : t1 * BANK].rearrange("p (t m j) -> p m j t", t=t1 - t0, j=PACK)[:, m0:m1],
                w1_raw[a][:].rearrange("p j (m t) -> p m j t", t=PACK)[:, m0:m1, :, t0:t1],
            )

        def quantise_w1(a, t0, t1):
            nc.vector.quantize_mx(
                out=w1_codes[:, a, t0 * P : t1 * P].bitcast(FP8X4),
                scales=w1_scales[:, a, t0 * P : t1 * P],
                in_=grouped[:, a, t0 * BANK : t1 * BANK],
            )

        st_cuts = ((0, TURNED_AT), (FAR, T2))
        st = [
            keep.tile([P, PACK, hi - lo], F32, name="st%d" % part, tag="tab%d" % part, align_bytes=256)
            for part, (lo, hi) in enumerate(st_cuts)
        ]
        for part, (lo, hi) in enumerate(st_cuts):
            nc.sync.dma_start(st[part][:], state_rows[:, :, lo:hi])

        h = [keep.tile([P, S], F32, name="h%d" % t, tag="h%d" % t, align_bytes=256) for t in range(PACK)]
        units = [(t, lo, min(lo + BANK, e1)) for t, e0, e1 in SCATTERS for lo in range(e0, e1, BANK)]
        sums = {}
        terms = {}

        def bank(b, name):
            return psum.tile([P, BANK], F32, name=name, tag="bank%d" % b)

        def sum_bank(u, k):
            if k == 1 and u >= TURN_AT_UNIT:
                return 4 + u % 2
            return u % 4 if k == 0 else 4 + u % 2 + 2 * ((max(u // 2, 1) + 1) % 2)

        def weights(k, a, t):
            if k == 0:
                return w1_codes[:, a, t * P : (t + 1) * P].bitcast(FP8X4), w1_scales[:, a, t * P : (t + 1) * P]
            at = a * PLANE + W4_AT + t * P
            return w4[a, t].bitcast(FP4X4), planes[:, at : at + P]

        def product(u, k, a):
            t, e0, e1 = units[u]
            if (u, k) not in sums:
                sums.setdefault((u, k), bank(sum_bank(u, k), "sum%d" % k))
            looked_up = [
                (v[a][:, lo:hi].bitcast(FP8X4), planes[:, a * PLANE + lo : a * PLANE + hi])
                for lo, hi in ([(e0, e1)] if u < DIRECT else [(e, e + P) for e in range(e0, e1, P)])
            ]
            for b, edges in enumerate(looked_up):
                still, moving = (weights(k, a, t), edges) if u < DIRECT else (edges, weights(k, a, t))
                width = e1 - e0 if u < DIRECT else P
                nc.tensor.matmul_mx(
                    out=sums[u, k][:, b * width : (b + 1) * width],
                    lhsT=still[0],
                    lhsT_scale=still[1],
                    rhs=moving[0],
                    rhs_scale=moving[1],
                    start=(a == 0 and b == 0),
                    stop=(a == PASSES - 1 and b == len(looked_up) - 1),
                )

        def term(u, k):
            width = units[u][2] - units[u][1]
            if u == DIRECT:
                sb = keep.tile([P, width], F32, name="term_behind", tag="d_first%d" % k, align_bytes=256)
            elif u == len(units) - 1:
                sb = keep.tile([P, width], F32, name="term_last", tag="v%d" % k, align_bytes=256)
            elif (u, k) == (DIRECT + 1, 0):
                sb = keep.tile([P, width], F32, name="term_ahead", tag="w4_late", align_bytes=256)
            else:
                sb = ring.tile([P, BANK], F32, name="term%d" % k, tag="term%d" % k, bufs=TERM_BUFS[k], align_bytes=256)
            if k == 0:
                nc.scalar.activation(sb[:, :width], sums[u, 0][:, :width], ACT.Relu)
            else:
                nc.scalar.activation(sb[:, :width], sums[u, 1][:, :width], ACT.Copy, scale=-1.0)
            terms.setdefault((u, k), sb)

        def linear_view(u):
            for a in range(1 if u in EARLY_UNITS[1] else 0, PASSES):
                product(u, 1, a)
            term(u, 1)

        def rectified_view(u):
            for a in range(1 if u in EARLY_UNITS[0] else 0, PASSES):
                product(u, 0, a)

        def gaps(u):
            t, e0, e1 = units[u]
            width = e1 - e0
            blocks = width // P
            d_ps = bank(sum_bank(u, 0) if u < len(units) - 1 else EXCESS_BANK, "d_ps")
            for k, sb in enumerate((terms[u, 1], terms[u, 0])):
                for b in range(blocks):
                    nc.tensor.matmul(
                        d_ps[:, b * P : (b + 1) * P],
                        lhsT=sb[:, b * P : (b + 1) * P],
                        rhs=ident[:],
                        is_transpose=True,
                        start=(k == 0 and b == 0),
                        stop=(k == 1 and b == blocks - 1),
                    )
            nc.scalar.activation(h[t][:, e0:e1], d_ps[:, :width], ACT.Abs)

        blocks = TURNED // P
        s_turned = keep.tile([P, blocks, PACK, P], F32, name="s_turned", tag="w1_raw0", align_bytes=256)
        s_minus = keep.tile([P, blocks, PACK, P], F32, name="s_minus", tag="w1_raw1", align_bytes=256)
        z_sums = []

        def turn(dst, src, start, stop):
            nc.tensor.matmul(dst, lhsT=src, rhs=ident[:], is_transpose=True, start=start, stop=stop)

        def turned_state():
            for b in range(blocks):
                ps = bank(BANKS - blocks + b, "s_ps")
                for t in range(PACK):
                    turn(ps[:, t * P : (t + 1) * P], st_turned[:, t, b * P : (b + 1) * P], t == 0, t == PACK - 1)
                nc.scalar.activation(s_turned[:, b].rearrange("p t n -> p (t n)"), ps[:], ACT.Relu)
            for b in range(blocks):
                ps = bank(BANKS - blocks + b, "m_ps")
                for t in range(PACK):
                    turn(ps[:, t * P : (t + 1) * P], s_turned[:, b, t, :], t == 0, t == PACK - 1)
                nc.scalar.activation(s_minus[:, b].rearrange("p t n -> p (t n)"), ps[:], ACT.Copy, scale=-1.0)
            for b in range(blocks):
                z_sums.append(bank(BANKS - blocks + b, "z_ps"))
                for t in range(PACK):
                    turn(z_sums[b][:, t * P : (t + 1) * P], s_turned[:, b, t, :], t == 0, False)

        def excess(slots, in_bank):
            ps = bank(in_bank, "r_ps")
            cells = [(i, t, b) for i, t in enumerate(slots) for b in range(blocks)]
            for n, (i, t, b) in enumerate(cells):
                turn(ps[:, n * P : (n + 1) * P], s_minus[:, b, t, :], n == 0, False)
            for n, (i, t, b) in enumerate(cells):
                at = TURNED_AT + b * P
                turn(ps[:, n * P : (n + 1) * P], pages[t][:, at : at + P], False, n == len(cells) - 1)
            return ps, cells

        def rectify(ps, cells, tag):
            r_turned = keep.tile([P, len(cells) * P], F32, name="r_turned", tag=tag, align_bytes=256)
            nc.scalar.activation(r_turned[:], ps[:, : len(cells) * P], ACT.Relu)
            for n, (i, t, b) in enumerate(cells):
                turn(z_sums[b][:, t * P : (t + 1) * P], r_turned[:, n * P : (n + 1) * P], False, t == PACK - 1)

        cast(0, 0, 2, nc.vector.tensor_copy)
        cast(0, 2, PACK, nc.scalar.copy)
        quantise_w1(0, 0, 2)
        quantise_w1(0, 2, PACK)
        for k in (1, 0):
            for u in EARLY_UNITS[k]:
                product(u, k, 0)
        cast(1, 0, 2, nc.vector.tensor_copy)
        order_w4(1, 0, 2, nc.scalar.copy, "w4_second")
        for m0 in (0, P // 2):
            cast(1, 2, PACK, nc.scalar.copy, m0, m0 + P // 2)
        for t in range(2):
            quantise_w1(1, t, t + 1)
        for view in (linear_view, rectified_view):
            for u in range(DIRECT):
                view(u)
        for u in range(DIRECT):
            d_first = keep.tile([P, FIRST], F32, name="d_first%d" % u, tag="d_first%d" % u, align_bytes=256)
            nc.vector.scalar_tensor_tensor(d_first[:], sums[u, 0][:, :FIRST], 0.0, terms[u, 1][:, :FIRST], ALU.max, ALU.add)
            nc.scalar.activation(h[u][:, :FIRST], d_first[:], ACT.Abs)
        quantise_w1(1, 2, PACK)
        for t in (2, 3):
            pages.setdefault(t, laid.tile([P, T2], F32, name="page%d" % t, offset=t * 8 * KIB, align_bytes=256))
            nc.gpsimd.memset(pages[t][:].bitcast(I32), 0)
        stack = []

        def scatter(t, e0, e1):
            nc.vector.tensor_tensor(
                pages[t][:].indirect(idx2[:, e0 // 16 : e1 // 16]), h[t][:, e0:e1], wg[:, t, e0:e1], ALU.mult
            )

        for u in range(DIRECT, len(units)):
            if u == TURN_AT_UNIT:
                turned_state()
            rectified_view(u)
            term(u, 0)
            linear_view(u)
            if u > DIRECT:
                gaps(u - 1)
            if u == DIRECT + 2:
                order_w4(1, 2, PACK, nc.scalar.copy, "w4_late")
        for t, e0, e1 in SCATTERS[: 2 * len(PIECES)]:
            scatter(t, e0, e1)
        rectify(*excess((0, 1), EXCESS_BANK), "r_early")
        gaps(len(units) - 1)

        stack.extend(
            keep.tile([P, PACK, HALF], F32, name="stack%d" % part, tag=tag, align_bytes=256)
            for part, tag in enumerate(("v0", "v1"))
        )
        for t, e0, e1 in SCATTERS:
            if t > 1:
                scatter(t, e0, e1)
            if e1 == S:
                for lo, hi in ((0, TURNED_AT), (FAR, T2)) if t < PACK - 1 else LAST_COPIES:
                    part, at = divmod(lo, HALF)
                    if t == PACK - 1 and hi == TURNED_AT:
                        rectify(*excess((t,), EXCESS_BANK + 1), "r_last")
                    nc.scalar.copy(stack[part][:, t, at : at + hi - lo], pages[t][:, lo:hi])
                if t == PACK - 2:
                    rectify(*excess((t,), EXCESS_BANK), "r_early")
                if t == PACK - 1:
                    nc.sync.dma_start(stack[1][:, t, FAR - HALF :], pages[t][:, FAR:])

        starts = [sum(NODE_CHUNKS[:c]) + (TURNED if c > TURNED_AFTER else 0) for c in range(len(NODE_CHUNKS))]
        last = len(NODE_CHUNKS) - 1

        wovens = {}
        stored = []

        def maximum(c, lo, hi):
            part, at = divmod(starts[c], HALF)
            far = c > TURNED_AFTER
            st_at = starts[c] - (FAR if far else 0)
            if c == last and c not in wovens:
                wovens.setdefault(c, keep.tile([P, PACK * NODE_CHUNKS[c]], BF16, name="woven", tag="woven_last", align_bytes=256))
            if c not in wovens:
                wovens.setdefault(c, ring.tile([P, PACK * max(NODE_CHUNKS)], BF16, name="woven", bufs=3, align_bytes=256))
            nc.vector.tensor_tensor(
                wovens[c][:, PACK * lo : PACK * hi].rearrange("p (c i t) -> p c t i", i=PAIR, t=PACK),
                stack[part][:, :, at + lo : at + hi].rearrange("p t (c i) -> p c t i", i=PAIR),
                st[far][:, :, st_at + lo : st_at + hi].rearrange("p t (c i) -> p c t i", i=PAIR),
                ALU.max,
            )

        def quantise(parts, tag=None):
            total = sum(width for width, woven in parts)
            if tag is not None:
                z_codes = keep.tile([P, total], U32, name="z_own", tag=tag, align_bytes=256)
            else:
                z_codes = ring.tile([P, total], U32, name="z_codes", bufs=3, align_bytes=256)
            z_scales = ring.tile([P, BANK], U8, name="z_scales", bufs=3, align_bytes=256)
            end = total
            for width, woven in parts[::-1]:
                nc.vector.quantize_mx(
                    out=z_codes[:, end - width : end].bitcast(FP8X4),
                    scales=z_scales[:, end - width : end],
                    in_=woven[:, : PACK * width],
                )
                end = end - width
            return total, z_codes, z_scales

        joint = []

        def store(b0, n0, rows):
            count, width = rows.shape[1:]
            nc.sync.dma_start(out[b0 * P : (b0 + count) * P, n0 : n0 + width].rearrange("(k p) n -> p k n", p=P), rows)

        def messages(c, width, z_codes, z_scales):
            n0 = starts[c]
            per_bank = 2 if c == last else BANK // width
            for b0 in range(0, N // P, per_bank):
                o_ps = bank(len(stored) % BANKS, "o_ps")
                stored.append((n0, b0))
                for k in range(per_bank):
                    b = b0 + k
                    nc.tensor.matmul_mx(
                        out=o_ps[:, k * width : (k + 1) * width],
                        lhsT=w8[:, b * P : (b + 1) * P].bitcast(FP8X4),
                        lhsT_scale=w8_plane[:, b * P : (b + 1) * P],
                        rhs=z_codes[:, :width].bitcast(FP8X4),
                        rhs_scale=z_scales[:, :width],
                        start=True,
                        stop=True,
                    )
                used = per_bank * width
                if c < last - 1:
                    o_sb = outs.tile([P, BANK], F32, name="o_sb", align_bytes=256)
                    nc.scalar.copy(o_sb[:, :used], o_ps[:, :used])
                    store(b0, n0, o_sb[:, :used].rearrange("p (k n) -> p k n", k=per_bank))
                    continue
                sums_out = o_ps[:, :used].rearrange("p (k n) -> p k n", k=per_bank)
                if c < last:
                    joint.append(keep.tile([P, N // P, 2 * width], F32, name="joint", tag="woven_last", align_bytes=256))
                    nc.vector.tensor_copy(joint[0][:, :, :width], sums_out)
                else:
                    copy = nc.vector.tensor_copy if b0 > 0 else nc.scalar.copy
                    copy(joint[0][:, b0 : b0 + per_bank, width:], sums_out)
                    store(b0, starts[c - 1], joint[0][:, b0 : b0 + per_bank, :])

        turned = []

        def weave(b, tag):
            woven = keep.tile([P, BANK], BF16, name="woven_turned", tag=tag, align_bytes=256)
            nc.scalar.copy(
                woven[:].rearrange("p (c i t) -> p c t i", i=PAIR, t=PACK),
                z_sums[b][:].rearrange("p (t c i) -> p c t i", i=PAIR, t=PACK),
            )
            turned.append((P, woven))

        weave(0, "woven_turned")
        made = {}
        for c, width in enumerate(NODE_CHUNKS):
            maximum(c, LEAD if c not in (0, TURNED_AFTER + 1) else 0, width)
            if c == TURNED_AFTER:
                made.setdefault(c, quantise([(width, wovens[c])] + turned, "h0"))
            else:
                if c < last:
                    maximum(c + 1, 0, LEAD)
                made.setdefault(c, quantise([(width, wovens[c])], "z_first%d" % c if c < 2 else None))
            if c < last - 1:
                messages(c, *made[c])
            if c == last:
                for d in range(last - 1, last + 1):
                    messages(d, *made[d])
            if c == 0:
                weave(1, "z_first0")
